import numpy as np, ml_dtypes
CORES = [3,7,11,15,131,135,139,143]
N = 8
import mx_ref
BF = ml_dtypes.bfloat16
def gentries(a):
    return np.ascontiguousarray(a.reshape(8, 16, -1).transpose(0, 2, 1)).reshape(8, -1)
def gtable(e):
    e = np.asarray(e); return np.ascontiguousarray(e.reshape(8, -1, 16).transpose(0, 2, 1)).reshape(128, -1).astype(np.int32)
def gcols(t, e):
    v = np.concatenate([t.reshape(8, 16, -1, 4), np.zeros((8, 16, 1, 4), BF)], axis=2)
    return np.ascontiguousarray(np.stack([v[g][:, e[g]] for g in range(8)])).reshape(128, -1)
def gpick(z, e):
    return np.concatenate([z[16 * g:16 * g + 16][:, e[g]] for g in range(8)])
def tile(rs):
    return np.stack(rs, axis=2).reshape(128, -1).astype(BF)
def pick(q, e):
    c = np.concatenate([q[0].reshape(128, -1, 4), np.zeros((128, 1, 4), np.uint8)], axis=1); s = np.concatenate([q[1], np.ones((16, 1), np.uint8)], axis=1)
    return (np.ascontiguousarray(c[:, e].reshape(128, -1)), np.ascontiguousarray(s[:, e]))
def join(*qs):
    return (np.concatenate([q[0] for q in qs], axis=1), np.concatenate([q[1] for q in qs], axis=1))
def put(q, e, v):
    c, s = q[0].reshape(128, -1, 4).copy(), q[1].copy(); c[:, e] = v[0].reshape(128, -1, 4); s[:, e] = v[1]
    return (c.reshape(128, -1), s)
def pk(c, s):
    return (np.ascontiguousarray(c), mx_ref.live(s))
def emit(q):
    return q[0], q[1]
def packed(v, rng):
    q = [mx_ref.quantize(np.ascontiguousarray(v[r])) for r in range(N)]
    return np.stack([a for a, b in q]), np.stack([mx_ref.plane(b, rng) for a, b in q])
def values_of_codes():
    e, c = np.zeros((128, 128, 4), np.float32), np.zeros((128, 2, 4), np.uint8)
    e[np.arange(128), np.arange(128), 0] = 1
    c[:127, :, 0] = np.arange(256).reshape(2, 128).T[:127]
    return mx_ref.matmul(mx_ref.quantize(e.reshape(128, 512).astype(BF)), (c.reshape(128, 8), np.full((16, 2), 127, np.uint8))).T.reshape(-1).astype(np.float64)
CODE_VALUE, SCALE_VALUE = values_of_codes(), 2.0 ** (np.arange(256) - 127.0)
def decode(q):
    return (CODE_VALUE[q[0]].reshape(16, 8, -1, 4) * SCALE_VALUE[q[1]][:, None, :, None] + 0.0).reshape(128, -1).astype(np.float32)
def f(rng, *shape):
    return mx_ref.flush((rng.standard_normal(shape, dtype=np.float32) * np.exp2(rng.integers(-2, 3, shape[:-1] + (1,)))).astype(BF))
def wide(rng, *shape, cols=0):
    v = rng.standard_normal(shape, dtype=np.float32) * np.exp2(rng.integers(-12, 13, shape)).astype(np.float32)
    if cols: v *= np.repeat(np.exp2(rng.integers(-cols, cols + 1, shape[:-2] + (1, shape[-1] // 4))) * (rng.random(shape[:-2] + (1, shape[-1] // 4)) > 0.0625), 4, axis=-1).astype(np.float32)
    return mx_ref.flush(v.astype(BF))
C, K, A, R, SWEEPS = 288, 112, 64, 3, 4
def big(v):
    v = v.astype(np.float32)
    v[np.abs(v) < np.float32(2.0 ** -16)] = 0
    return v.astype(BF)
def numbers_of(rng):
    return {"x": big(f(rng, N, 128, 4 * C)), "u": np.array(f(rng, N, 128, 512)), "v": np.array(f(rng, N, 128, 512))}
def stored(t):
    return np.stack([gtable(np.clip(t[r], 0, C - 1)) for r in range(N)])
def received(rng):
    return stored(np.arange(C) + rng.integers(-6, 26, (N, 8, C)))
def give(rng, w):
    c, s = packed(np.ascontiguousarray(w).reshape(N, 128, 2048), rng)
    return {"wc": c, "ws": s}
def weights(rng, still=[]):
    w = np.array(mx_ref.flush((rng.standard_normal((N, 128, 2048), dtype=np.float32) * np.float32(0.25)).astype(BF))).reshape(N, 8, 16, 4, 8, 16, 4)
    for i in still:
        w[:, :, i] = 0
        w[:, :, :, :, :, i] = 0
    return give(rng, w)
def setup_inputs(rng):
    return {**numbers_of(rng), "rv": received(rng), **weights(rng)}
def setup_inputs_ties(rng):
    d = numbers_of(rng)
    x = d["x"].reshape(N, 8, 16, C, 4)
    x[:, :, 0] = 0
    x[:, :, 8] = 0
    x[:, :, 0, :, 0] = rng.integers(0, 3, (N, 8, C)).astype(np.float32).astype(BF)
    x[:, :, 8, :, 0] = rng.integers(-1, 2, (N, 8, C)).astype(np.float32).astype(BF)
    u = d["u"].reshape(N, 128, 128, 4)
    u[:, :, ::8] = 0
    o = rng.permutation(N)
    for r in range(N):
        for h in range(0, 128, 16):
            u[r, h, h, 0] = 0.0 if r == o[0] else -1.0 if r == o[1] else 1.0
            u[r, h + 8, h + 8, 0] = 1.0
    t = np.arange(C) + rng.integers(-6, 26, (N, 8, C))
    g = rng.integers(8)
    t[o[0] - 1, g - 1] = 21
    t[o[0], g, C - 1] = 1
    x[o[0], g, 8, C - 1, 0] = 1.0
    return {"x": x.reshape(N, 128, 4 * C), "u": u.reshape(N, 128, 512), "v": d["v"], "rv": stored(t), **weights(rng, [0, 8])}
def setup_inputs_near(rng):
    d = numbers_of(rng)
    x = d["x"].astype(np.float32).reshape(N, 8, 16, C, 4)
    x[:, :, 0] = 0
    x[:, :, 8:] = 0
    x[:, :, 0, :, 0] = rng.integers(0, 2, (N, 8, C)) * 2.0 - 1.0
    s = rng.integers(0, 16, (N, 8, C))
    t = rng.integers(-1, 2, (N, 8, C))
    x[:, :, 8] = ((s[:, :, :, None] >> np.arange(4)) & 1) * np.exp2(np.arange(4) - 23.0)
    x[:, :, 11, :, 0] = 2.0 ** -10
    x[:, :, 12, :, 0] = t * 2.0 ** -10
    u = d["u"].reshape(N, 128, 128, 4)
    u[:, :, ::8] = 0
    u[:, :, 8::16] = 0
    o = rng.permutation(N) % 2
    for r in range(N):
        if o[r] == 1:
            x[r, :, 8:] = 0
            x[r, :, 8, :, 0] = (s[r] - 8) * 2.0 ** -28
            x[r, :, 12, :, 0] = t[r] * 2.0 ** -28
            x[r, :, 13, :, 0] = rng.integers(0, 2, (8, C)) * 1.125 * 2.0 ** -28
            for g in rng.permutation(8)[:4]: x[r, g, 8, rng.integers(C), 0] = 2.0 ** 20 * rng.choice([-1.0, 1.0])
        for h in range(0, 128, 16):
            k = 2.0 ** -30 if o[r] == 1 else 1.0
            u[r, h + 12, h + 8, 0] = k
            if o[r] == 1:
                u[r, h + 8, h, 0] = k
                u[r, h + 13, h, 0] = k
                u[r, h + 13, h + 8, 0] = k
            else:
                u[r, h, h, 0] = k
                u[r, h + 8, h] = k
                u[r, h + 11, h, 0] = k
    return {"x": x.reshape(N, 128, 4 * C).astype(BF), "u": u.reshape(N, 128, 512), "v": d["v"], "rv": received(rng), **weights(rng, [0, 8, 9, 10, 11, 12, 13, 14, 15])}
def setup_inputs_chains(rng):
    d = numbers_of(rng)
    x = d["x"].reshape(N, 8, 16, C, 4)
    m = np.exp2(rng.integers(-12, -5, (N, 8, 8, C, 4))) * (1 + (2 * rng.integers(0, 64, (N, 8, 8, C, 4)) + 1) * 2.0 ** -7) * rng.choice([-1.0, 1.0], (N, 8, 8, C, 4))
    m[:, :, 3, :, 0] = 7.875 * rng.choice([-1.0, 1.0], (N, 8, C))
    x[:, :, :8] = m.astype(np.float32).astype(BF)
    x[:, :, 12] = 0
    x[:, :, 12, :, 0] = np.where(rng.random((N, 8, C)) < 0.0625, -1, 1).astype(np.float32).astype(BF)
    u = d["u"].reshape(N, 128, 128, 4)
    u[:, :, 8::16] = 0
    for h in range(0, 128, 16): u[:, h + 12, h + 8, 0] = 1
    t = np.arange(C) + np.zeros((N, 8, 1), np.int64)
    o = np.repeat(rng.permutation(4), 2) if N == 8 else np.concatenate([[1, 1], rng.permutation([0, 3])])
    o = np.roll(o, rng.integers(N))
    for r in range(N):
        if o[r] == 0: t[r] -= rng.integers(2, 5, (8, 1))
        elif o[r] == 1: t[r, rng.integers(8)] -= 21
        elif o[r] == 2: t[r] = C - 1
        else: t[r] += rng.integers(-30, 61, (8, C))
    return {"x": x.reshape(N, 128, 4 * C), "u": u.reshape(N, 128, 512), "v": d["v"], "rv": stored(t), **weights(rng, [12])}
def setup_inputs_ends(rng):
    d = numbers_of(rng)
    x = np.zeros((N, 8, 16, C, 4))
    u = d["u"].reshape(N, 128, 128, 4)
    w = np.full((N, 128, 2048), 0.25)
    t = np.full((N, 8, C), C - 1)
    i = np.arange(128)
    o = np.roll(np.concatenate([[3, 0], rng.permutation([1, 2])] * (N // 4)), rng.integers(N))
    for r in range(N):
        a = (0.9375 + 0.0625 * rng.integers(0, 2, (8, 16, C, 4))) * 2.0 ** 20
        c = (0.9375 + 0.0625 * rng.integers(0, 2, (128, 128, 4))) * 2.0 ** 30
        if o[r] < 2:
            x[r] = -a
            c[:, 8::16] *= 1.0 if o[r] == 0 else -1.0
            if o[r] == 1: t[r] = 0
            else:
                x[r] = -2.0 ** 20
                z = x[r].reshape(128, C, 4)
                z[:65:8] = 0
                z[:65:8, :, 0] = -((rng.permutation(C) >> np.arange(9)[:, None]) & 1) * np.exp2(11.0 + np.arange(9))[:, None]
                c[:, ::16] = 2.0 ** 30
                for g in rng.permutation(8)[:4]: c[:, 16 * g] *= -1.0
                c[:65:8, ::16, 0] = 2.0 ** 30
                w[r] = 0
                for b in range(4): w[r].reshape(128, 4, 128, 4)[i, b, i, b] = 128.0
            d["v"][r] = 2.0 ** 30
        elif o[r] == 2:
            e = np.arange(C) // 2
            x[r] = (a * rng.choice([-1.0, 1.0], (8, 1, C, 1)))[:, :, e]
            for g in range(8): c[np.arange(128) // 16 != g, 16 * g:16 * g + 16] = 0
            t[r, rng.permutation(8)[:4]] = 0
            d["v"][r] = (2.0 ** 30 * rng.choice([-1.0, 1.0], (128, 512))).astype(np.float32).astype(BF)
        else:
            x[r] = 2.0 ** -28
            c[:] = 2.0 ** -30
            w[r] = 2.0 ** -30
            d["v"][r] = 2.0 ** -30
        u[r] = c.astype(np.float32).astype(BF)
    return {"x": x.reshape(N, 128, 4 * C).astype(np.float32).astype(BF), "u": u.reshape(N, 128, 512), "v": d["v"], "rv": stored(t), **give(rng, w.astype(np.float32).astype(BF))}
def setup_inputs_spread(rng):
    d = setup_inputs(rng)
    d["x"] = big(np.clip(wide(rng, N, 128, 4 * C, cols=6).astype(np.float32), -2.0 ** 20, 2.0 ** 20))
    return d
def check_inputs(d):
    b = []
    for k, lo, hi in (("x", 2.0 ** -28, 2.0 ** 20), ("u", 2.0 ** -30, 2.0 ** 30), ("v", 2.0 ** -30, 2.0 ** 30)):
        a = np.abs(d[k].astype(np.float32))
        if not (np.isfinite(a).all() and ((a == 0) | (a >= lo) & (a <= hi)).all()): b.append("a value of " + k)
    if not ((d["rv"] >= 0) & (d["rv"] < C)).all(): b.append("an entry of rv")
    none, least, most = [emit(mx_ref.quantize(np.full((128, 16), k, np.float32).astype(BF)))[1][0, 0] for k in (0.0, 2.0 ** -30, 2.0 ** 30)]
    for r in range(N):
        if ((d["wc"][r] == 0x7F) | (d["wc"][r] == 0xFF)).any(): b.append("wc: a code that is no number")
        s = mx_ref.live(d["ws"][r])
        if ((s != none) & ((s < least) | (s > most))).any(): b.append("ws: a scale out of range")
        elif not (np.sum(np.abs(decode(pk(d["wc"][r], d["ws"][r])).astype(np.float64)).reshape(128, 512, 4), axis=(0, 2)) <= 128).all(): b.append("a column of W: its sizes")
    return b
def fall(p, b):
    for i in range(SWEEPS): p = np.minimum(p, np.roll(np.take_along_axis(b, p, axis=1), 1, axis=0))
    return p
def mean(a, b):
    return ((a.astype(np.float32) + b.astype(np.float32)) * np.float32(0.5)).astype(BF)
def reference(x, u, v, rv, wc, ws):
    qu = [mx_ref.quantize(u[r]) for r in range(N)]
    lay = [pk(wc[r], ws[r]) for r in range(N)]
    now = [x[r] for r in range(N)]
    p0 = np.zeros((8, 1), np.int64) + A + 2 * np.arange(K)
    lq = np.zeros((N, 8, K), np.float32)
    for t in range(R):
        own, order, bound, sent, line = [], [], [], [], []
        for r in range(N):
            q = mx_ref.quantize(now[r])
            own.append(decode(q).astype(BF))
            s = mx_ref.matmul(qu[r], q) + np.float32(0.0)
            o = np.argsort(-s[::16], axis=1, kind="stable")
            a = np.where(np.take_along_axis(s[8::16], o, axis=1) > 0, np.maximum(gentries(rv[r]) - 1, 0), C - 1)
            a = np.minimum.accumulate(a[:, ::-1], axis=1)[:, ::-1]
            order.append(o)
            bound.append(np.concatenate([a[:, 1:], np.full((8, 1), C - 1)], axis=1))
            line.append(fall(p0, bound[r]))
            sent.append(mx_ref.quantize(mean(gcols(own[r], np.take_along_axis(o, p0, axis=1)), gcols(own[r], np.take_along_axis(o, line[r], axis=1)))))
        for r in range(N):
            e = (r - 1) % N
            p = fall(line[e], bound[r])
            z = mx_ref.quantize(mean(decode(sent[e]), gcols(own[r], np.take_along_axis(order[r], p, axis=1))))
            hit = p[:, None, :] == np.arange(C)[:, None]
            low = np.zeros((8, C), np.int64)
            np.put_along_axis(low, order[r], np.where(hit.any(axis=2), np.argmax(hit, axis=2), K), axis=1)
            new = []
            for b in range(4):
                h = mx_ref.matmul(pick(lay[r], np.arange(128 * b, 128 * b + 128)), z) * np.float32(0.0625)
                new.append(own[r][:, b::4].astype(np.float32) + gpick(np.concatenate([h, np.zeros((128, 1), np.float32)], axis=1), low))
            now[r] = tile(new)
            lq[r] = p
    y = np.zeros((N, 128, C), np.float32)
    oc, osc = np.zeros((N, 128, 4 * C), np.uint8), np.zeros((N, 16, C), np.uint8)
    for r in range(N):
        q = mx_ref.quantize(now[r])
        y[r] = mx_ref.matmul(mx_ref.quantize(v[r]), q)
        oc[r], osc[r] = emit(q)
    return {"y": y, "lq": lq, "oc": oc, "osc": osc}

@@ -1,0 +1,474 @@
+from concourse.mybir import dt, AluOpType, ActivationFunctionType
+
+C, K, ROUNDS = 288, 112, 3
+NJ = C // 16
+UNIT = 1024.0
+TAGU = 4096.0
+CODE, F32, BF, I32, U16, U8 = "float8_e4m3fn_x4", "float32", "bfloat16", "int32", "uint16", "uint8"
+SB = (9, 8, 7)
+SLOTS = NJ + 1
+GW = 72 * SLOTS + 72
+CE, CC, CT, CZ = 0, 512, 640, 768
+
+SCRATCH = {"ps": ("psum", [128, 4096], F32)}
+
+
+def _sb(dtype, **names):
+    for n, w in names.items():
+        SCRATCH[n] = ("sbuf", [128, w], dtype)
+
+
+_sb(BF, x0=4 * C, X=1600, ub=512, vb=512, nega=512, negb=512, cb=4 * 768, G=4 * GW, m4=C, m16=C, junk=4 * C,
+    FS=4 * C, A5=448, Et=512, Vt=512, DE=448, CV=448)
+_sb(F32, r4=C, r16=C, pflt=8, ic=C, I=C, dmy=K, cs=96, yl=NJ, ya=NJ, yb=NJ, yc=28, yd=28, wr=C,
+    z=C, zs=C, zz=144, KK=2 * C, M1=K, OE=C, sg=C, Vr=C, Rs=NJ, R2=NJ, rk=NJ, PL=C, am=C, rl=480, Bx=292, TAG=C,
+    T1=C, T2=C, T3=C, T4=C, Q1=C, Q2=C, Q3=C, Q4=C, P1=K, P2=K, P3=K, P4=K, w=K, w1=K, wE=K, FQ=448, eqn=K, sel=28, lqf=K,
+    q0=K, q1=K, q4=K, yo=C)
+_sb(I32, rvt=NJ, pint=8, yi=NJ, yj=NJ, oi1=C, oi=C, qi=28, qj=28, qz=K)
+_sb(U16, rvl=NJ, sOM=16, lOE=NJ, lp18=NJ, lp7=8, lpo=8, Bo=K, Lo=8, lrv=NJ, lrq=8, lA=28, rkl=NJ, Bp=C, L1=NJ, L2=NJ, L3=NJ, L4=NJ, lo=72,
+    Pp=K, lE=28, lQ=28, lX=28, pls=40 * ROUNDS, pll=40 * ROUNDS)
+for _n, _w in [("qx", C), ("qu", 128), ("qv", 128), ("uo", 128), ("um", 128), ("wq", 512), ("cq", 768), ("gq", GW), ("vq", 128),
+               ("eq", 128 * ROUNDS), ("le", 128 * ROUNDS)]:
+    SCRATCH[_n] = ("sbuf", [128, _w], CODE)
+    SCRATCH[_n + "s"] = ("sbuf", [128, _w], U8)
+
+QS = {"v": "qsv", "a": "qsa", "t": "qst", "g": "qsg"}
+DS = ["dx", "du", "dv", "drv", "dwc", "dws", "dz", "dT1", "dL2", "dL3", "dLo", "dL4", "dP", "dlq", "doc", "dy"]
+SEMAPHORES = list(QS.values()) + DS + ["rl"] + ["ap%d" % _t for _t in range(ROUNDS)] + ["ae%d" % _t for _t in range(ROUNDS)]
+
+
+def make_tracker(g, T):
+    eng = {"v": g.vector, "a": g.scalar, "t": g.tensor, "g": g, "s": g.sync}
+    clk = {q: {} for q in eng}
+    cnt = {}
+    snaps = {}
+    acc = {}
+    seq = [0]
+
+    def hit(a, b):
+        if a[1] >= b[2] or b[1] >= a[2] or a[3] >= b[4] or b[3] >= a[4]:
+            return False
+        return not (a[5] == b[5] and a[5] > 1 and (a[3] - b[3]) % a[5])
+
+    def bank(r):
+        return (r[0], 0, 128, r[3] // 512 * 512, (r[4] + 511) // 512 * 512, 1) if r[0] == "ps" else r
+
+    def merge(q, sem, val):
+        own = clk[q]
+        own[sem] = max(own.get(sem, 0), val)
+        for v, s in snaps.get(sem, []):
+            if v <= val:
+                for a, b in s.items():
+                    own[a] = max(own.get(a, 0), b)
+
+    def emit(q, call, outs, ins, dma=None, remote=False):
+        need = {}
+
+        def want(rec):
+            sem, val, order = rec[2], rec[3], rec[4]
+            if clk[q].get(sem, 0) >= val:
+                return
+            if sem in DS:
+                val = cnt[sem]
+            if need.get(sem, (0, 0))[0] < val:
+                need[sem] = (val, order)
+        for r0 in ins:
+            r = bank(r0)
+            for rec in acc.get(r[0], []):
+                if hit(r, rec[0]) and (rec[1] or (r[0] == "ps" and rec[5] != q)):
+                    want(rec)
+        for r0 in outs:
+            r = bank(r0)
+            for rec in acc.get(r[0], []):
+                if hit(r, rec[0]) and not (rec[5] == q == "t"):
+                    want(rec)
+        for sem, (val, order) in sorted(need.items(), key=lambda e: -e[1][1]):
+            if clk[q].get(sem, 0) < val:
+                eng[q].wait_ge(T.sem[sem], val)
+                merge(q, sem, val)
+        made = call()
+        seq[0] += 1
+        if remote:
+            return
+        sem = dma or QS[q]
+        cnt[sem] = cnt.get(sem, 0) + (16 if dma else 1)
+        made.then_inc(T.sem[sem], 16 if dma else 1)
+        snaps.setdefault(sem, []).append((cnt[sem], dict(clk[q])))
+        for r0, wr in [(r, True) for r in outs] + [(r, False) for r in ins]:
+            r = bank(r0)
+            lst = acc.setdefault(r[0], [])
+            if wr:
+                lst[:] = [e for e in lst if not (e[0][1] >= r[1] and e[0][2] <= r[2] and e[0][3] >= r[3] and e[0][4] <= r[4] and r[5] == 1)]
+            lst.append((r, wr, sem, cnt[sem], seq[0], q, dma))
+
+    def arrive(regs, sem, val):
+        seq[0] += 1
+        for r in regs:
+            acc.setdefault(r[0], []).append((r, True, sem, val, seq[0], "r", sem))
+
+    def finish(extra):
+        for sem in list(cnt):
+            if clk["g"].get(sem, 0) < cnt[sem]:
+                g.wait_ge(T.sem[sem], cnt[sem])
+                merge("g", sem, cnt[sem])
+        for sem, val in extra:
+            if clk["g"].get(sem, 0) < val:
+                g.wait_ge(T.sem[sem], val)
+    return emit, arrive, finish
+
+
+def rank_program(g, core, T, topo):
+    rank = T.rank_of(core)
+    if rank is None:
+        return
+    N = len(T.cores)
+    nxt, prv = T.cores[(rank + 1) % N], T.cores[(rank - 1) % N]
+    A, AF = AluOpType, ActivationFunctionType
+    emit, arrive, finish = make_tracker(g, T)
+
+    def W(n, c0=0, c1=None, s=1, p0=0, p1=128):
+        return (n, p0, p1, c0, c1 if c1 is not None else (SCRATCH[n][1][1] if n in SCRATCH else T[n].shape[1]), s)
+
+    def ap(r):
+        if len(r) == 2:
+            return ap(r[0]).indirect(ap(r[1]))
+        n, p0, p1, c0, c1, s = r
+        return T[n][p0:p1, c0:c1] if s == 1 else T[n][p0:p1, c0:c1:s]
+
+    def by(r):
+        return ap(r).bitcast(dt.uint8)
+
+    def rg(*rs):
+        o = []
+        for r in rs:
+            o += list(r) if len(r) == 2 else [r]
+        return o
+
+    def ind(win, off):
+        return (win, off)
+
+    def tt(out, a, b, op):
+        emit("v", lambda: g.vector.tensor_tensor(ap(out), ap(a), ap(b), op), rg(out), rg(a, b))
+
+    def ts(out, a, s1, op0, s2=None, op1=None):
+        x1, x2 = (ap(s) if isinstance(s, tuple) else s for s in (s1, s2))
+        sc = [s for s in (s1, s2) if isinstance(s, tuple)]
+        if op1 is None:
+            emit("v", lambda: g.vector.tensor_scalar(ap(out), ap(a), x1, None, op0), rg(out), rg(a, *sc))
+        else:
+            emit("v", lambda: g.vector.tensor_scalar(ap(out), ap(a), x1, x2, op0, op1), rg(out), rg(a, *sc))
+
+    def cp(out, a):
+        emit("v", lambda: g.vector.tensor_copy(ap(out), ap(a)), rg(out), rg(a))
+
+    def scatter(win, off, a):
+        emit("v", lambda: g.vector.tensor_copy(ap((win, off)), ap(a)), [win], [off, a])
+
+    def fill(out, val):
+        emit("v", lambda: g.vector.memset(ap(out), val), rg(out), [])
+
+    def scan(out, d0, d1, init, op0, op1):
+        emit("v", lambda: g.vector.tensor_tensor_scan(ap(out), ap(d0), ap(d1), init, op0, op1), [out], [d0, d1])
+
+    def act(out, a, fn, scale=1.0, bias=0.0, accum=None):
+        kw, ins, outs = {}, rg(a), rg(out)
+        if scale != 1.0:
+            kw["scale"] = scale
+        if isinstance(bias, tuple):
+            kw["bias"] = ap(bias)
+            ins.append(bias)
+        elif bias != 0.0:
+            kw["bias"] = bias
+        if accum is not None:
+            kw["accum_out"] = ap(accum)
+            outs.append(accum)
+        emit("a", lambda: g.scalar.activation(ap(out), ap(a), fn, **kw), outs, ins)
+
+    def iota(out, pattern, base=0, cm=0):
+        kw = {} if SCRATCH[out[0]][2] == I32 else {"allow_small_or_imprecise_dtypes": True}
+        emit("g", lambda: g.iota(ap(out), pattern, base, cm, **kw), rg(out), [])
+
+    def asel(out, a, pattern, op, base, cm):
+        emit("g", lambda: g.affine_select(ap(out), ap(a), pattern, op, 0.0, base, cm), rg(out), rg(a))
+
+    def dma(q, sem, out, a, o8=False, a8=False):
+        e = {"s": g.sync, "a": g.scalar}[q]
+        emit(q, lambda: e.dma_start(by(out) if o8 else ap(out), by(a) if a8 else ap(a)), rg(out), rg(a), dma=sem)
+
+    def rows_on(q, sem, out, o0, o1, src, n, d):
+        for p0, p1, to in ((0, 128 - 16 * d, 16 * d), (128 - 16 * d, 128, 0)):
+            if p0 < p1:
+                o, a = W(out, o0, o1, p0=to, p1=to + p1 - p0), W(src, p0=p0, p1=p1)
+                e = {"s": g.sync, "a": g.scalar}[q]
+                emit(q, lambda: e.dma_start(ap(o), T[src][p0:p1:16, 0:n]), [o], [a], dma=sem)
+
+    def quant(n, c0, c1, src):
+        o, s = W(n, c0, c1), W(n + "s", c0, c1)
+        emit("v", lambda: g.vector.quantize_mx(ap(o), ap(s), ap(src)), rg(o, s), rg(src))
+
+    def mm(bank, wn, w0, xn, x0, n, start=True, stop=True):
+        o = W("ps", 512 * bank, 512 * bank + n)
+        w, ws, x, xs = W(wn, w0, w0 + 128), W(wn + "s", w0, w0 + 128), W(xn, x0, x0 + n), W(xn + "s", x0, x0 + n)
+        emit("t", lambda: g.tensor.matmul_mx(ap(o), ap(w), ap(ws), ap(x), ap(xs), start, stop), rg(o), rg(w, ws, x, xs))
+
+    def bk(b, c0, c1):
+        return W("ps", 512 * b + c0, 512 * b + c1)
+
+    def pick(out, off):
+        emit("v", lambda: g.vector.tensor_copy(ap(W(out)).bitcast(dt.uint32), ap(W("qu")).bitcast(dt.uint32).indirect(ap(off))), [W(out)], [W("qu"), off])
+        emit("a", lambda: g.scalar.activation(ap(W(out + "s")), ap(W("qus")).indirect(ap(off)), AF.Copy), [W(out + "s")], [W("qus"), off])
+
+    LF, LH, LB, LHE, LP, LZ, LBZ = (W("pflt", i, i + 1) for i in range(7))
+    PI, LI, LHI, LBI, LPI, LPJ = (W("pint", i, i + 1) for i in range(6))
+    C8, C28, C16, KC = W("cs", 0, 8), W("cs", 32, 60), W("cs", 32, 32 + NJ), W("cs", 64, 64 + NJ)
+    B16, B4 = W("KK", 0, C), W("KK", C, 2 * C)
+
+    def last(out, a, keep):
+        scan(out, keep, a, 0.0, A.mult, A.add)
+
+    def to28(row, tmp, out):
+        scan(tmp, row, W("M1"), 1.0, A.min, A.add)
+        ts(out, (tmp[0], 0, 128, 3, K, 4), 4 * UNIT, A.mult, LBZ, A.add)
+
+    dma("s", "du", W("ub"), W("u"))
+    dma("a", "dx", W("x0"), W("x"))
+    dma("a", "drv", W("rvt"), W("rv"))
+    dma("s", "dwc", W("wq"), W("wc"), o8=True)
+    dma("s", "dws", W("wqs"), W("ws"))
+    dma("s", "dv", W("vb"), W("v"))
+
+    iota(PI, [[0, 1]], 0, 1)
+    iota(C8, [[16, 8]])
+    iota(W("ic"), [[1, C]])
+    iota(C28, [[16, 28]])
+    iota(W("r16"), [[0, NJ], [1, 16]])
+    iota(W("r4"), [[0, 72], [1, 4]])
+    iota(KC, [[-16, NJ]], C - 1)
+    fill(W("nega"), -1.0)
+    ts(LI, PI, 15, A.bitwise_and)
+    cp(W("sOM", 0, 8), C8)
+    ts(W("sOM", 8, 16), C8, 8.0, A.add)
+    cp(LF, LI)
+    ts(LHI, LI, 2, A.logical_shift_right)
+    ts(LBI, LI, 3, A.bitwise_and)
+    for s in range(1, 9):
+        fill(W("G", 288 * s + 288 - 16 * s, 288 * s + 288), 0.0)
+    asel(W("negb"), W("nega"), [[-16, 8], [0, 64]], A.is_ge, 0, 1)
+    asel(W("negb"), W("negb"), [[16, 8], [0, 64]], A.is_ge, 15, -1)
+    asel(W("cb", 4 * CC, 4 * CC + 512), W("negb"), [[0, 32], [1, 4], [-1, 4]], A.is_equal, 0, 0)
+    asel(W("cb", 4 * CT, 4 * CT + 512), W("cb", 4 * CC, 4 * CC + 512), [[1, 128], [0, 4]], A.is_ge, -1, -1)
+    for b in range(4):
+        asel(W("cb", 512 * b, 512 * b + 512), W("nega"), [[-1, 512]], A.is_equal, b, 4)
+    for n in ("Et", "Vt"):
+        asel(W(n, 448, 512), W("nega", 0, 64), [[0, 64]], A.is_ge, -1, 0)
+    iota(W("w", K - 1, K), [[0, 1]])
+    cp(LH, LHI)
+    cp(LB, LBI)
+    ts(LPI, PI, 3.0 * 4, A.add)
+    ts(W("yl"), C16, LF, A.add)
+    ts(W("lOE"), C16, 15.0, A.add)
+    ts(LPJ, LPI, 2, A.logical_shift_right)
+    ts(W("ya"), W("yl"), -8.5, A.add, 1.0 / 18, A.mult)
+    ts(W("yd", 0, NJ), W("yl"), -3.0, A.add, 1.0 / 7, A.mult)
+    ts(LPI, LPJ, 3, A.bitwise_and)
+    cp(W("yi"), W("ya"))
+    cp(W("yj"), W("yd", 0, NJ))
+    ts(W("ya"), W("yl"), 16.0, A.mult)
+    ts(W("m16"), W("r16"), LF, A.is_equal)
+    fill(W("pls"), 0)
+    cp(W("rvl"), W("rvt"))
+    act(W("yo"), W("ic"), AF.Relu, bias=-1.0)
+    act(W("I"), W("ic"), AF.Copy, scale=1.0 / UNIT)
+    act(W("T3"), W("yo"), AF.Identity, scale=-1.0 / UNIT, bias=(C - 1) / UNIT)
+    act(B16, W("r16"), AF.Sign)
+    act(B4, W("r4"), AF.Sign)
+    quant("qu", 0, 128, W("ub"))
+    pick("uo", W("sOM", 0, 8))
+
+    def consts_first():
+        pick("um", W("sOM", 8, 16))
+        ts(W("m4"), W("r4"), LH, A.is_equal)
+        for s in list(range(9, NJ)) + [SLOTS]:
+            act(W("G", 288 * s, 288 * s + 288), W("ic"), AF.Copy, scale=0.0)
+
+    def consts_count():
+        ts(W("yb"), W("yi"), -287.0, A.mult)
+        ts(W("yd", 0, NJ), W("yj"), -111.0, A.mult)
+        ts(W("lrv"), W("yl"), -1.0, A.mult, float(C - 1), A.add)
+        ts(LHE, LH, 8.0, A.mult)
+        cp(LP, LPI)
+        ts(LZ, LH, 0.0, A.is_equal, -4.0 * UNIT, A.mult)
+        ts(W("yc"), C28, 2.0, A.mult, 4.0, A.add)
+        ts(W("lrq", 0, 7), W("yl", 0, 7), -1.0, A.mult, float(K - 1), A.add)
+        ts(W("M1"), W("r4", 0, K), LP, A.is_equal)
+        tt(LBZ, LZ, LB, A.add)
+        ts(W("yc"), W("yc"), LHE, A.add)
+        ts(W("lA"), W("yc"), LB, A.add)
+        quant("cq", CC, CZ, W("cb", 4 * CC, 4 * CZ))
+        tt(W("yb"), W("yb"), W("ya"), A.add)
+        tt(W("yd", 0, NJ), W("yd", 0, NJ), W("ya"), A.add)
+        fill(W("Rs", 0, 1), 0.0)
+        cp(W("lp18"), W("yb"))
+        cp(W("lp7", 0, 7), W("yd", 0, 7))
+        ts(W("lpo", 0, 7), W("yd", 0, 7), 2.0, A.mult, 1.0, A.add)
+        fill(W("Bx", 0, 1), 0.0)
+
+    def pads():
+        for t in range(ROUNDS):
+            dma("s", "dz", W("le", 128 * t + K, 128 * t + 128), W("eq", K, 128), o8=True, a8=True)
+            dma("s", "dz", W("les", 128 * t + K, 128 * t + 128), W("eqs", K, 128))
+
+    ne, np_ = len(topo.engines(core, nxt)[:8]), len(topo.engines(prv, core)[:8])
+    emask = sum(1 << e for e in topo.engines(core, nxt)[:8])
+    rid, pid = topo.addr(nxt, core)
+    rlc = [0]
+
+    def send(out_ap, src, in_ap, sem):
+        emit("g", lambda: g.remote_dma(out_ap, in_ap, T.sem[sem], T.sem.rl, pid, rid, emask), [], [src], remote=True)
+        rlc[0] += ne
+
+    for t in range(ROUNDS):
+        quant("qx", 0, C, W("x0") if t == 0 else W("X", 0, 4 * C))
+        if t == 0:
+            consts_first()
+        mm(0, "uo", 0, "qx", 0, C)
+        mm(1, "um", 0, "qx", 0, C)
+        mm(7, "uo", 0, "qx", 0, C)
+        So = bk(0, 0, C)
+        tt(W("z"), So, W("m16"), A.mult)
+        act(W("sg"), bk(1, 0, C), AF.Sign)
+        last(W("zs"), W("z"), B16)
+        act(W("sg"), W("sg"), AF.Sign, bias=-0.5)
+        for j in SB:
+            r = 160 * (j - SB[-1])
+            act(W("rl", r, r + 16 * j + 16), bk(7, 0, 16 * j + 16), AF.Relu, scale=-1.0, bias=W("zs", 16 * j + 15, 16 * j + 16))
+        for j in SB:
+            s, r = 288 * (NJ - 1 - j), 160 * (j - SB[-1])
+            act(W("G", s, s + 16 * j), W("rl", r, r + 16 * j), AF.Sign, accum=W("Rs", j, j + 1))
+            act(W("G", s + 16 * j, s + 16 * j + 16), W("rl", r + 16 * j, r + 16 * j + 16), AF.Sign)
+        act(W("OE"), ind(W("zs"), W("lOE")), AF.Copy)
+
+        def chunk(k, n):
+            quant("gq", 288 * k, 288 * k + 72 * n, W("G", 1152 * k, 1152 * k + 288 * n))
+            n = min(n, SLOTS - 4 * k)
+            for s in range(max(4 * k - 1, 0), 4 * k + n - (n == 4)):
+                mm(6, "cq", CT if s == NJ else CC, "gq", 72 * s, 128, start=(s == 0), stop=(s == NJ))
+        for s in range(SLOTS):
+            if s % 4 == 1 and s > 1:
+                if t == 0 and s == 5:
+                    consts_count()
+                chunk(s // 4 - 1, 4)
+            j = NJ - 1 - s
+            if j < 0:
+                tt(W("G", 288 * s, 288 * s + 288), So, W("OE"), A.is_equal)
+            elif j not in SB:
+                ts(W("G", 288 * s, 288 * s + 16 * j + 16), bk(0, 0, 16 * j + 16), W("zs", 16 * j + 15, 16 * j + 16), A.is_lt)
+                if j:
+                    act(W("junk", 288 * (s % 4), 288 * (s % 4) + 16 * j), W("G", 288 * s, 288 * s + 16 * j), AF.Copy, accum=W("Rs", j, j + 1))
+        chunk(4, 4 if t == 0 else 3)
+        if t == 0:
+            act(W("T4"), ind(W("T3"), W("rvl")), AF.Copy)
+            act(W("wr"), ind(W("T4"), W("lrv")), AF.Copy)
+        tt(W("Vr"), W("sg"), W("I"), A.add)
+        tt(W("zz", 0, 72), bk(6, 0, 72), W("m4", 0, 72), A.mult)
+        last(W("zz", 72, 144), W("zz", 0, 72), W("KK", C, C + 72))
+        tt(W("R2"), W("Rs"), KC, A.add)
+        tt(W("rk"), W("zz", 75, 144, 4), W("R2"), A.add)
+        cp(W("rkl"), W("rk"))
+        scatter(W("PL"), W("rkl"), W("Vr"))
+        tt(W("am"), W("PL"), W("wr"), A.min)
+        scan(W("Bx", 1, C + 1), W("am"), W("am"), 0.0, A.max, A.max)
+        dma("s", "dT1", W("T1", p0=16), W("Bx", 0, C, p1=112))
+        dma("s", "dT1", W("T1", p1=16), W("Bx", 0, C, p0=112))
+        ts(W("Bp"), ind(W("Bx", 0, C), W("lp18")), UNIT, A.mult)
+        rows_on("s", "dL2", "L2", 0, NJ, "Bp", C, 2)
+        rows_on("s", "dL3", "L3", 0, NJ, "Bp", C, 3)
+        ts(W("Bo"), ind(W("Bx", 0, C), W("lpo", 0, 7)), UNIT, A.mult)
+        rows_on("s", "dLo", "Lo", 0, 7, "Bo", K, 4)
+        rows_on("s", "dL4", "L4", 0, NJ, "Bp", C, 4)
+        rows_on("s", "dL4", "L1", 0, NJ, "Bp", C, 1)
+        if t == 0:
+            quant("cq", CE, CC, W("cb", 0, 4 * CC))
+        for b in range(4):
+            mm(2 + b, "cq", 128 * b, "qx", 0, C)
+        for b in range(4):
+            act(W("X", b, 4 * C, 4), bk(2 + b, 0, C), AF.Copy, scale=-1.0)
+        ts(W("oi1"), W("PL"), UNIT, A.mult, UNIT, A.add)
+        ts(W("oi"), W("oi1"), 1023, A.bitwise_and)
+        tt(W("z"), W("oi"), W("m4"), A.mult)
+        last(W("zs"), W("z"), B4)
+        ts(W("lo"), W("zs", 3, C, 4), 4.0, A.mult, LB, A.add)
+        act(W("FS"), ind(W("X", 0, 4 * C), W("lo")), AF.Copy, scale=2.0 ** -5)
+        act(W("A5"), ind(W("FS"), W("lA")), AF.Copy)
+        odd = [(n, 0, 128, 1, 2 * K, 2) for n in ("T1", "T2", "T3")]
+        tt(W("P1"), odd[0], W("I", 1, 2 * K, 2), A.max)
+        cp(W("T2"), ind(W("T1"), W("L2")))
+        cp(W("T3"), ind(W("T2"), W("L3")))
+        tt(W("P2"), odd[1], W("P1"), A.max)
+        tt(W("P3"), odd[2], W("P2"), A.max)
+        tt(W("P4"), ind(W("T3"), W("Lo", 0, 7)), W("P3"), A.max)
+        ts(W("Pp"), ind(W("P4"), W("lp7", 0, 7)), UNIT, A.mult)
+        o = 40 * t
+        for d in range(5):
+            rows_on("sa"[d % 2], "dP", "pls", o + 8 * d, o + 8 * d + 7, "Pp", K, d)
+        to28(W("P4"), W("wE"), W("lE"))
+        tt(W("Et", 0, 448), ind(W("FS"), W("lE")), W("A5"), A.add)
+        quant("eq", 128 * t, 128 * t + 128, W("Et"))
+        if t == 0:
+            pads()
+        pl, plo = W("pls", o, o + 40), W("pll", o, o + 40)
+        e, eo = W("eq", 128 * t, 128 * t + K), W("le", 128 * t, 128 * t + K)
+        send(by(eo), e, by(e), "ae%d" % t)
+        send(ap(plo), pl, ap(pl), "ap%d" % t)
+        es, eso = W("eqs", 128 * t, 128 * t + K), W("les", 128 * t, 128 * t + K)
+        send(ap(eso), es, ap(es), "ae%d" % t)
+        if t == 0:
+            act(W("T3", 0, K), W("ic", 0, K), AF.Identity, bias=float(C))
+            tt(W("dmy"), W("T3", 0, K), W("m4", 0, K), A.mult)
+        ts(W("yo"), W("oi"), 1.0 / (TAGU * UNIT), A.mult)
+        tt(W("TAG"), W("yo"), W("I"), A.add)
+        act(W("Q1"), ind(W("TAG"), W("L1")), AF.Copy)
+        for d in (2, 3, 4):
+            act(W("Q%d" % d), ind(W("Q%d" % (d - 1)), W("L%d" % d)), AF.Copy)
+        arrive([plo], "ap%d" % t, np_)
+        arrive([eo, eso], "ae%d" % t, 2 * np_)
+        for b in range(4):
+            mm(2 + b, "cq", 128 * b, "le", 128 * t, 128)
+        for b in range(4):
+            act(W("DE", b, 448, 4), bk(2 + b, 0, K), AF.Copy, scale=-0.5)
+        cp(W("q0"), ind(W("Q1"), W("pll", o + 8, o + 15)))
+        tt(W("q1"), ind(W("TAG"), W("pll", o, o + 7)), W("q0"), A.max)
+        tt(W("q0"), ind(W("Q2"), W("pll", o + 16, o + 23)), W("q1"), A.max)
+        tt(W("q1"), ind(W("Q3"), W("pll", o + 24, o + 31)), W("q0"), A.max)
+        tt(W("q4"), ind(W("Q4"), W("pll", o + 32, o + 39)), W("q1"), A.max)
+        to28(W("q4"), W("wE"), W("lQ"))
+        tt(W("Vt", 0, 448), ind(W("FS"), W("lQ")), W("DE"), A.add)
+        act(W("FQ"), ind(W("FS"), W("lQ")), AF.Copy, scale=32.0)
+        quant("vq", 0, 128, W("Vt"))
+        hb = (0, 1, 6, 7)
+        for b in range(4):
+            mm(hb[b], "wq", 128 * b, "vq", 0, 128)
+        tt(W("eqn", 0, K - 1), W("q4", 0, K - 1), W("q4", 1, K), A.is_equal)
+        ts(W("qi"), W("wE", 3, K, 4), TAGU * UNIT, A.mult)
+        tt(W("w", 0, K - 1), W("eqn", 0, K - 1), W("dmy", 0, K - 1), A.mult)
+        ts(W("qj"), W("qi"), 511, A.bitwise_and)
+        last(W("w1"), W("w"), W("KK", C, C + K))
+        for b in range(3):
+            tt(W("CV", b, 448, 4), bk(hb[b], 0, K), W("FQ", b, 448, 4), A.add)
+        tt(W("sel"), W("qj"), W("w1", 3, K, 4), A.max)
+        tt(W("CV", 3, 448, 4), bk(hb[3], 0, K), W("FQ", 3, 448, 4), A.add)
+        ts(W("lX"), W("sel"), 4.0, A.mult, LB, A.add)
+        scatter(W("X"), W("lX"), W("CV"))
+        if t == 0:
+            quant("qv", 0, 128, W("vb"))
+    quant("qx", 0, C, W("X", 0, 4 * C))
+    mm(0, "qv", 0, "qx", 0, C)
+    emit("s", lambda: g.sync.dma_start(T.oc[:, :], by(W("qx"))), [], [W("qx")], dma="doc")
+    ts(W("qz"), ind(W("q4"), W("lrq", 0, 7)), UNIT, A.mult)
+    act(W("yo"), bk(0, 0, C), AF.Copy)
+    ts(W("lqf"), W("qz"), -1.0, A.mult, float(C - 1), A.add)
+    emit("a", lambda: g.scalar.dma_start(T.y[:, :], T.yo[:, :]), [], [W("yo")], dma="dy")
+    for k in range(4):
+        emit("s", lambda: g.sync.dma_start(T.osc[4 * k:4 * k + 4, :], T.qxs[32 * k:32 * k + 4, 0:C]), [], [W("qxs")], dma="doc")
+    emit("s", lambda: g.sync.dma_start(T.lq[:, :], T.lqf[0:128:16, 0:K]), [], [W("lqf")], dma="dlq")
+    finish([("rl", rlc[0])] + [("ap%d" % t, np_) for t in range(ROUNDS)] + [("ae%d" % t, 2 * np_) for t in range(ROUNDS)])

@@ -2,13 +2,29 @@ from concourse.mybir import dt, AluOpType, ActivationFunctionType
 
 C, K, ROUNDS = 288, 112, 3
 NJ = C // 16
-UNIT = 1024.0
-TAGU = 4096.0
+TAG = 2048.0
+MID = 144.0
+BIG = 1024.0
+LIFT = 512.0
+TINY = 1e-36
+MW = C + 16
 CODE, F32, BF, I32, U16, U8 = "float8_e4m3fn_x4", "float32", "bfloat16", "int32", "uint16", "uint8"
-SB = (9, 8, 7)
-SLOTS = NJ + 1
-GW = 72 * SLOTS + 72
-CE, CC, CT, CZ = 0, 512, 640, 768
+ND = 6
+NR = NJ - 1 - ND
+CHUNKS = [[("lt", "eq"), (("r", 11), ("r", 10))], [(("d", 4), ("d", 3)), (("r", 9), ("r", 8))], [(("d", 6), ("d", 5)), (("r", 7), ("r", 6))],
+          [(("d", 2), ("d", 1)), (("r", 5), ("r", 4))], [(("r", 3), ("r", 2)), (("r", 1), None)]]
+
+
+def _cols(plane):
+    return 0 if plane is None else C if plane in ("lt", "eq") else C - 16 * plane[1] if plane[0] == "d" else 16 * plane[1]
+
+
+PAIR, GW = {}, 0
+for _ch in CHUNKS:
+    for _p in _ch:
+        PAIR[_p] = (GW, 128 if _p[0][0] == "r" else 144)
+        GW += PAIR[_p][1]
+CE, CC, CD, CI, CS, CZ = 0, 512, 640, 768, 1024, 1152
 
 SCRATCH = {"ps": ("psum", [128, 4096], F32)}
 
@@ -18,22 +34,20 @@ def _sb(dtype, **names):
         SCRATCH[n] = ("sbuf", [128, w], dtype)
 
 
-_sb(BF, x0=4 * C, X=1600, ub=512, vb=512, nega=512, negb=512, cb=4 * 768, G=4 * GW, m4=C, m16=C, junk=4 * C,
-    FS=4 * C, A5=448, Et=512, Vt=512, DE=448, CV=448)
-_sb(F32, r4=C, r16=C, pflt=8, ic=C, I=C, dmy=K, cs=96, yl=NJ, ya=NJ, yb=NJ, yc=28, yd=28, wr=C,
-    z=C, zs=C, zz=144, KK=2 * C, M1=K, OE=C, sg=C, Vr=C, Rs=NJ, R2=NJ, rk=NJ, PL=C, am=C, rl=480, Bx=292, TAG=C,
-    T1=C, T2=C, T3=C, T4=C, Q1=C, Q2=C, Q3=C, Q4=C, P1=K, P2=K, P3=K, P4=K, w=K, w1=K, wE=K, FQ=448, eqn=K, sel=28, lqf=K,
-    q0=K, q1=K, q4=K, yo=C)
-_sb(I32, rvt=NJ, pint=8, yi=NJ, yj=NJ, oi1=C, oi=C, qi=28, qj=28, qz=K)
-_sb(U16, rvl=NJ, sOM=16, lOE=NJ, lp18=NJ, lp7=8, lpo=8, Bo=K, Lo=8, lrv=NJ, lrq=8, lA=28, rkl=NJ, Bp=C, L1=NJ, L2=NJ, L3=NJ, L4=NJ, lo=72,
-    Pp=K, lE=28, lQ=28, lX=28, pls=40 * ROUNDS, pll=40 * ROUNDS)
-for _n, _w in [("qx", C), ("qu", 128), ("qv", 128), ("uo", 128), ("um", 128), ("wq", 512), ("cq", 768), ("gq", GW), ("vq", 128),
-               ("eq", 128 * ROUNDS), ("le", 128 * ROUNDS)]:
+_sb(BF, x0=4 * C, X=1600, XS=4 * C, ub=512, vb=512, neg=528, OH=528, cb=2560, G=4 * GW, m16=C, e64=128,
+    A5=448, Et=512, Vt=512, DE=448, CV=448, MT=4 * MW, wrb=C, wrS=MW, am=MW, BR=320, TR=320)
+_sb(F32, r4=K, r8=144, r16=C, pflt=24, ic=C, cd=C, dm=28, c16=28, yl=NJ, lf=72, ya=16, yb=16, yc=16,
+    z=C, zs=C, zz=144, B16=C, B8=144, M4=K, M8=144, Mb=NJ, Mc=NJ, OE=C, sg=C, Vr=C, Rs=NJ, PL=C, ab=C, rl=8 * NR * (NR + 1), TG=C,
+    Q1=C, Q2=C, Q3=C, Q4=C, P1=K, P2=K, P4=K, w1=K, wA=K, wE=K, FQ=448, eqn=28, sel=28, lqf=K, q0=K, q1=K, q4=K + 1, yo=C)
+_sb(I32, rvt=NJ, pint=8, yi=16, qi=28, qj=28, qz=K)
+_sb(U16, rvl=NJ, lu=76, lA=28, rkl=NJ, LL=80, Pp=K, lE=28, lQ=28, lX=28, pls=40 * ROUNDS, pll=40 * ROUNDS)
+for _n, _w in [("qx", C), ("qu", 128), ("qv", 128), ("uo", 128), ("um", 128), ("wq", 512), ("cq", CZ), ("gq", GW), ("vq", 128),
+               ("mq", MW), ("zq", 128), ("eq", 128 * ROUNDS), ("le", 128 * ROUNDS)]:
     SCRATCH[_n] = ("sbuf", [128, _w], CODE)
     SCRATCH[_n + "s"] = ("sbuf", [128, _w], U8)
 
 QS = {"v": "qsv", "a": "qsa", "t": "qst", "g": "qsg"}
-DS = ["dx", "du", "dv", "drv", "dwc", "dws", "dz", "dT1", "dL2", "dL3", "dLo", "dL4", "dP", "dlq", "doc", "dy"]
+DS = ["dx", "du", "dv", "drv", "dwc", "dws", "dgq", "dle", "dwr", "dP", "dlq", "doc", "dy"]
 SEMAPHORES = list(QS.values()) + DS + ["rl"] + ["ap%d" % _t for _t in range(ROUNDS)] + ["ae%d" % _t for _t in range(ROUNDS)]
 
 
@@ -170,7 +184,10 @@ def rank_program(g, core, T, topo):
     def scan(out, d0, d1, init, op0, op1):
         emit("v", lambda: g.vector.tensor_tensor_scan(ap(out), ap(d0), ap(d1), init, op0, op1), [out], [d0, d1])
 
-    def act(out, a, fn, scale=1.0, bias=0.0, accum=None):
+    def turn(out, a):
+        emit("v", lambda: g.vector.transpose(ap(out), ap(a)), [out], [a])
+
+    def act(out, a, fn=AF.Identity, scale=1.0, bias=0.0, accum=None):
         kw, ins, outs = {}, rg(a), rg(out)
         if scale != 1.0:
             kw["scale"] = scale
@@ -188,19 +205,16 @@ def rank_program(g, core, T, topo):
         kw = {} if SCRATCH[out[0]][2] == I32 else {"allow_small_or_imprecise_dtypes": True}
         emit("g", lambda: g.iota(ap(out), pattern, base, cm, **kw), rg(out), [])
 
-    def asel(out, a, pattern, op, base, cm):
-        emit("g", lambda: g.affine_select(ap(out), ap(a), pattern, op, 0.0, base, cm), rg(out), rg(a))
+    def asel(out, a, pattern, op, base, cm, other=0.0):
+        emit("g", lambda: g.affine_select(ap(out), ap(a), pattern, op, other, base, cm), rg(out), rg(a))
 
     def dma(q, sem, out, a, o8=False, a8=False):
         e = {"s": g.sync, "a": g.scalar}[q]
         emit(q, lambda: e.dma_start(by(out) if o8 else ap(out), by(a) if a8 else ap(a)), rg(out), rg(a), dma=sem)
 
-    def rows_on(q, sem, out, o0, o1, src, n, d):
-        for p0, p1, to in ((0, 128 - 16 * d, 16 * d), (128 - 16 * d, 128, 0)):
-            if p0 < p1:
-                o, a = W(out, o0, o1, p0=to, p1=to + p1 - p0), W(src, p0=p0, p1=p1)
-                e = {"s": g.sync, "a": g.scalar}[q]
-                emit(q, lambda: e.dma_start(ap(o), T[src][p0:p1:16, 0:n]), [o], [a], dma=sem)
+    def rows_to(q, sem, o, src, g0, g1, n):
+        e = {"s": g.sync, "a": g.scalar}[q]
+        emit(q, lambda: e.dma_start(ap(o), T[src][16 * g0:16 * g1:16, 0:n]), [o], [W(src, p0=16 * g0, p1=16 * g1)], dma=sem)
 
     def quant(n, c0, c1, src):
         o, s = W(n, c0, c1), W(n + "s", c0, c1)
@@ -218,105 +232,137 @@ def rank_program(g, core, T, topo):
         emit("v", lambda: g.vector.tensor_copy(ap(W(out)).bitcast(dt.uint32), ap(W("qu")).bitcast(dt.uint32).indirect(ap(off))), [W(out)], [W("qu"), off])
         emit("a", lambda: g.scalar.activation(ap(W(out + "s")), ap(W("qus")).indirect(ap(off)), AF.Copy), [W(out + "s")], [W("qus"), off])
 
-    LF, LH, LB, LHE, LP, LZ, LBZ = (W("pflt", i, i + 1) for i in range(7))
-    PI, LI, LHI, LBI, LPI, LPJ = (W("pint", i, i + 1) for i in range(6))
-    C8, C28, C16, KC = W("cs", 0, 8), W("cs", 32, 60), W("cs", 32, 32 + NJ), W("cs", 64, 64 + NJ)
-    B16, B4 = W("KK", 0, C), W("KK", C, 2 * C)
+    LF, L2, L4, LQ, SF, EF, LB, LR, LA, LM, K2, K3, K4, K5, K6, KP = (W("pflt", i, i + 1) for i in range(16))
+    PI = W("pint", 0, 1)
+    C16 = W("c16", 0, NJ)
+    sO, sM, lOE, lrv, lrq, lsel, lp7 = (W("lu", a, b) for a, b in ((0, 8), (8, 16), (16, 34), (34, 52), (52, 59), (60, 65), (68, 75)))
 
-    def last(out, a, keep):
-        scan(out, keep, a, 0.0, A.mult, A.add)
+    def columns(row, tmp, i1, i2, out):
+        scan(tmp, row, W("M4"), LIFT, A.min, A.add)
+        ts(i1, (tmp[0], 0, 128, 3, K, 4), 4 * TAG, A.mult, LB, A.add)
+        ts(i2, i1, int(4 * TAG) - 1, A.bitwise_and)
+        cp(out, i2)
 
-    def to28(row, tmp, out):
-        scan(tmp, row, W("M1"), 1.0, A.min, A.add)
-        ts(out, (tmp[0], 0, 128, 3, K, 4), 4 * UNIT, A.mult, LBZ, A.add)
+    def lane(plane):
+        for p, (o, n) in PAIR.items():
+            if plane in p:
+                return W("G", 4 * o + p.index(plane), 4 * o + p.index(plane) + 2 * _cols(plane) - 1, 2)
 
-    dma("s", "du", W("ub"), W("u"))
-    dma("a", "dx", W("x0"), W("x"))
+    def gap(p):
+        o, n = PAIR[p]
+        return W("G", 4 * o + 2 * min(_cols(p[0]), _cols(p[1])), 4 * (o + words(p)))
+
+    def words(p):
+        return max(_cols(p[0]), _cols(p[1])) // 2 if p in [ch[-1] for ch in CHUNKS] else PAIR[p][1]
+
+    def zeros(n, c0, c1):
+        dma("s", "d" + n, W(n, c0, c1), W("zq", 0, c1 - c0), o8=True, a8=True)
+        dma("s", "d" + n, W(n + "s", c0, c1), W("zqs", 0, c1 - c0))
+
     dma("a", "drv", W("rvt"), W("rv"))
-    dma("s", "dwc", W("wq"), W("wc"), o8=True)
-    dma("s", "dws", W("wqs"), W("ws"))
-    dma("s", "dv", W("vb"), W("v"))
+    dma("s", "du", W("ub"), W("u"))
+    dma("s", "dx", W("x0"), W("x"))
 
     iota(PI, [[0, 1]], 0, 1)
-    iota(C8, [[16, 8]])
-    iota(W("ic"), [[1, C]])
-    iota(C28, [[16, 28]])
+    iota(W("c16"), [[16, 28]])
+    iota(W("lf", 0, 16), [[8, 2], [16, 8]])
     iota(W("r16"), [[0, NJ], [1, 16]])
-    iota(W("r4"), [[0, 72], [1, 4]])
-    iota(KC, [[-16, NJ]], C - 1)
-    fill(W("nega"), -1.0)
-    ts(LI, PI, 15, A.bitwise_and)
-    cp(W("sOM", 0, 8), C8)
-    ts(W("sOM", 8, 16), C8, 8.0, A.add)
-    cp(LF, LI)
-    ts(LHI, LI, 2, A.logical_shift_right)
-    ts(LBI, LI, 3, A.bitwise_and)
-    for s in range(1, 9):
-        fill(W("G", 288 * s + 288 - 16 * s, 288 * s + 288), 0.0)
-    asel(W("negb"), W("nega"), [[-16, 8], [0, 64]], A.is_ge, 0, 1)
-    asel(W("negb"), W("negb"), [[16, 8], [0, 64]], A.is_ge, 15, -1)
-    asel(W("cb", 4 * CC, 4 * CC + 512), W("negb"), [[0, 32], [1, 4], [-1, 4]], A.is_equal, 0, 0)
-    asel(W("cb", 4 * CT, 4 * CT + 512), W("cb", 4 * CC, 4 * CC + 512), [[1, 128], [0, 4]], A.is_ge, -1, -1)
-    for b in range(4):
-        asel(W("cb", 512 * b, 512 * b + 512), W("nega"), [[-1, 512]], A.is_equal, b, 4)
-    for n in ("Et", "Vt"):
-        asel(W(n, 448, 512), W("nega", 0, 64), [[0, 64]], A.is_ge, -1, 0)
-    iota(W("w", K - 1, K), [[0, 1]])
-    cp(LH, LHI)
-    cp(LB, LBI)
-    ts(LPI, PI, 3.0 * 4, A.add)
-    ts(W("yl"), C16, LF, A.add)
-    ts(W("lOE"), C16, 15.0, A.add)
-    ts(LPJ, LPI, 2, A.logical_shift_right)
-    ts(W("ya"), W("yl"), -8.5, A.add, 1.0 / 18, A.mult)
-    ts(W("yd", 0, NJ), W("yl"), -3.0, A.add, 1.0 / 7, A.mult)
-    ts(LPI, LPJ, 3, A.bitwise_and)
-    cp(W("yi"), W("ya"))
-    cp(W("yj"), W("yd", 0, NJ))
-    ts(W("ya"), W("yl"), 16.0, A.mult)
-    ts(W("m16"), W("r16"), LF, A.is_equal)
-    fill(W("pls"), 0)
+    iota(W("r8"), [[0, NJ], [2, 8]], 1)
+    fill(W("neg"), -1.0)
+    for i, (sh, mask) in enumerate(((0, 15), (0, 14), (0, 12), (0, 3), (0, 1), (4, 1))):
+        ts(W("pint", i + 1, i + 2), PI, sh, A.logical_shift_right, mask, A.bitwise_and)
+    cp(W("pflt", 0, 6), W("pint", 1, 7))
+    fill(W("cb"), 0.0)
+    act(W("lf", 16, 34), C16, bias=15.0)
+    act(W("wrS"), W("neg", 0, MW), AF.Copy, scale=MID)
+    act(W("yl"), C16, bias=LF)
+    act(LM, L2, AF.Relu, scale=-10 * BIG, bias=10 * BIG)
+    act(K2, L2, scale=-BIG / 2, bias=7 * BIG + C - 1)
+    act(W("lf", 34, 52), W("yl"), scale=-1.0, bias=C - 1.0)
+    act(W("lf", 52, 59), W("yl", 0, 7), scale=-1.0, bias=K - 1.0)
+    act(W("Mb"), C16, scale=-1.0, bias=LM)
+    act(LR, LM, scale=-1.0, bias=K2)
+    quant("zq", 0, 128, W("cb", 2048, 2560))
+    cp(W("lu", 0, 59), W("lf", 0, 59))
     cp(W("rvl"), W("rvt"))
-    act(W("yo"), W("ic"), AF.Relu, bias=-1.0)
-    act(W("I"), W("ic"), AF.Copy, scale=1.0 / UNIT)
-    act(W("T3"), W("yo"), AF.Identity, scale=-1.0 / UNIT, bias=(C - 1) / UNIT)
-    act(B16, W("r16"), AF.Sign)
-    act(B4, W("r4"), AF.Sign)
+    pairs = list(PAIR)
+    for p in pairs[1::2]:
+        o, n = PAIR[p]
+        zeros("gq", (o + words(p)) // 16 * 16, o + n)
+    ts(W("m16"), W("r16"), LF, A.is_equal)
+    act(W("B16"), W("r16"), AF.Sign)
+    act(W("zz"), W("r8"), AF.Sign, scale=-1.0, bias=L2)
+    act(W("B8"), W("r8"), AF.Sign, bias=-1.0)
+    act(W("M8"), W("zz"), scale=5 * BIG, bias=4 * BIG)
+    asel(W("e64", 0, 64), W("neg", 0, 64), [[-16, 8], [0, 8]], A.is_ge, 0, 1)
+    asel(W("e64", 64, 128), W("e64", 0, 64), [[16, 8], [0, 8]], A.is_ge, 15, -1)
+    iota(W("ic"), [[1, C]])
+    asel(W("cb", 513, 1024, 8), W("e64", 64, 128), [[16, 8], [2, 8]], A.is_gt, 0, -1)
+    asel(W("cb", 519, 1024, 8), W("e64", 64, 128), [[16, 8], [2, 8]], A.is_ge, 0, -1)
+    for e in (0, 1, 6, 7, 512, 518):
+        act(W("cb", e, e // 512 * 512 + 512, 8), W("e64", 64, 128), AF.Copy)
     quant("qu", 0, 128, W("ub"))
-    pick("uo", W("sOM", 0, 8))
+    pick("uo", sO)
+    act(W("yo"), W("ic"), AF.Relu, bias=-1.0)
+    for p in pairs[1::2]:
+        o = gap(p)
+        iota(o, [[0, o[4] - o[3]]])
+    for e in (0, 2, 513, 515):
+        o = W("cb", 1024 + e, 1024 + e // 512 * 512 + 512, 4)
+        asel(o, o, [[1, 128]], A.not_equal, 0, -1, 1.0)
+    iota(W("Rs", 0, ND + 1), [[0, ND + 1]])
+    iota(W("r4"), [[0, 28], [4, 4]], 2)
+    iota(W("yc"), [[178, 2], [0, 8]], -289)
+    asel(W("OH"), W("neg"), [[-1, 528]], A.is_equal, 3, 4)
+    for k in range(2):
+        for base in (-64, 64):
+            o = W("cb", 2048 + k, 2560, 4)
+            asel(o, o, [[32, 4], [1000, 4], [16, 8]], A.not_equal, base - 1000 * k, -1, LIFT)
+    iota(W("BR", MW, 320), [[0, 320 - MW]])
+    for n in ("Et", "Vt"):
+        iota(W(n, 448, 512), [[0, 64]])
+    iota(W("q4", K, K + 1), [[0, 1]], int(LIFT))
 
     def consts_first():
-        pick("um", W("sOM", 8, 16))
-        ts(W("m4"), W("r4"), LH, A.is_equal)
-        for s in list(range(9, NJ)) + [SLOTS]:
-            act(W("G", 288 * s, 288 * s + 288), W("ic"), AF.Copy, scale=0.0)
+        pick("um", sM)
+        act(W("Q4"), ind(W("yo"), W("rvl")), scale=-1.0, bias=C - 1 - MID)
+        for p in pairs[2::2]:
+            fill(gap(p), 0.0)
+        dma("s", "dwc", W("wq"), W("wc"), o8=True)
+        dma("s", "dws", W("wqs"), W("ws"))
+        dma("s", "dv", W("vb"), W("v"))
 
-    def consts_count():
-        ts(W("yb"), W("yi"), -287.0, A.mult)
-        ts(W("yd", 0, NJ), W("yj"), -111.0, A.mult)
-        ts(W("lrv"), W("yl"), -1.0, A.mult, float(C - 1), A.add)
-        ts(LHE, LH, 8.0, A.mult)
-        cp(LP, LPI)
-        ts(LZ, LH, 0.0, A.is_equal, -4.0 * UNIT, A.mult)
-        ts(W("yc"), C28, 2.0, A.mult, 4.0, A.add)
-        ts(W("lrq", 0, 7), W("yl", 0, 7), -1.0, A.mult, float(K - 1), A.add)
-        ts(W("M1"), W("r4", 0, K), LP, A.is_equal)
-        tt(LBZ, LZ, LB, A.add)
-        ts(W("yc"), W("yc"), LHE, A.add)
-        ts(W("lA"), W("yc"), LB, A.add)
-        quant("cq", CC, CZ, W("cb", 4 * CC, 4 * CZ))
+    def consts_rv():
+        act(W("wrb"), ind(W("Q4"), lrv), AF.Copy)
+        act(W("cd"), W("ic"), scale=1.0 / TAG, bias=1.0 / TAG)
+        for k in range(2):
+            for a in range(4):
+                g0 = (2 * a - 4) % 8
+                for r0, r1 in ((0, min(5, 8 - g0)), (min(5, 8 - g0), 5)):
+                    if r0 < r1:
+                        n = C if k == 0 else C - 1
+                        o = W("wrS", 1 + 16 * k, 1 + 16 * k + n, p0=32 * a + 8 * k + r0, p1=32 * a + 8 * k + r1)
+                        rows_to("s", "dwr", o, "wrb", (g0 + r0) % 8, (g0 + r0) % 8 + r1 - r0, n)
+
+    def consts_bounds():
+        act(K3, EF, scale=-48.0, bias=24.0)
+        act(K4, EF, scale=9.0, bias=3.0)
+        act(W("ya", 0, 8), W("yl", 0, 8), scale=1.0 / 18, bias=-8.5 / 18)
+        act(W("ya", 8, 16), W("yl", 0, 8), scale=1.0 / 7, bias=-3.0 / 7)
+        act(W("yb", 8, 16), W("yl", 0, 8), scale=16.0)
+        ts(KP, K3, SF, A.mult, K4, A.add)
+        cp(W("yi"), W("ya"))
+        act(W("w1"), W("r4"), AF.Sign, scale=-1.0, bias=L4)
+        act(K5, L4, AF.Relu, scale=-LIFT, bias=LIFT)
+        act(LB, LQ, bias=3 * 4 * TAG - 4)
+        act(W("yb", 0, 8), W("yl", 0, 8), scale=16.0, bias=KP)
+        tt(W("ya"), W("yi"), W("yc"), A.mult)
+        act(W("M4"), W("w1"), scale=(LIFT + 1) / 2, bias=(LIFT - 1) / 2)
+        act(K6, L4, scale=-TAG, bias=LB)
         tt(W("yb"), W("yb"), W("ya"), A.add)
-        tt(W("yd", 0, NJ), W("yd", 0, NJ), W("ya"), A.add)
-        fill(W("Rs", 0, 1), 0.0)
-        cp(W("lp18"), W("yb"))
-        cp(W("lp7", 0, 7), W("yd", 0, 7))
-        ts(W("lpo", 0, 7), W("yd", 0, 7), 2.0, A.mult, 1.0, A.add)
-        fill(W("Bx", 0, 1), 0.0)
-
-    def pads():
-        for t in range(ROUNDS):
-            dma("s", "dz", W("le", 128 * t + K, 128 * t + 128), W("eq", K, 128), o8=True, a8=True)
-            dma("s", "dz", W("les", 128 * t + K, 128 * t + 128), W("eqs", K, 128))
+        act(W("M4", 3, K, 4), W("r4", 0, 28), scale=0.0, bias=K5)
+        act(LA, K5, scale=-4 * TAG, bias=K6)
+        cp(W("lu", 60, 76), W("yb"))
 
     ne, np_ = len(topo.engines(core, nxt)[:8]), len(topo.engines(prv, core)[:8])
     emask = sum(1 << e for e in topo.engines(core, nxt)[:8])
@@ -334,137 +380,161 @@ def rank_program(g, core, T, topo):
         mm(0, "uo", 0, "qx", 0, C)
         mm(1, "um", 0, "qx", 0, C)
         mm(7, "uo", 0, "qx", 0, C)
+
+        def unpack():
+            for b in range(4):
+                mm(2 + b, "cq", 128 * b, "qx", 0, C)
+        if t:
+            unpack()
         So = bk(0, 0, C)
         tt(W("z"), So, W("m16"), A.mult)
-        act(W("sg"), bk(1, 0, C), AF.Sign)
-        last(W("zs"), W("z"), B16)
-        act(W("sg"), W("sg"), AF.Sign, bias=-0.5)
-        for j in SB:
-            r = 160 * (j - SB[-1])
-            act(W("rl", r, r + 16 * j + 16), bk(7, 0, 16 * j + 16), AF.Relu, scale=-1.0, bias=W("zs", 16 * j + 15, 16 * j + 16))
-        for j in SB:
-            s, r = 288 * (NJ - 1 - j), 160 * (j - SB[-1])
-            act(W("G", s, s + 16 * j), W("rl", r, r + 16 * j), AF.Sign, accum=W("Rs", j, j + 1))
-            act(W("G", s + 16 * j, s + 16 * j + 16), W("rl", r + 16 * j, r + 16 * j + 16), AF.Sign)
-        act(W("OE"), ind(W("zs"), W("lOE")), AF.Copy)
+        act(W("sg"), bk(1, 0, C), AF.Sign, bias=-TINY)
+        scan(W("zs"), W("B16"), W("z"), 0.0, A.mult, A.add)
+        if t == 0:
+            consts_rv()
+        act(W("OE"), ind(W("zs"), lOE), AF.Copy)
+        if t == 0:
+            quant("cq", CC, CI, W("cb", 0, 1024))
+        scan(W("Vr"), W("cd"), W("sg"), 0.0, A.max, A.mult)
 
-        def chunk(k, n):
-            quant("gq", 288 * k, 288 * k + 72 * n, W("G", 1152 * k, 1152 * k + 288 * n))
-            n = min(n, SLOTS - 4 * k)
-            for s in range(max(4 * k - 1, 0), 4 * k + n - (n == 4)):
-                mm(6, "cq", CT if s == NJ else CC, "gq", 72 * s, 128, start=(s == 0), stop=(s == NJ))
-        for s in range(SLOTS):
-            if s % 4 == 1 and s > 1:
-                if t == 0 and s == 5:
-                    consts_count()
-                chunk(s // 4 - 1, 4)
-            j = NJ - 1 - s
-            if j < 0:
-                tt(W("G", 288 * s, 288 * s + 288), So, W("OE"), A.is_equal)
-            elif j not in SB:
-                ts(W("G", 288 * s, 288 * s + 16 * j + 16), bk(0, 0, 16 * j + 16), W("zs", 16 * j + 15, 16 * j + 16), A.is_lt)
-                if j:
-                    act(W("junk", 288 * (s % 4), 288 * (s % 4) + 16 * j), W("G", 288 * s, 288 * s + 16 * j), AF.Copy, accum=W("Rs", j, j + 1))
-        chunk(4, 4 if t == 0 else 3)
+        def relu(i):
+            o = 8 * i * (i - 1)
+            act(W("rl", o, o + 16 * i), bk(7, 0, 16 * i), AF.Relu, scale=-1.0, bias=W("zs", 16 * (ND + i) + 15, 16 * (ND + i) + 16))
+
+        def sign(i):
+            o = 8 * i * (i - 1)
+            act(lane(("r", i)), W("rl", o, o + 16 * i), AF.Sign, accum=W("Rs", ND + i, ND + i + 1))
+
+        def chunk(k):
+            ch = CHUNKS[k]
+            o0, end = PAIR[ch[0]][0], PAIR[ch[-1]][0] + words(ch[-1])
+            quant("gq", o0, end, W("G", 4 * o0, 4 * end))
+            for p in ch:
+                o, n = PAIR[p]
+                if p[0][0] == "d":
+                    for e in range(2):
+                        mm(1, "cq", CI + 128 * e, "gq", o - 8 * p[e][1], n, start=(k == 1 and e == 0), stop=(p[e][1] == 1))
+                mm(6, "cq", CD if p[0] == "lt" else CC, "gq", o, n, start=(o == 0), stop=(p == pairs[-1]))
+        relu(NR)
+        for i in range(NR, 0, -1):
+            if i > 1:
+                relu(i - 1)
+            sign(i)
+        tt(lane("lt"), So, W("OE"), A.is_lt)
+        tt(lane("eq"), So, W("OE"), A.is_equal)
+        for k in range(1, 4):
+            for d in CHUNKS[k][0]:
+                tt(lane(d), bk(0, 0, _cols(d)), W("OE", 16 * d[1], C), A.is_lt)
+            if t == 0 and k == 2:
+                quant("cq", CI, CS, W("cb", 1024, 2048))
+            chunk(k - 1)
+        chunk(3)
         if t == 0:
-            act(W("T4"), ind(W("T3"), W("rvl")), AF.Copy)
-            act(W("wr"), ind(W("T4"), W("lrv")), AF.Copy)
-        tt(W("Vr"), W("sg"), W("I"), A.add)
-        tt(W("zz", 0, 72), bk(6, 0, 72), W("m4", 0, 72), A.mult)
-        last(W("zz", 72, 144), W("zz", 0, 72), W("KK", C, C + 72))
-        tt(W("R2"), W("Rs"), KC, A.add)
-        tt(W("rk"), W("zz", 75, 144, 4), W("R2"), A.add)
-        cp(W("rkl"), W("rk"))
-        scatter(W("PL"), W("rkl"), W("Vr"))
-        tt(W("am"), W("PL"), W("wr"), A.min)
-        scan(W("Bx", 1, C + 1), W("am"), W("am"), 0.0, A.max, A.max)
-        dma("s", "dT1", W("T1", p0=16), W("Bx", 0, C, p1=112))
-        dma("s", "dT1", W("T1", p1=16), W("Bx", 0, C, p0=112))
-        ts(W("Bp"), ind(W("Bx", 0, C), W("lp18")), UNIT, A.mult)
-        rows_on("s", "dL2", "L2", 0, NJ, "Bp", C, 2)
-        rows_on("s", "dL3", "L3", 0, NJ, "Bp", C, 3)
-        ts(W("Bo"), ind(W("Bx", 0, C), W("lpo", 0, 7)), UNIT, A.mult)
-        rows_on("s", "dLo", "Lo", 0, 7, "Bo", K, 4)
-        rows_on("s", "dL4", "L4", 0, NJ, "Bp", C, 4)
-        rows_on("s", "dL4", "L1", 0, NJ, "Bp", C, 1)
+            fill(W("MT"), 0.0)
+        chunk(4)
+        scan(W("zz"), W("B8"), bk(1, 0, 144), 0.0, A.mult, A.add)
         if t == 0:
-            quant("cq", CE, CC, W("cb", 0, 4 * CC))
-        for b in range(4):
-            mm(2 + b, "cq", 128 * b, "qx", 0, C)
-        for b in range(4):
+            consts_bounds()
+        tt(W("Mc"), W("zz", 7, 144, 8), W("Mb"), A.add)
+        for b in range(4 if t else 0):
             act(W("X", b, 4 * C, 4), bk(2 + b, 0, C), AF.Copy, scale=-1.0)
-        ts(W("oi1"), W("PL"), UNIT, A.mult, UNIT, A.add)
-        ts(W("oi"), W("oi1"), 1023, A.bitwise_and)
-        tt(W("z"), W("oi"), W("m4"), A.mult)
-        last(W("zs"), W("z"), B4)
-        ts(W("lo"), W("zs", 3, C, 4), 4.0, A.mult, LB, A.add)
-        act(W("FS"), ind(W("X", 0, 4 * C), W("lo")), AF.Copy, scale=2.0 ** -5)
-        act(W("A5"), ind(W("FS"), W("lA")), AF.Copy)
-        odd = [(n, 0, 128, 1, 2 * K, 2) for n in ("T1", "T2", "T3")]
-        tt(W("P1"), odd[0], W("I", 1, 2 * K, 2), A.max)
-        cp(W("T2"), ind(W("T1"), W("L2")))
-        cp(W("T3"), ind(W("T2"), W("L3")))
-        tt(W("P2"), odd[1], W("P1"), A.max)
-        tt(W("P3"), odd[2], W("P2"), A.max)
-        tt(W("P4"), ind(W("T3"), W("Lo", 0, 7)), W("P3"), A.max)
-        ts(W("Pp"), ind(W("P4"), W("lp7", 0, 7)), UNIT, A.mult)
+        tt(W("M8", 7, 144, 8), W("Rs"), W("Mc"), A.add)
+        scan(W("zz"), bk(6, 0, 144), W("M8"), 4 * BIG, A.min, A.add)
+        ts(W("rkl"), W("zz", 7, 144, 8), LR, A.add)
+        if t == 0:
+            quant("cq", CS, CZ, W("cb", 2048, 2560))
+        scatter(W("PL"), W("rkl"), W("Vr"))
+        ts(W("MT", 4, 4 * C + 4, 4), W("PL"), 0.0, A.is_gt, -0.5, A.add)
+        act(W("MT", 69, 4 * MW, 4), W("PL", 0, C - 1), AF.Sign)
+        act(W("ab"), W("PL"), AF.Abs)
+        quant("mq", 0, MW, W("MT"))
+        mm(1, "cq", CS, "mq", 0, MW)
+        if t == 0:
+            for b in range(4):
+                quant("cq", 128 * b, 128 * b + 128, W("OH", 3 - b, 515 - b))
+            unpack()
+            for b in range(4):
+                act(W("X", b, 4 * C, 4), bk(2 + b, 0, C), AF.Copy, scale=-1.0)
+        scan(W("TG"), W("ic"), W("ab"), 0.0, A.max, A.add)
+        tt(W("am"), bk(1, 0, MW), W("wrS"), A.min)
+        scan(W("wA"), W("ab", 1, 2 * K, 2), W("M4"), LIFT, A.min, A.add)
+        scan(W("BR", 0, MW), W("am"), W("am"), -MID, A.max, A.max)
+        ts(W("lA"), W("wA", 3, K, 4), 4 * TAG, A.mult, LA, A.add)
+        if t:
+            act(W("A5"), ind(W("X", 0, 4 * C), W("lA")), AF.Copy)
+        odd = {n: (n, 0, 128, 1, 2 * K, 2) for n in ("TG", "Q1", "Q2", "Q3", "Q4")}
+        turn(W("TR"), W("BR"))
+        ts(W("LL"), ind(W("TR"), lsel), MID, A.add)
+        for d in range(1, 5):
+            H = 10 if d == 1 else 6
+            src, o = W("TG") if d == 1 else W("Q%d" % (d - 1)), NJ * (d - 1)
+            cp(W("Q%d" % d, 0, 16 * H), ind(src, W("LL", o, o + H)))
+            act(W("Q%d" % d, 16 * H, C), ind(src, W("LL", o + H, o + NJ)), AF.Copy)
+            if d == 2:
+                scan(W("P1"), odd["TG"], odd["Q1"], 0.0, A.max, A.max)
+            if d == 3:
+                scan(W("P2"), W("P1"), odd["Q2"], 0.0, A.max, A.max)
+            if d == 4:
+                scan(W("P1"), W("P2"), odd["Q3"], 0.0, A.max, A.max)
+        scan(W("P4"), W("P1"), odd["Q4"], 0.0, A.max, A.max)
+        if t == 0:
+            act(W("A5"), ind(W("X", 0, 4 * C), W("lA")), AF.Copy)
+            fill(W("pls"), 0)
+            for u in range(ROUNDS):
+                zeros("le", 128 * u + K, 128 * u + 128)
+        ts(W("Pp"), ind(W("P4"), lp7), 1.0, A.mult)
         o = 40 * t
         for d in range(5):
-            rows_on("sa"[d % 2], "dP", "pls", o + 8 * d, o + 8 * d + 7, "Pp", K, d)
-        to28(W("P4"), W("wE"), W("lE"))
-        tt(W("Et", 0, 448), ind(W("FS"), W("lE")), W("A5"), A.add)
+            for g0, g1, to in ((0, 8 - d, 16 * d), (8 - d, 8, 0)):
+                if g0 < g1:
+                    rows_to("sa"[g0 > 0], "dP", W("pls", o + 8 * d, o + 8 * d + 7, p0=to, p1=to + 16 * (g1 - g0)), "Pp", g0, g1, K)
+        columns(W("P4"), W("wE"), W("qi"), W("qj"), W("lE"))
+        tt(W("Et", 0, 448), ind(W("X", 0, 4 * C), W("lE")), W("A5"), A.add)
         quant("eq", 128 * t, 128 * t + 128, W("Et"))
-        if t == 0:
-            pads()
         pl, plo = W("pls", o, o + 40), W("pll", o, o + 40)
         e, eo = W("eq", 128 * t, 128 * t + K), W("le", 128 * t, 128 * t + K)
-        send(by(eo), e, by(e), "ae%d" % t)
         send(ap(plo), pl, ap(pl), "ap%d" % t)
+        send(by(eo), e, by(e), "ae%d" % t)
         es, eso = W("eqs", 128 * t, 128 * t + K), W("les", 128 * t, 128 * t + K)
         send(ap(eso), es, ap(es), "ae%d" % t)
+        ts(W("XS"), W("X", 0, 4 * C), 2.0 ** -5, A.mult)
         if t == 0:
-            act(W("T3", 0, K), W("ic", 0, K), AF.Identity, bias=float(C))
-            tt(W("dmy"), W("T3", 0, K), W("m4", 0, K), A.mult)
-        ts(W("yo"), W("oi"), 1.0 / (TAGU * UNIT), A.mult)
-        tt(W("TAG"), W("yo"), W("I"), A.add)
-        act(W("Q1"), ind(W("TAG"), W("L1")), AF.Copy)
-        for d in (2, 3, 4):
-            act(W("Q%d" % d), ind(W("Q%d" % (d - 1)), W("L%d" % d)), AF.Copy)
+            act(W("dm"), W("c16"), bias=LF)
+            act(W("dm"), W("dm"), bias=4.0 * C)
+            quant("qv", 0, 128, W("vb"))
         arrive([plo], "ap%d" % t, np_)
         arrive([eo, eso], "ae%d" % t, 2 * np_)
         for b in range(4):
             mm(2 + b, "cq", 128 * b, "le", 128 * t, 128)
         for b in range(4):
-            act(W("DE", b, 448, 4), bk(2 + b, 0, K), AF.Copy, scale=-0.5)
+            act(W("DE", b, 448, 4), bk(2 + b, 0, K), AF.Copy, scale=-2.0 ** -6)
+        q4 = W("q4", 0, K)
         cp(W("q0"), ind(W("Q1"), W("pll", o + 8, o + 15)))
-        tt(W("q1"), ind(W("TAG"), W("pll", o, o + 7)), W("q0"), A.max)
+        tt(W("q1"), ind(W("TG"), W("pll", o, o + 7)), W("q0"), A.max)
         tt(W("q0"), ind(W("Q2"), W("pll", o + 16, o + 23)), W("q1"), A.max)
         tt(W("q1"), ind(W("Q3"), W("pll", o + 24, o + 31)), W("q0"), A.max)
-        tt(W("q4"), ind(W("Q4"), W("pll", o + 32, o + 39)), W("q1"), A.max)
-        to28(W("q4"), W("wE"), W("lQ"))
-        tt(W("Vt", 0, 448), ind(W("FS"), W("lQ")), W("DE"), A.add)
-        act(W("FQ"), ind(W("FS"), W("lQ")), AF.Copy, scale=32.0)
+        tt(q4, ind(W("Q4"), W("pll", o + 32, o + 39)), W("q1"), A.max)
+        columns(q4, W("wE"), W("qi"), W("qj"), W("lQ"))
+        tt(W("Vt", 0, 448), ind(W("XS"), W("lQ")), W("DE"), A.add)
+        act(W("FQ"), ind(W("X", 0, 4 * C), W("lQ")), AF.Copy)
         quant("vq", 0, 128, W("Vt"))
         hb = (0, 1, 6, 7)
         for b in range(4):
             mm(hb[b], "wq", 128 * b, "vq", 0, 128)
-        tt(W("eqn", 0, K - 1), W("q4", 0, K - 1), W("q4", 1, K), A.is_equal)
-        ts(W("qi"), W("wE", 3, K, 4), TAGU * UNIT, A.mult)
-        tt(W("w", 0, K - 1), W("eqn", 0, K - 1), W("dmy", 0, K - 1), A.mult)
-        ts(W("qj"), W("qi"), 511, A.bitwise_and)
-        last(W("w1"), W("w"), W("KK", C, C + K))
-        for b in range(3):
-            tt(W("CV", b, 448, 4), bk(hb[b], 0, K), W("FQ", b, 448, 4), A.add)
-        tt(W("sel"), W("qj"), W("w1", 3, K, 4), A.max)
+        scan(W("w1"), W("q4", 1, K + 1), W("M4"), LIFT, A.min, A.add)
+        tt(W("CV", 0, 448, 4), bk(hb[0], 0, K), W("FQ", 0, 448, 4), A.add)
+        tt(W("eqn"), W("wE", 3, K, 4), W("w1", 3, K, 4), A.is_equal)
+        tt(W("CV", 1, 448, 4), bk(hb[1], 0, K), W("FQ", 1, 448, 4), A.add)
+        tt(W("eqn"), W("eqn"), W("dm"), A.mult)
+        tt(W("CV", 2, 448, 4), bk(hb[2], 0, K), W("FQ", 2, 448, 4), A.add)
+        tt(W("sel"), W("qj"), W("eqn"), A.max)
         tt(W("CV", 3, 448, 4), bk(hb[3], 0, K), W("FQ", 3, 448, 4), A.add)
-        ts(W("lX"), W("sel"), 4.0, A.mult, LB, A.add)
+        cp(W("lX"), W("sel"))
         scatter(W("X"), W("lX"), W("CV"))
-        if t == 0:
-            quant("qv", 0, 128, W("vb"))
     quant("qx", 0, C, W("X", 0, 4 * C))
     mm(0, "qv", 0, "qx", 0, C)
     emit("s", lambda: g.sync.dma_start(T.oc[:, :], by(W("qx"))), [], [W("qx")], dma="doc")
-    ts(W("qz"), ind(W("q4"), W("lrq", 0, 7)), UNIT, A.mult)
+    ts(W("qz"), ind(W("q4", 0, K), lrq), 1.0, A.mult)
     act(W("yo"), bk(0, 0, C), AF.Copy)
     ts(W("lqf"), W("qz"), -1.0, A.mult, float(C - 1), A.add)
     emit("a", lambda: g.scalar.dma_start(T.y[:, :], T.yo[:, :]), [], [W("yo")], dma="dy")

@@ -2,28 +2,22 @@ from concourse.mybir import dt, AluOpType, ActivationFunctionType
 
 C, K, ROUNDS = 288, 112, 3
 NJ = C // 16
-TAG = 2048.0
+UNIT = 8192.0
 MID = 144.0
 BIG = 1024.0
 LIFT = 512.0
 TINY = 1e-36
 MW = C + 16
+PW = 40
 CODE, F32, BF, I32, U16, U8 = "float8_e4m3fn_x4", "float32", "bfloat16", "int32", "uint16", "uint8"
-ND = 6
-NR = NJ - 1 - ND
-CHUNKS = [[("lt", "eq"), (("r", 11), ("r", 10))], [(("d", 4), ("d", 3)), (("r", 9), ("r", 8))], [(("d", 6), ("d", 5)), (("r", 7), ("r", 6))],
-          [(("d", 2), ("d", 1)), (("r", 5), ("r", 4))], [(("r", 3), ("r", 2)), (("r", 1), None)]]
-
-
-def _cols(plane):
-    return 0 if plane is None else C if plane in ("lt", "eq") else C - 16 * plane[1] if plane[0] == "d" else 16 * plane[1]
-
-
-PAIR, GW = {}, 0
-for _ch in CHUNKS:
-    for _p in _ch:
-        PAIR[_p] = (GW, 128 if _p[0][0] == "r" else 144)
-        GW += PAIR[_p][1]
+ORD, NA = (0, 1, 2), 3
+CHUNKS = [[9, 8, 7], [6, 5], [4, 3], [2, 1], ["lt", "eq"]]
+PLANE = {"lt": (0, 0), "eq": (0, 1), 9: (216, 0)}
+GW = 360
+for _k in (8, 6, 4, 2):
+    GW += 8 * _k if _k < 8 else 0
+    PLANE[_k], PLANE[_k - 1] = (GW, 0), (GW, 1)
+    GW += 144
 CE, CC, CD, CI, CS, CZ = 0, 512, 640, 768, 1024, 1152
 
 SCRATCH = {"ps": ("psum", [128, 4096], F32)}
@@ -34,20 +28,21 @@ def _sb(dtype, **names):
         SCRATCH[n] = ("sbuf", [128, w], dtype)
 
 
-_sb(BF, x0=4 * C, X=1600, XS=4 * C, ub=512, vb=512, neg=528, OH=528, cb=2560, G=4 * GW, m16=C, e64=128,
+_sb(BF, x0=4 * C, X=1600, XS=4 * C, ub=512, vb=512, neg=528, OH=528, cb=2568, G=4 * GW, m16=C, e64=128,
     A5=448, Et=512, Vt=512, DE=448, CV=448, MT=4 * MW, wrb=C, wrS=MW, am=MW, BR=320, TR=320)
 _sb(F32, r4=K, r8=144, r16=C, pflt=24, ic=C, cd=C, dm=28, c16=28, yl=NJ, lf=72, ya=16, yb=16, yc=16,
-    z=C, zs=C, zz=144, B16=C, B8=144, M4=K, M8=144, Mb=NJ, Mc=NJ, OE=C, sg=C, Vr=C, Rs=NJ, PL=C, ab=C, rl=8 * NR * (NR + 1), TG=C,
-    Q1=C, Q2=C, Q3=C, Q4=C, P1=K, P2=K, P4=K, w1=K, wA=K, wE=K, FQ=448, eqn=28, sel=28, lqf=K, q0=K, q1=K, q4=K + 1, yo=C)
+    z=C, zs=C, zz=144, B16=C, B8=144, M4=K, M5=K, M8=144, OE=C, sg=C, Vr=C, Rs=NJ, PL=C, ab=C, rl=2 * C, TG=C, c9=NJ,
+    Q1=C, Q2=C, Q3=C, Q4=C, P1=K, P2=K, P4=K, w1=K, wA=K, wE=K, FQ=448, eqn=28, sel=28, lqf=K, q0=K, q1=K, qa=2 * K, qb=2 * K,
+    q4=2 * K + 2, yo=C)
 _sb(I32, rvt=NJ, pint=8, yi=16, qi=28, qj=28, qz=K)
-_sb(U16, rvl=NJ, lu=76, lA=28, rkl=NJ, LL=80, Pp=K, lE=28, lQ=28, lX=28, pls=40 * ROUNDS, pll=40 * ROUNDS)
+_sb(U16, rvl=NJ, lu=76, lA=28, rkl=NJ, LL=80, Pp=K, lE=28, lQ=28, lX=28, pls=PW * ROUNDS, pll=PW * ROUNDS)
 for _n, _w in [("qx", C), ("qu", 128), ("qv", 128), ("uo", 128), ("um", 128), ("wq", 512), ("cq", CZ), ("gq", GW), ("vq", 128),
-               ("mq", MW), ("zq", 128), ("eq", 128 * ROUNDS), ("le", 128 * ROUNDS)]:
+               ("mq", MW), ("eq", 128 * ROUNDS), ("le", 128 * ROUNDS)]:
     SCRATCH[_n] = ("sbuf", [128, _w], CODE)
     SCRATCH[_n + "s"] = ("sbuf", [128, _w], U8)
 
 QS = {"v": "qsv", "a": "qsa", "t": "qst", "g": "qsg"}
-DS = ["dx", "du", "dv", "drv", "dwc", "dws", "dgq", "dle", "dwr", "dP", "dlq", "doc", "dy"]
+DS = ["dx", "du", "dv", "drv", "dwc", "dws", "dG", "dpad", "dwr", "dP", "dlq", "doc", "dy"]
 SEMAPHORES = list(QS.values()) + DS + ["rl"] + ["ap%d" % _t for _t in range(ROUNDS)] + ["ae%d" % _t for _t in range(ROUNDS)]
 
 
@@ -189,7 +184,10 @@ def rank_program(g, core, T, topo):
 
     def act(out, a, fn=AF.Identity, scale=1.0, bias=0.0, accum=None):
         kw, ins, outs = {}, rg(a), rg(out)
-        if scale != 1.0:
+        if isinstance(scale, tuple):
+            kw["scale"] = ap(scale)
+            ins.append(scale)
+        elif scale != 1.0:
             kw["scale"] = scale
         if isinstance(bias, tuple):
             kw["bias"] = ap(bias)
@@ -238,26 +236,17 @@ def rank_program(g, core, T, topo):
     sO, sM, lOE, lrv, lrq, lsel, lp7 = (W("lu", a, b) for a, b in ((0, 8), (8, 16), (16, 34), (34, 52), (52, 59), (60, 65), (68, 75)))
 
     def columns(row, tmp, i1, i2, out):
-        scan(tmp, row, W("M4"), LIFT, A.min, A.add)
-        ts(i1, (tmp[0], 0, 128, 3, K, 4), 4 * TAG, A.mult, LB, A.add)
-        ts(i2, i1, int(4 * TAG) - 1, A.bitwise_and)
+        scan(tmp, row, W("M4"), LIFT * UNIT, A.min, A.add)
+        ts(i1, (tmp[0], 0, 128, 3, K, 4), LB, A.add)
+        ts(i2, i1, int(UNIT) - 1, A.bitwise_and)
         cp(out, i2)
 
-    def lane(plane):
-        for p, (o, n) in PAIR.items():
-            if plane in p:
-                return W("G", 4 * o + p.index(plane), 4 * o + p.index(plane) + 2 * _cols(plane) - 1, 2)
+    def lane(k, c0, c1):
+        o = 4 * PLANE[k][0] + PLANE[k][1]
+        return W("G", o + 2 * c0, o + 2 * c1 - 1, 2)
 
-    def gap(p):
-        o, n = PAIR[p]
-        return W("G", 4 * o + 2 * min(_cols(p[0]), _cols(p[1])), 4 * (o + words(p)))
-
-    def words(p):
-        return max(_cols(p[0]), _cols(p[1])) // 2 if p in [ch[-1] for ch in CHUNKS] else PAIR[p][1]
-
-    def zeros(n, c0, c1):
-        dma("s", "d" + n, W(n, c0, c1), W("zq", 0, c1 - c0), o8=True, a8=True)
-        dma("s", "d" + n, W(n + "s", c0, c1), W("zqs", 0, c1 - c0))
+    def zero(sem, o):
+        dma("s", sem, o, W("MT", 0, o[4] - o[3]))
 
     dma("a", "drv", W("rvt"), W("rv"))
     dma("s", "du", W("ub"), W("u"))
@@ -266,75 +255,79 @@ def rank_program(g, core, T, topo):
     iota(PI, [[0, 1]], 0, 1)
     iota(W("c16"), [[16, 28]])
     iota(W("lf", 0, 16), [[8, 2], [16, 8]])
-    iota(W("r16"), [[0, NJ], [1, 16]])
-    iota(W("r8"), [[0, NJ], [2, 8]], 1)
     fill(W("neg"), -1.0)
+    fill(W("MT"), 0.0)
+    for k in (6, 4, 2):
+        zero("dG", W("G", 4 * PLANE[k][0] - 32 * k, 4 * PLANE[k][0]))
     for i, (sh, mask) in enumerate(((0, 15), (0, 14), (0, 12), (0, 3), (0, 1), (4, 1))):
         ts(W("pint", i + 1, i + 2), PI, sh, A.logical_shift_right, mask, A.bitwise_and)
-    cp(W("pflt", 0, 6), W("pint", 1, 7))
-    fill(W("cb"), 0.0)
     act(W("lf", 16, 34), C16, bias=15.0)
-    act(W("wrS"), W("neg", 0, MW), AF.Copy, scale=MID)
-    act(W("yl"), C16, bias=LF)
-    act(LM, L2, AF.Relu, scale=-10 * BIG, bias=10 * BIG)
-    act(K2, L2, scale=-BIG / 2, bias=7 * BIG + C - 1)
-    act(W("lf", 34, 52), W("yl"), scale=-1.0, bias=C - 1.0)
-    act(W("lf", 52, 59), W("yl", 0, 7), scale=-1.0, bias=K - 1.0)
-    act(W("Mb"), C16, scale=-1.0, bias=LM)
-    act(LR, LM, scale=-1.0, bias=K2)
-    quant("zq", 0, 128, W("cb", 2048, 2560))
-    cp(W("lu", 0, 59), W("lf", 0, 59))
-    cp(W("rvl"), W("rvt"))
-    pairs = list(PAIR)
-    for p in pairs[1::2]:
-        o, n = PAIR[p]
-        zeros("gq", (o + words(p)) // 16 * 16, o + n)
-    ts(W("m16"), W("r16"), LF, A.is_equal)
-    act(W("B16"), W("r16"), AF.Sign)
-    act(W("zz"), W("r8"), AF.Sign, scale=-1.0, bias=L2)
-    act(W("B8"), W("r8"), AF.Sign, bias=-1.0)
-    act(W("M8"), W("zz"), scale=5 * BIG, bias=4 * BIG)
+    for e in (0, 512):
+        act(W("cb", e, e + 512), W("neg", 0, 512), AF.Copy, scale=0.0)
+    cp(W("pflt", 0, 6), W("pint", 1, 7))
+    cp(W("lu", 0, 34), W("lf", 0, 34))
     asel(W("e64", 0, 64), W("neg", 0, 64), [[-16, 8], [0, 8]], A.is_ge, 0, 1)
     asel(W("e64", 64, 128), W("e64", 0, 64), [[16, 8], [0, 8]], A.is_ge, 15, -1)
-    iota(W("ic"), [[1, C]])
-    asel(W("cb", 513, 1024, 8), W("e64", 64, 128), [[16, 8], [2, 8]], A.is_gt, 0, -1)
-    asel(W("cb", 519, 1024, 8), W("e64", 64, 128), [[16, 8], [2, 8]], A.is_ge, 0, -1)
-    for e in (0, 1, 6, 7, 512, 518):
-        act(W("cb", e, e // 512 * 512 + 512, 8), W("e64", 64, 128), AF.Copy)
+    for e in (0, 1, 6):
+        act(W("cb", e, 512, 8), W("e64", 64, 128), AF.Copy)
     quant("qu", 0, 128, W("ub"))
     pick("uo", sO)
-    act(W("yo"), W("ic"), AF.Relu, bias=-1.0)
-    for p in pairs[1::2]:
-        o = gap(p)
-        iota(o, [[0, o[4] - o[3]]])
-    for e in (0, 2, 513, 515):
-        o = W("cb", 1024 + e, 1024 + e // 512 * 512 + 512, 4)
-        asel(o, o, [[1, 128]], A.not_equal, 0, -1, 1.0)
-    iota(W("Rs", 0, ND + 1), [[0, ND + 1]])
-    iota(W("r4"), [[0, 28], [4, 4]], 2)
+    pick("um", sM)
+    iota(W("r16"), [[0, NJ], [1, 16]])
+    asel(W("cb", 1024, 1544), W("neg", 0, 520), [[-1, 520]], A.is_equal, 1, 4)
+    asel(W("cb", 1027, 1539, 4), W("cb", 1027, 1539, 4), [[1, 128]], A.not_equal, 0, -1, -1.0)
+    asel(W("cb", 513, 1024, 8), W("e64", 64, 128), [[16, 8], [2, 8]], A.is_gt, 0, -1)
+    asel(W("cb", 519, 1024, 8), W("e64", 64, 128), [[16, 8], [2, 8]], A.is_ge, 0, -1)
+    iota(W("r8"), [[0, NJ], [2, 8]], 1)
+    iota(W("ic"), [[int(UNIT), C]])
+    iota(W("Rs", 8, NJ), [[0, NJ - 8]])
+    iota(W("c9"), [[16, 2], [0, 9]], -16)
+    iota(W("cd"), [[4, C]], 4)
     iota(W("yc"), [[178, 2], [0, 8]], -289)
-    asel(W("OH"), W("neg"), [[-1, 528]], A.is_equal, 3, 4)
+    zero("dpad", W("cb", 2048, 2560))
+    zero("dpad", W("BR", MW, 320))
+    for n in ("Et", "Vt"):
+        zero("dpad", W(n, 448, 512))
     for k in range(2):
         for base in (-64, 64):
             o = W("cb", 2048 + k, 2560, 4)
             asel(o, o, [[32, 4], [1000, 4], [16, 8]], A.not_equal, base - 1000 * k, -1, LIFT)
-    iota(W("BR", MW, 320), [[0, 320 - MW]])
-    for n in ("Et", "Vt"):
-        iota(W(n, 448, 512), [[0, 64]])
-    iota(W("q4", K, K + 1), [[0, 1]], int(LIFT))
+    iota(W("r4"), [[0, 28], [4, 4]], 2)
+    asel(W("OH"), W("neg"), [[-1, 528]], A.is_equal, 3, 4)
+    iota(W("q4", 2 * K + 1, 2 * K + 2), [[0, 1]], int(LIFT * UNIT))
+    iota(W("qb", 1, 2 * K, 2), [[0, K]])
 
     def consts_first():
-        pick("um", sM)
-        act(W("Q4"), ind(W("yo"), W("rvl")), scale=-1.0, bias=C - 1 - MID)
-        for p in pairs[2::2]:
-            fill(gap(p), 0.0)
+        ts(W("m16"), W("r16"), LF, A.is_equal)
+        act(W("B16"), W("r16"), AF.Sign)
+        act(W("yl"), C16, bias=LF)
+        act(W("lf", 34, 52), W("yl"), scale=-1.0, bias=C - 1.0)
         dma("s", "dwc", W("wq"), W("wc"), o8=True)
         dma("s", "dws", W("wqs"), W("ws"))
         dma("s", "dv", W("vb"), W("v"))
 
+    def consts_count():
+        fill(W("G", 4 * 144, 4 * PLANE[8][0]), 0.0)
+        for e in (7, 512, 518):
+            cp(W("cb", e, e // 512 * 512 + 512, 8), W("e64", 64, 128))
+        quant("cq", CI, CI + 128, W("cb", 1025, 1537))
+        quant("cq", CI + 128, CS, W("cb", 1024, 1536))
+
+    def consts_rank():
+        cp(W("rvl"), W("rvt"))
+        cp(lrv, W("lf", 34, 52))
+        fill(W("wrS"), -MID)
+        act(W("B8"), W("r8"), scale=0.0, bias=-100 * BIG)
+        ts(LM, L2, 0.0, A.is_equal, 10 * BIG, A.mult)
+        ts(K2, L2, -BIG / 2, A.mult, 7 * BIG + C // 2 - 1, A.add)
+        act(W("zz"), W("r8"), AF.Sign, scale=-1.0, bias=L2)
+        act(W("yo"), W("ic"), AF.Relu, scale=1.0 / UNIT, bias=-1.0)
+        act(W("M8"), W("zz"), scale=5 * BIG, bias=4 * BIG)
+        ts(LR, K2, LM, A.subtract)
+
     def consts_rv():
+        act(W("Q4"), ind(W("yo"), W("rvl")), scale=-1.0, bias=C - 1 - MID)
         act(W("wrb"), ind(W("Q4"), lrv), AF.Copy)
-        act(W("cd"), W("ic"), scale=1.0 / TAG, bias=1.0 / TAG)
         for k in range(2):
             for a in range(4):
                 g0 = (2 * a - 4) % 8
@@ -348,29 +341,34 @@ def rank_program(g, core, T, topo):
         act(K3, EF, scale=-48.0, bias=24.0)
         act(K4, EF, scale=9.0, bias=3.0)
         act(W("ya", 0, 8), W("yl", 0, 8), scale=1.0 / 18, bias=-8.5 / 18)
+        act(KP, SF, scale=K3, bias=K4)
         act(W("ya", 8, 16), W("yl", 0, 8), scale=1.0 / 7, bias=-3.0 / 7)
-        act(W("yb", 8, 16), W("yl", 0, 8), scale=16.0)
-        ts(KP, K3, SF, A.mult, K4, A.add)
-        cp(W("yi"), W("ya"))
-        act(W("w1"), W("r4"), AF.Sign, scale=-1.0, bias=L4)
-        act(K5, L4, AF.Relu, scale=-LIFT, bias=LIFT)
-        act(LB, LQ, bias=3 * 4 * TAG - 4)
         act(W("yb", 0, 8), W("yl", 0, 8), scale=16.0, bias=KP)
-        tt(W("ya"), W("yi"), W("yc"), A.mult)
-        act(W("M4"), W("w1"), scale=(LIFT + 1) / 2, bias=(LIFT - 1) / 2)
-        act(K6, L4, scale=-TAG, bias=LB)
-        tt(W("yb"), W("yb"), W("ya"), A.add)
-        act(W("M4", 3, K, 4), W("r4", 0, 28), scale=0.0, bias=K5)
-        act(LA, K5, scale=-4 * TAG, bias=K6)
-        cp(W("lu", 60, 76), W("yb"))
+        act(W("yb", 8, 16), W("yl", 0, 8), scale=16.0)
 
-    ne, np_ = len(topo.engines(core, nxt)[:8]), len(topo.engines(prv, core)[:8])
-    emask = sum(1 << e for e in topo.engines(core, nxt)[:8])
+    def consts_lists():
+        act(W("w1"), W("r4"), AF.Sign, scale=-1.0, bias=L4)
+        act(K5, L4, AF.Relu, scale=-LIFT * UNIT, bias=LIFT * UNIT)
+        act(LB, LQ, bias=3 * UNIT - 4)
+        act(W("M4"), W("w1"), scale=(LIFT + 1) / 2 * UNIT, bias=(LIFT - 1) / 2 * UNIT)
+        act(K6, L4, scale=-UNIT / 4, bias=LB)
+        act(W("M4", 3, K, 4), W("r4", 0, 28), scale=0.0, bias=K5)
+        act(LA, K5, scale=-1.0, bias=K6)
+
+    def consts_late():
+        act(W("dm"), W("c16"), scale=-1.0, bias=K5)
+        act(W("lf", 52, 59), W("yl", 0, 7), scale=-1.0, bias=K - 1.0)
+        cp(W("M5"), W("M4"))
+        ts(W("M5", 3, K, 4), W("dm"), LF, A.subtract, -4.0 * C, A.add)
+        cp(lrq, W("lf", 52, 59))
+        quant("qv", 0, 128, W("vb"))
+
+    ne, np_ = len(topo.engines(core, nxt)), len(topo.engines(prv, core))
     rid, pid = topo.addr(nxt, core)
     rlc = [0]
 
-    def send(out_ap, src, in_ap, sem):
-        emit("g", lambda: g.remote_dma(out_ap, in_ap, T.sem[sem], T.sem.rl, pid, rid, emask), [], [src], remote=True)
+    def send(out, src, view, sem):
+        emit("g", lambda: g.remote_dma(view(out), view(src), T.sem[sem], T.sem.rl, pid, rid, topo.mask(core, nxt)), [], [src], remote=True)
         rlc[0] += ne
 
     for t in range(ROUNDS):
@@ -384,6 +382,10 @@ def rank_program(g, core, T, topo):
         def unpack():
             for b in range(4):
                 mm(2 + b, "cq", 128 * b, "qx", 0, C)
+
+        def state():
+            for b in range(4):
+                act(W("X", b, 4 * C, 4), bk(2 + b, 0, C), AF.Copy, scale=-1.0)
         if t:
             unpack()
         So = bk(0, 0, C)
@@ -391,58 +393,67 @@ def rank_program(g, core, T, topo):
         act(W("sg"), bk(1, 0, C), AF.Sign, bias=-TINY)
         scan(W("zs"), W("B16"), W("z"), 0.0, A.mult, A.add)
         if t == 0:
-            consts_rv()
-        act(W("OE"), ind(W("zs"), lOE), AF.Copy)
-        if t == 0:
-            quant("cq", CC, CI, W("cb", 0, 1024))
-        scan(W("Vr"), W("cd"), W("sg"), 0.0, A.max, A.mult)
+            act(W("OE"), ind(W("zs"), lOE), AF.Copy)
+            consts_count()
+        else:
+            cp(W("OE", 64, C), ind(W("zs"), W("lu", 20, 34)))
 
-        def relu(i):
-            o = 8 * i * (i - 1)
-            act(W("rl", o, o + 16 * i), bk(7, 0, 16 * i), AF.Relu, scale=-1.0, bias=W("zs", 16 * (ND + i) + 15, 16 * (ND + i) + 16))
+        def far(k):
+            o = 8 * k * (k - 1)
+            act(W("rl", o, o + 16 * k), bk(7, C - 16 * k, C), AF.Sign, scale=-1.0, bias=W("zs", 16 * (8 - k) + 15, 16 * (8 - k) + 16))
 
-        def sign(i):
-            o = 8 * i * (i - 1)
-            act(lane(("r", i)), W("rl", o, o + 16 * i), AF.Sign, accum=W("Rs", ND + i, ND + i + 1))
+        def won(k):
+            o = 8 * k * (k - 1)
+            act(lane(k, C - 16 * k, C), W("rl", o, o + 16 * k), AF.Sign, bias=1.0, accum=W("Rs", 8 - k, 9 - k))
 
-        def chunk(k):
-            ch = CHUNKS[k]
-            o0, end = PAIR[ch[0]][0], PAIR[ch[-1]][0] + words(ch[-1])
+        def chunk(ch):
+            o0, end = PLANE[ch[0]][0], PLANE[ch[-1]][0] + 144
+            if t == 0 and ch[0] != "lt":
+                o0 -= 8 * ch[0]
             quant("gq", o0, end, W("G", 4 * o0, 4 * end))
-            for p in ch:
-                o, n = PAIR[p]
-                if p[0][0] == "d":
-                    for e in range(2):
-                        mm(1, "cq", CI + 128 * e, "gq", o - 8 * p[e][1], n, start=(k == 1 and e == 0), stop=(p[e][1] == 1))
-                mm(6, "cq", CD if p[0] == "lt" else CC, "gq", o, n, start=(o == 0), stop=(p == pairs[-1]))
-        relu(NR)
-        for i in range(NR, 0, -1):
-            if i > 1:
-                relu(i - 1)
-            sign(i)
-        tt(lane("lt"), So, W("OE"), A.is_lt)
-        tt(lane("eq"), So, W("OE"), A.is_equal)
-        for k in range(1, 4):
-            for d in CHUNKS[k][0]:
-                tt(lane(d), bk(0, 0, _cols(d)), W("OE", 16 * d[1], C), A.is_lt)
-            if t == 0 and k == 2:
-                quant("cq", CI, CS, W("cb", 1024, 2048))
-            chunk(k - 1)
-        chunk(3)
+            if ch[0] != "lt":
+                for k in ch:
+                    mm(1, "cq", CI + 128 * PLANE[k][1], "gq", PLANE[k][0] - 8 * k, 144, start=(k == 9), stop=(k == 1))
+            for k in ch:
+                if PLANE[k][1] == 0:
+                    mm(6, "cq", CD if k == "lt" else CC, "gq", PLANE[k][0], 144, start=(k == 9), stop=(k == "lt"))
+        far(8)
+        for k in range(8, 0, -1):
+            if k > 1:
+                far(k - 1)
+            won(k)
+            if t and k == 7:
+                act(W("OE", 0, 64), ind(W("zs"), W("lu", 16, 20)), AF.Copy)
+        for n, ch in enumerate(CHUNKS):
+            for k in ch:
+                if k in ("lt", "eq"):
+                    tt(lane(k, 0, C), So, W("OE"), A.is_lt if k == "lt" else A.is_equal)
+                else:
+                    tt(lane(k, 0, C - 16 * k), bk(0, 0, C - 16 * k), W("OE", 16 * k, C), A.is_lt)
+            if t == 0 and n == 0:
+                quant("cq", CC, CI, W("cb", 0, 1024))
+            if t == 0 and n == 2:
+                consts_rank()
+                consts_rv()
+            if n:
+                chunk(CHUNKS[n - 1])
+        chunk(CHUNKS[-1])
         if t == 0:
-            fill(W("MT"), 0.0)
-        chunk(4)
-        scan(W("zz"), W("B8"), bk(1, 0, 144), 0.0, A.mult, A.add)
-        if t == 0:
-            consts_bounds()
-        tt(W("Mc"), W("zz", 7, 144, 8), W("Mb"), A.add)
-        for b in range(4 if t else 0):
-            act(W("X", b, 4 * C, 4), bk(2 + b, 0, C), AF.Copy, scale=-1.0)
-        tt(W("M8", 7, 144, 8), W("Rs"), W("Mc"), A.add)
+            ts(W("B8", 0, 144, 8), W("c9"), LM, A.subtract)
+        scan(W("Vr"), W("cd"), W("sg"), 0.0, A.max, A.mult)
+        scan(W("zz"), W("B8"), bk(1, 0, 144), -100 * BIG, A.max, A.add)
+        if t:
+            state()
+        tt(W("M8", 7, 144, 8), W("Rs"), W("zz", 7, 144, 8), A.subtract)
         scan(W("zz"), bk(6, 0, 144), W("M8"), 4 * BIG, A.min, A.add)
         ts(W("rkl"), W("zz", 7, 144, 8), LR, A.add)
         if t == 0:
             quant("cq", CS, CZ, W("cb", 2048, 2560))
+            consts_bounds()
+            consts_lists()
+            for b in range(4):
+                quant("cq", 128 * b, 128 * b + 128, W("OH", 3 - b, 515 - b))
+            unpack()
         scatter(W("PL"), W("rkl"), W("Vr"))
         ts(W("MT", 4, 4 * C + 4, 4), W("PL"), 0.0, A.is_gt, -0.5, A.add)
         act(W("MT", 69, 4 * MW, 4), W("PL", 0, C - 1), AF.Sign)
@@ -450,18 +461,24 @@ def rank_program(g, core, T, topo):
         quant("mq", 0, MW, W("MT"))
         mm(1, "cq", CS, "mq", 0, MW)
         if t == 0:
-            for b in range(4):
-                quant("cq", 128 * b, 128 * b + 128, W("OH", 3 - b, 515 - b))
-            unpack()
-            for b in range(4):
-                act(W("X", b, 4 * C, 4), bk(2 + b, 0, C), AF.Copy, scale=-1.0)
-        scan(W("TG"), W("ic"), W("ab"), 0.0, A.max, A.add)
-        tt(W("am"), bk(1, 0, MW), W("wrS"), A.min)
-        scan(W("wA"), W("ab", 1, 2 * K, 2), W("M4"), LIFT, A.min, A.add)
-        scan(W("BR", 0, MW), W("am"), W("am"), -MID, A.max, A.max)
-        ts(W("lA"), W("wA", 3, K, 4), 4 * TAG, A.mult, LA, A.add)
+            state()
+            cp(W("yi"), W("ya"))
+            fill(W("pls"), 0)
+            tt(W("ya"), W("yi"), W("yc"), A.mult)
+
+        def fixed():
+            scan(W("wA"), W("ab", 1, 2 * K, 2), W("M4"), LIFT * UNIT, A.min, A.add)
+            ts(W("lA"), W("wA", 3, K, 4), LA, A.add)
         if t:
+            fixed()
             act(W("A5"), ind(W("X", 0, 4 * C), W("lA")), AF.Copy)
+        tt(W("am"), bk(1, 0, MW), W("wrS"), A.min)
+        if t == 0:
+            tt(W("yb"), W("yb"), W("ya"), A.add)
+        scan(W("TG"), W("ic"), W("ab"), 0.0, A.max, A.add)
+        scan(W("BR", 0, MW), W("am"), W("am"), -MID, A.max, A.max)
+        if t == 0:
+            cp(W("lu", 60, 76), W("yb"))
         odd = {n: (n, 0, 128, 1, 2 * K, 2) for n in ("TG", "Q1", "Q2", "Q3", "Q4")}
         turn(W("TR"), W("BR"))
         ts(W("LL"), ind(W("TR"), lsel), MID, A.add)
@@ -469,75 +486,80 @@ def rank_program(g, core, T, topo):
             H = 10 if d == 1 else 6
             src, o = W("TG") if d == 1 else W("Q%d" % (d - 1)), NJ * (d - 1)
             cp(W("Q%d" % d, 0, 16 * H), ind(src, W("LL", o, o + H)))
-            act(W("Q%d" % d, 16 * H, C), ind(src, W("LL", o + H, o + NJ)), AF.Copy)
+            if H < NJ:
+                act(W("Q%d" % d, 16 * H, C), ind(src, W("LL", o + H, o + NJ)), AF.Copy)
             if d == 2:
                 scan(W("P1"), odd["TG"], odd["Q1"], 0.0, A.max, A.max)
             if d == 3:
                 scan(W("P2"), W("P1"), odd["Q2"], 0.0, A.max, A.max)
             if d == 4:
                 scan(W("P1"), W("P2"), odd["Q3"], 0.0, A.max, A.max)
+            if t == 0 and d == 1:
+                fixed()
         scan(W("P4"), W("P1"), odd["Q4"], 0.0, A.max, A.max)
-        if t == 0:
-            act(W("A5"), ind(W("X", 0, 4 * C), W("lA")), AF.Copy)
-            fill(W("pls"), 0)
-            for u in range(ROUNDS):
-                zeros("le", 128 * u + K, 128 * u + 128)
-        ts(W("Pp"), ind(W("P4"), lp7), 1.0, A.mult)
-        o = 40 * t
+        ts(W("Pp"), ind(W("P4"), lp7), 1.0 / UNIT, A.mult)
+        o = PW * t
         for d in range(5):
             for g0, g1, to in ((0, 8 - d, 16 * d), (8 - d, 8, 0)):
                 if g0 < g1:
-                    rows_to("sa"[g0 > 0], "dP", W("pls", o + 8 * d, o + 8 * d + 7, p0=to, p1=to + 16 * (g1 - g0)), "Pp", g0, g1, K)
+                    rows_to("sa"[d > 2], "dP", W("pls", o + 8 * d, o + 8 * d + 7, p0=to, p1=to + 16 * (g1 - g0)), "Pp", g0, g1, K)
+        if t == 0:
+            act(W("A5"), ind(W("X", 0, 4 * C), W("lA")), AF.Copy)
         columns(W("P4"), W("wE"), W("qi"), W("qj"), W("lE"))
         tt(W("Et", 0, 448), ind(W("X", 0, 4 * C), W("lE")), W("A5"), A.add)
         quant("eq", 128 * t, 128 * t + 128, W("Et"))
-        pl, plo = W("pls", o, o + 40), W("pll", o, o + 40)
-        e, eo = W("eq", 128 * t, 128 * t + K), W("le", 128 * t, 128 * t + K)
-        send(ap(plo), pl, ap(pl), "ap%d" % t)
-        send(by(eo), e, by(e), "ae%d" % t)
-        es, eso = W("eqs", 128 * t, 128 * t + K), W("les", 128 * t, 128 * t + K)
-        send(ap(eso), es, ap(es), "ae%d" % t)
+        pl, plo = W("pls", o, o + PW), W("pll", o, o + PW)
+        e, eo = W("eq", 128 * t, 128 * t + 128), W("le", 128 * t, 128 * t + 128)
+        es, eso = W("eqs", 128 * t, 128 * t + 128), W("les", 128 * t, 128 * t + 128)
+        for i in ORD:
+            send(*[(plo, pl, ap, "ap%d" % t), (eo, e, by, "ae%d" % t), (eso, es, ap, "ae%d" % t)][i])
         ts(W("XS"), W("X", 0, 4 * C), 2.0 ** -5, A.mult)
         if t == 0:
-            act(W("dm"), W("c16"), bias=LF)
-            act(W("dm"), W("dm"), bias=4.0 * C)
-            quant("qv", 0, 128, W("vb"))
+            consts_late()
         arrive([plo], "ap%d" % t, np_)
         arrive([eo, eso], "ae%d" % t, 2 * np_)
+        act(W("qa", 1, 2 * K, 2), ind(W("Q3"), W("pll", o + 24, o + 31)), AF.Copy)
+        act(W("qb", 0, 2 * K, 2), ind(W("Q4"), W("pll", o + 32, o + 39)), AF.Copy)
         for b in range(4):
             mm(2 + b, "cq", 128 * b, "le", 128 * t, 128)
-        for b in range(4):
+        for b in range(NA):
             act(W("DE", b, 448, 4), bk(2 + b, 0, K), AF.Copy, scale=-2.0 ** -6)
-        q4 = W("q4", 0, K)
         cp(W("q0"), ind(W("Q1"), W("pll", o + 8, o + 15)))
         tt(W("q1"), ind(W("TG"), W("pll", o, o + 7)), W("q0"), A.max)
-        tt(W("q0"), ind(W("Q2"), W("pll", o + 16, o + 23)), W("q1"), A.max)
-        tt(W("q1"), ind(W("Q3"), W("pll", o + 24, o + 31)), W("q0"), A.max)
-        tt(q4, ind(W("Q4"), W("pll", o + 32, o + 39)), W("q1"), A.max)
-        columns(q4, W("wE"), W("qi"), W("qj"), W("lQ"))
-        tt(W("Vt", 0, 448), ind(W("XS"), W("lQ")), W("DE"), A.add)
+        tt(W("qa", 0, 2 * K, 2), ind(W("Q2"), W("pll", o + 16, o + 23)), W("q1"), A.max)
+        scan(W("q4", 0, 2 * K), W("qa"), W("qb"), 0.0, A.max, A.max)
+        columns(W("q4", 1, 2 * K, 2), W("wE"), W("qi"), W("qj"), W("lQ"))
         act(W("FQ"), ind(W("X", 0, 4 * C), W("lQ")), AF.Copy)
+        for b in range(NA, 4):
+            ts(W("DE", b, 448, 4), bk(2 + b, 0, K), -2.0 ** -6, A.mult)
+        tt(W("Vt", 0, 448), ind(W("XS"), W("lQ")), W("DE"), A.add)
+        if t == ROUNDS - 1:
+            act(W("q0"), W("q4", 1, 2 * K, 2), AF.Copy)
+            act(W("q1"), ind(W("q0"), lrq), scale=-1.0 / UNIT, bias=C - 1.0)
         quant("vq", 0, 128, W("Vt"))
         hb = (0, 1, 6, 7)
         for b in range(4):
             mm(hb[b], "wq", 128 * b, "vq", 0, 128)
-        scan(W("w1"), W("q4", 1, K + 1), W("M4"), LIFT, A.min, A.add)
+        scan(W("w1"), W("q4", 3, 2 * K + 2, 2), W("M5"), LIFT * UNIT, A.min, A.add)
         tt(W("CV", 0, 448, 4), bk(hb[0], 0, K), W("FQ", 0, 448, 4), A.add)
-        tt(W("eqn"), W("wE", 3, K, 4), W("w1", 3, K, 4), A.is_equal)
+        tt(W("eqn"), W("wE", 3, K, 4), W("w1", 3, K, 4), A.subtract)
         tt(W("CV", 1, 448, 4), bk(hb[1], 0, K), W("FQ", 1, 448, 4), A.add)
-        tt(W("eqn"), W("eqn"), W("dm"), A.mult)
-        tt(W("CV", 2, 448, 4), bk(hb[2], 0, K), W("FQ", 2, 448, 4), A.add)
         tt(W("sel"), W("qj"), W("eqn"), A.max)
-        tt(W("CV", 3, 448, 4), bk(hb[3], 0, K), W("FQ", 3, 448, 4), A.add)
+        tt(W("CV", 2, 448, 4), bk(hb[2], 0, K), W("FQ", 2, 448, 4), A.add)
         cp(W("lX"), W("sel"))
+        tt(W("CV", 3, 448, 4), bk(hb[3], 0, K), W("FQ", 3, 448, 4), A.add)
         scatter(W("X"), W("lX"), W("CV"))
     quant("qx", 0, C, W("X", 0, 4 * C))
-    mm(0, "qv", 0, "qx", 0, C)
-    emit("s", lambda: g.sync.dma_start(T.oc[:, :], by(W("qx"))), [], [W("qx")], dma="doc")
-    ts(W("qz"), ind(W("q4", 0, K), lrq), 1.0, A.mult)
-    act(W("yo"), bk(0, 0, C), AF.Copy)
-    ts(W("lqf"), W("qz"), -1.0, A.mult, float(C - 1), A.add)
-    emit("a", lambda: g.scalar.dma_start(T.y[:, :], T.yo[:, :]), [], [W("yo")], dma="dy")
+    HY = 160
+    mm(0, "qv", 0, "qx", 0, HY)
+    mm(1, "qv", 0, "qx", HY, C - HY)
+    emit("a", lambda: g.scalar.dma_start(T.oc[:, :], by(W("qx"))), [], [W("qx")], dma="doc")
+    cp(W("qz"), W("q1"))
+    cp(W("yo", 0, HY), bk(0, 0, HY))
+    act(W("yo", HY, C), bk(1, 0, C - HY), AF.Copy)
+    emit("s", lambda: g.sync.dma_start(T.y[:, 0:HY], T.yo[:, 0:HY]), [], [W("yo", 0, HY)], dma="dy")
+    emit("a", lambda: g.scalar.dma_start(T.y[:, HY:C], T.yo[:, HY:C]), [], [W("yo", HY, C)], dma="dy")
+    cp(W("lqf"), W("qz"))
     for k in range(4):
         emit("s", lambda: g.sync.dma_start(T.osc[4 * k:4 * k + 4, :], T.qxs[32 * k:32 * k + 4, 0:C]), [], [W("qxs")], dma="doc")
     emit("s", lambda: g.sync.dma_start(T.lq[:, :], T.lqf[0:128:16, 0:K]), [], [W("lqf")], dma="dlq")

@@ -6,11 +6,12 @@ UNIT = 8192.0
 MID = 144.0
 BIG = 1024.0
 LIFT = 512.0
+WHOLE = 2.0 ** 23
 TINY = 1e-36
 MW = C + 16
-PW = 40
+PW = 48
 CODE, F32, BF, I32, U16, U8 = "float8_e4m3fn_x4", "float32", "bfloat16", "int32", "uint16", "uint8"
-ORD, NA = (0, 1, 2), 3
+HV = (6, 6, 6, 6)
 CHUNKS = [[9, 8, 7], [6, 5], [4, 3], [2, 1], ["lt", "eq"]]
 PLANE = {"lt": (0, 0), "eq": (0, 1), 9: (216, 0)}
 GW = 360
@@ -28,21 +29,21 @@ def _sb(dtype, **names):
         SCRATCH[n] = ("sbuf", [128, w], dtype)
 
 
-_sb(BF, x0=4 * C, X=1600, XS=4 * C, ub=512, vb=512, neg=528, OH=528, cb=2568, G=4 * GW, m16=C, e64=128,
+_sb(BF, x0=4 * C, X=1600, ub=512, vb=512, neg=528, OH=528, cb=1536, G=4 * GW, m16=C, e64=128,
     A5=448, Et=512, Vt=512, DE=448, CV=448, MT=4 * MW, wrb=C, wrS=MW, am=MW, BR=320, TR=320)
-_sb(F32, r4=K, r8=144, r16=C, pflt=24, ic=C, cd=C, dm=28, c16=28, yl=NJ, lf=72, ya=16, yb=16, yc=16,
+_sb(F32, r4=K, r8=144, r16=C, pflt=24, ic=C, cd=C, dm=28, c16=28, yl=NJ, lf=72, ya=8, yb=16, KR=96, KT=96, TP=320,
     z=C, zs=C, zz=144, B16=C, B8=144, M4=K, M5=K, M8=144, OE=C, sg=C, Vr=C, Rs=NJ, PL=C, ab=C, rl=2 * C, TG=C, c9=NJ,
-    Q1=C, Q2=C, Q3=C, Q4=C, P1=K, P2=K, P4=K, w1=K, wA=K, wE=K, FQ=448, eqn=28, sel=28, lqf=K, q0=K, q1=K, qa=2 * K, qb=2 * K,
+    Q1=C, Q2=C, Q3=C, Q4=C, P1=K, P2=K, P4=144, w1=K, wA=K, wE=K, FQ=448, eqn=28, sel=28, lqf=K, q0=K, q1=K, qa=2 * K, qb=2 * K,
     q4=2 * K + 2, yo=C)
-_sb(I32, rvt=NJ, pint=8, yi=16, qi=28, qj=28, qz=K)
-_sb(U16, rvl=NJ, lu=76, lA=28, rkl=NJ, LL=80, Pp=K, lE=28, lQ=28, lX=28, pls=PW * ROUNDS, pll=PW * ROUNDS)
-for _n, _w in [("qx", C), ("qu", 128), ("qv", 128), ("uo", 128), ("um", 128), ("wq", 512), ("cq", CZ), ("gq", GW), ("vq", 128),
+_sb(I32, rvt=NJ, pint=8, yi=8, qi=28, qj=28)
+_sb(U16, rvl=NJ, lu=76, lA=28, rkl=NJ, LL=80, lE=28, lQ=28, lX=28, pls=PW * ROUNDS, pll=PW * ROUNDS)
+for _n, _w in [("qx", C), ("qu", 128), ("qv", 128), ("uo", 128), ("um", 128), ("wq", 512), ("cq", CZ + 512), ("gq", GW), ("vq", 128),
                ("mq", MW), ("eq", 128 * ROUNDS), ("le", 128 * ROUNDS)]:
     SCRATCH[_n] = ("sbuf", [128, _w], CODE)
     SCRATCH[_n + "s"] = ("sbuf", [128, _w], U8)
 
 QS = {"v": "qsv", "a": "qsa", "t": "qst", "g": "qsg"}
-DS = ["dx", "du", "dv", "drv", "dwc", "dws", "dG", "dpad", "dwr", "dP", "dlq", "doc", "dy"]
+DS = ["dx", "du", "dv", "drv", "dwc", "dws", "dG", "dpad", "dwr", "dlq", "doc", "dy"]
 SEMAPHORES = list(QS.values()) + DS + ["rl"] + ["ap%d" % _t for _t in range(ROUNDS)] + ["ae%d" % _t for _t in range(ROUNDS)]
 
 
@@ -230,13 +231,14 @@ def rank_program(g, core, T, topo):
         emit("v", lambda: g.vector.tensor_copy(ap(W(out)).bitcast(dt.uint32), ap(W("qu")).bitcast(dt.uint32).indirect(ap(off))), [W(out)], [W("qu"), off])
         emit("a", lambda: g.scalar.activation(ap(W(out + "s")), ap(W("qus")).indirect(ap(off)), AF.Copy), [W(out + "s")], [W("qus"), off])
 
-    LF, L2, L4, LQ, SF, EF, LB, LR, LA, LM, K2, K3, K4, K5, K6, KP = (W("pflt", i, i + 1) for i in range(16))
+    LF, L2, L4, LQ, LB, LR, LA, LM, K2, K5, K6 = (W("pflt", i, i + 1) for i in range(11))
     PI = W("pint", 0, 1)
     C16 = W("c16", 0, NJ)
-    sO, sM, lOE, lrv, lrq, lsel, lp7 = (W("lu", a, b) for a, b in ((0, 8), (8, 16), (16, 34), (34, 52), (52, 59), (60, 65), (68, 75)))
+    sO, sM, lOE, lrv, lrq, lsel, lsp = (W("lu", a, b) for a, b in ((0, 8), (8, 16), (16, 34), (34, 52), (52, 59), (60, 65), (68, 71)))
 
-    def columns(row, tmp, i1, i2, out):
+    def columns(row, tmp, i1, i2, out, between):
         scan(tmp, row, W("M4"), LIFT * UNIT, A.min, A.add)
+        between()
         ts(i1, (tmp[0], 0, 128, 3, K, 4), LB, A.add)
         ts(i2, i1, int(UNIT) - 1, A.bitwise_and)
         cp(out, i2)
@@ -257,15 +259,17 @@ def rank_program(g, core, T, topo):
     iota(W("lf", 0, 16), [[8, 2], [16, 8]])
     fill(W("neg"), -1.0)
     fill(W("MT"), 0.0)
+    zero("dG", W("G", 4 * 144, 4 * PLANE[8][0]))
     for k in (6, 4, 2):
         zero("dG", W("G", 4 * PLANE[k][0] - 32 * k, 4 * PLANE[k][0]))
-    for i, (sh, mask) in enumerate(((0, 15), (0, 14), (0, 12), (0, 3), (0, 1), (4, 1))):
-        ts(W("pint", i + 1, i + 2), PI, sh, A.logical_shift_right, mask, A.bitwise_and)
+    for i, mask in enumerate((15, 14, 12, 3)):
+        ts(W("pint", i + 1, i + 2), PI, mask, A.bitwise_and)
     act(W("lf", 16, 34), C16, bias=15.0)
     for e in (0, 512):
         act(W("cb", e, e + 512), W("neg", 0, 512), AF.Copy, scale=0.0)
-    cp(W("pflt", 0, 6), W("pint", 1, 7))
+    cp(W("pflt", 0, 4), W("pint", 1, 5))
     cp(W("lu", 0, 34), W("lf", 0, 34))
+    cp(W("rvl"), W("rvt"))
     asel(W("e64", 0, 64), W("neg", 0, 64), [[-16, 8], [0, 8]], A.is_ge, 0, 1)
     asel(W("e64", 64, 128), W("e64", 0, 64), [[16, 8], [0, 8]], A.is_ge, 15, -1)
     for e in (0, 1, 6):
@@ -273,60 +277,68 @@ def rank_program(g, core, T, topo):
     quant("qu", 0, 128, W("ub"))
     pick("uo", sO)
     pick("um", sM)
+    ts(LM, L2, 0.0, A.is_equal, 10 * BIG, A.mult)
+    ts(K2, L2, -BIG / 2, A.mult, 7 * BIG + C // 2 - 1, A.add)
     iota(W("r16"), [[0, NJ], [1, 16]])
-    asel(W("cb", 1024, 1544), W("neg", 0, 520), [[-1, 520]], A.is_equal, 1, 4)
-    asel(W("cb", 1027, 1539, 4), W("cb", 1027, 1539, 4), [[1, 128]], A.not_equal, 0, -1, -1.0)
+    asel(W("OH"), W("neg"), [[-1, 528]], A.is_equal, 3, 4)
+    asel(W("OH", 1, 513, 4), W("OH", 1, 513, 4), [[1, 128]], A.not_equal, 0, -1, -1.0)
     asel(W("cb", 513, 1024, 8), W("e64", 64, 128), [[16, 8], [2, 8]], A.is_gt, 0, -1)
     asel(W("cb", 519, 1024, 8), W("e64", 64, 128), [[16, 8], [2, 8]], A.is_ge, 0, -1)
     iota(W("r8"), [[0, NJ], [2, 8]], 1)
-    iota(W("ic"), [[int(UNIT), C]])
-    iota(W("Rs", 8, NJ), [[0, NJ - 8]])
-    iota(W("c9"), [[16, 2], [0, 9]], -16)
-    iota(W("cd"), [[4, C]], 4)
-    iota(W("yc"), [[178, 2], [0, 8]], -289)
-    zero("dpad", W("cb", 2048, 2560))
+    zero("dpad", W("cb", 1024, 1536))
     zero("dpad", W("BR", MW, 320))
     for n in ("Et", "Vt"):
         zero("dpad", W(n, 448, 512))
-    for k in range(2):
-        for base in (-64, 64):
-            o = W("cb", 2048 + k, 2560, 4)
-            asel(o, o, [[32, 4], [1000, 4], [16, 8]], A.not_equal, base - 1000 * k, -1, LIFT)
-    iota(W("r4"), [[0, 28], [4, 4]], 2)
-    asel(W("OH"), W("neg"), [[-1, 528]], A.is_equal, 3, 4)
-    iota(W("q4", 2 * K + 1, 2 * K + 2), [[0, 1]], int(LIFT * UNIT))
-    iota(W("qb", 1, 2 * K, 2), [[0, K]])
+
+    def consts_later():
+        iota(W("OH", 1, 513, 4), [[0, 128]])
+        iota(W("ic"), [[int(UNIT), C]])
+        iota(W("Rs", 8, NJ), [[0, NJ - 8]])
+        iota(W("c9"), [[16, 2], [0, 9]], -16)
+        iota(W("cd"), [[4, C]], 4)
+        for k in range(2):
+            for base in (-64, 64):
+                o = W("cb", 1024 + k, 1536, 4)
+                asel(o, o, [[32, 4], [1000, 4], [16, 8]], A.not_equal, base - 1000 * k, -1, LIFT)
+        for c0, c1, pattern, base in ((0, 16, [[0, 8], [24, 2]], 3), (16, 32, [[0, 8], [-24, 2]], 12),
+                                      (32, 40, [[32, 4], [160, 2]], 0), (40, 48, [[2, 4], [10, 2]], 257), (48, 64, [[-16, 2], [32, 4], [-128, 2]], 144),
+                                      (64, 80, [[17, 2], [2, 4], [10, 2]], 240), (80, 96, [[-1, 2], [2, 4], [-8, 2]], 249)):
+            iota(W("KR", c0, c1), pattern, base)
+        iota(W("r4"), [[0, 28], [4, 4]], 2)
+        iota(W("P4", 0, 16), [[0, 16]])
+        iota(W("P4", 128, 144), [[0, 16]])
+        iota(W("TP", 288, 320), [[0, 32]])
+        iota(W("q4", 2 * K + 1, 2 * K + 2), [[0, 1]], int(LIFT * UNIT))
+        iota(W("qb", 1, 2 * K, 2), [[0, K]])
 
     def consts_first():
         ts(W("m16"), W("r16"), LF, A.is_equal)
         act(W("B16"), W("r16"), AF.Sign)
-        act(W("yl"), C16, bias=LF)
-        act(W("lf", 34, 52), W("yl"), scale=-1.0, bias=C - 1.0)
+        for e in (7, 512, 518):
+            act(W("cb", e, e // 512 * 512 + 512, 8), W("e64", 64, 128), AF.Copy)
         dma("s", "dwc", W("wq"), W("wc"), o8=True)
         dma("s", "dws", W("wqs"), W("ws"))
         dma("s", "dv", W("vb"), W("v"))
 
     def consts_count():
-        fill(W("G", 4 * 144, 4 * PLANE[8][0]), 0.0)
-        for e in (7, 512, 518):
-            cp(W("cb", e, e // 512 * 512 + 512, 8), W("e64", 64, 128))
-        quant("cq", CI, CI + 128, W("cb", 1025, 1537))
-        quant("cq", CI + 128, CS, W("cb", 1024, 1536))
+        ts(W("yl"), C16, LF, A.add)
+        quant("cq", CI, CI + 128, W("OH", 1, 513))
+        quant("cq", CI + 128, CS, W("OH", 0, 512))
+        ts(lrv, W("yl"), -1.0, A.mult, C - 1.0, A.add)
+        consts_later()
 
     def consts_rank():
-        cp(W("rvl"), W("rvt"))
-        cp(lrv, W("lf", 34, 52))
-        fill(W("wrS"), -MID)
-        act(W("B8"), W("r8"), scale=0.0, bias=-100 * BIG)
-        ts(LM, L2, 0.0, A.is_equal, 10 * BIG, A.mult)
-        ts(K2, L2, -BIG / 2, A.mult, 7 * BIG + C // 2 - 1, A.add)
         act(W("zz"), W("r8"), AF.Sign, scale=-1.0, bias=L2)
         act(W("yo"), W("ic"), AF.Relu, scale=1.0 / UNIT, bias=-1.0)
         act(W("M8"), W("zz"), scale=5 * BIG, bias=4 * BIG)
-        ts(LR, K2, LM, A.subtract)
+        act(LR, LM, scale=-1.0, bias=K2)
+        for b in range(4):
+            quant("cq", 128 * b, 128 * b + 128, W("OH", 3 - b, 515 - b))
 
     def consts_rv():
         act(W("Q4"), ind(W("yo"), W("rvl")), scale=-1.0, bias=C - 1 - MID)
+        act(W("B8"), W("r8"), scale=0.0, bias=-100 * BIG)
+        act(W("wrS"), W("neg", 0, MW), AF.Copy, scale=MID)
         act(W("wrb"), ind(W("Q4"), lrv), AF.Copy)
         for k in range(2):
             for a in range(4):
@@ -338,13 +350,12 @@ def rank_program(g, core, T, topo):
                         rows_to("s", "dwr", o, "wrb", (g0 + r0) % 8, (g0 + r0) % 8 + r1 - r0, n)
 
     def consts_bounds():
-        act(K3, EF, scale=-48.0, bias=24.0)
-        act(K4, EF, scale=9.0, bias=3.0)
-        act(W("ya", 0, 8), W("yl", 0, 8), scale=1.0 / 18, bias=-8.5 / 18)
-        act(KP, SF, scale=K3, bias=K4)
-        act(W("ya", 8, 16), W("yl", 0, 8), scale=1.0 / 7, bias=-3.0 / 7)
-        act(W("yb", 0, 8), W("yl", 0, 8), scale=16.0, bias=KP)
-        act(W("yb", 8, 16), W("yl", 0, 8), scale=16.0)
+        turn(W("KT"), W("KR"))
+        ts(W("yi"), W("yl", 0, 8), -8.5, A.add, 1.0 / 18, A.mult)
+        act(W("yb", 0, 8), W("yl", 0, 8), scale=16.0, bias=W("KT", 0, 1))
+        act(W("yb", 8, 9), W("KT", 32, 33))
+        act(W("yb", 9, 11), W("c16", 1, 3), bias=W("KT", 64, 65))
+        ts(W("ya"), W("yi"), -289.0, A.mult)
 
     def consts_lists():
         act(W("w1"), W("r4"), AF.Sign, scale=-1.0, bias=L4)
@@ -360,8 +371,11 @@ def rank_program(g, core, T, topo):
         act(W("lf", 52, 59), W("yl", 0, 7), scale=-1.0, bias=K - 1.0)
         cp(W("M5"), W("M4"))
         ts(W("M5", 3, K, 4), W("dm"), LF, A.subtract, -4.0 * C, A.add)
+        act(W("OH"), W("OH"), AF.Copy, scale=2.0 ** -6)
         cp(lrq, W("lf", 52, 59))
         quant("qv", 0, 128, W("vb"))
+        for b in range(4):
+            quant("cq", CZ + 128 * b, CZ + 128 * b + 128, W("OH", 3 - b, 515 - b))
 
     ne, np_ = len(topo.engines(core, nxt)), len(topo.engines(prv, core))
     rid, pid = topo.addr(nxt, core)
@@ -396,7 +410,9 @@ def rank_program(g, core, T, topo):
             act(W("OE"), ind(W("zs"), lOE), AF.Copy)
             consts_count()
         else:
-            cp(W("OE", 64, C), ind(W("zs"), W("lu", 20, 34)))
+            act(W("OE", 64, C), ind(W("zs"), W("lu", 20, 34)), AF.Copy)
+            scan(W("Vr"), W("cd"), W("sg"), 0.0, A.max, A.mult)
+            cp(W("OE", 0, 64), ind(W("zs"), W("lu", 16, 20)))
 
         def far(k):
             o = 8 * k * (k - 1)
@@ -422,14 +438,9 @@ def rank_program(g, core, T, topo):
             if k > 1:
                 far(k - 1)
             won(k)
-            if t and k == 7:
-                act(W("OE", 0, 64), ind(W("zs"), W("lu", 16, 20)), AF.Copy)
-        for n, ch in enumerate(CHUNKS):
+        for n, ch in enumerate(CHUNKS[:-1]):
             for k in ch:
-                if k in ("lt", "eq"):
-                    tt(lane(k, 0, C), So, W("OE"), A.is_lt if k == "lt" else A.is_equal)
-                else:
-                    tt(lane(k, 0, C - 16 * k), bk(0, 0, C - 16 * k), W("OE", 16 * k, C), A.is_lt)
+                tt(lane(k, 0, C - 16 * k), bk(0, 0, C - 16 * k), W("OE", 16 * k, C), A.is_lt)
             if t == 0 and n == 0:
                 quant("cq", CC, CI, W("cb", 0, 1024))
             if t == 0 and n == 2:
@@ -437,23 +448,22 @@ def rank_program(g, core, T, topo):
                 consts_rv()
             if n:
                 chunk(CHUNKS[n - 1])
+        tt(lane("lt", 0, C), So, W("OE"), A.is_lt)
+        chunk(CHUNKS[-2])
+        tt(lane("eq", 0, C), So, W("OE"), A.is_equal)
         chunk(CHUNKS[-1])
         if t == 0:
             ts(W("B8", 0, 144, 8), W("c9"), LM, A.subtract)
-        scan(W("Vr"), W("cd"), W("sg"), 0.0, A.max, A.mult)
+            scan(W("Vr"), W("cd"), W("sg"), 0.0, A.max, A.mult)
         scan(W("zz"), W("B8"), bk(1, 0, 144), -100 * BIG, A.max, A.add)
-        if t:
-            state()
+        if t == 0:
+            unpack()
+        state()
         tt(W("M8", 7, 144, 8), W("Rs"), W("zz", 7, 144, 8), A.subtract)
         scan(W("zz"), bk(6, 0, 144), W("M8"), 4 * BIG, A.min, A.add)
         ts(W("rkl"), W("zz", 7, 144, 8), LR, A.add)
         if t == 0:
-            quant("cq", CS, CZ, W("cb", 2048, 2560))
-            consts_bounds()
-            consts_lists()
-            for b in range(4):
-                quant("cq", 128 * b, 128 * b + 128, W("OH", 3 - b, 515 - b))
-            unpack()
+            quant("cq", CS, CZ, W("cb", 1024, 1536))
         scatter(W("PL"), W("rkl"), W("Vr"))
         ts(W("MT", 4, 4 * C + 4, 4), W("PL"), 0.0, A.is_gt, -0.5, A.add)
         act(W("MT", 69, 4 * MW, 4), W("PL", 0, C - 1), AF.Sign)
@@ -461,29 +471,24 @@ def rank_program(g, core, T, topo):
         quant("mq", 0, MW, W("MT"))
         mm(1, "cq", CS, "mq", 0, MW)
         if t == 0:
-            state()
-            cp(W("yi"), W("ya"))
-            fill(W("pls"), 0)
-            tt(W("ya"), W("yi"), W("yc"), A.mult)
+            consts_bounds()
+            consts_lists()
 
         def fixed():
             scan(W("wA"), W("ab", 1, 2 * K, 2), W("M4"), LIFT * UNIT, A.min, A.add)
             ts(W("lA"), W("wA", 3, K, 4), LA, A.add)
-        if t:
-            fixed()
-            act(W("A5"), ind(W("X", 0, 4 * C), W("lA")), AF.Copy)
+        scan(W("TG"), W("ic"), W("ab"), 0.0, A.max, A.add)
         tt(W("am"), bk(1, 0, MW), W("wrS"), A.min)
         if t == 0:
-            tt(W("yb"), W("yb"), W("ya"), A.add)
-        scan(W("TG"), W("ic"), W("ab"), 0.0, A.max, A.add)
+            tt(W("yb", 0, 8), W("yb", 0, 8), W("ya"), A.add)
         scan(W("BR", 0, MW), W("am"), W("am"), -MID, A.max, A.max)
         if t == 0:
-            cp(W("lu", 60, 76), W("yb"))
+            cp(W("lu", 60, 71), W("yb", 0, 11))
         odd = {n: (n, 0, 128, 1, 2 * K, 2) for n in ("TG", "Q1", "Q2", "Q3", "Q4")}
         turn(W("TR"), W("BR"))
         ts(W("LL"), ind(W("TR"), lsel), MID, A.add)
         for d in range(1, 5):
-            H = 10 if d == 1 else 6
+            H = HV[d - 1]
             src, o = W("TG") if d == 1 else W("Q%d" % (d - 1)), NJ * (d - 1)
             cp(W("Q%d" % d, 0, 16 * H), ind(src, W("LL", o, o + H)))
             if H < NJ:
@@ -494,26 +499,31 @@ def rank_program(g, core, T, topo):
                 scan(W("P2"), W("P1"), odd["Q2"], 0.0, A.max, A.max)
             if d == 4:
                 scan(W("P1"), W("P2"), odd["Q3"], 0.0, A.max, A.max)
-            if t == 0 and d == 1:
+            if d == 1:
                 fixed()
-        scan(W("P4"), W("P1"), odd["Q4"], 0.0, A.max, A.max)
-        ts(W("Pp"), ind(W("P4"), lp7), 1.0 / UNIT, A.mult)
+        P4 = W("P4", 16, 16 + K)
+        scan(P4, W("P1"), odd["Q4"], 0.0, A.max, A.max)
+        turn(W("TP", 0, 128), W("P4", 16, 144))
+        turn(W("TP", 128, 256), W("P4", 0, 128))
+        for p in (0, 64):
+            cp(W("TP", 272, 288, p0=p, p1=p + 64), W("TP", 0, 256, 16, p0=64 - p, p1=128 - p))
+        for p in (32, 64, 96):
+            act(W("TP", 256, 272, p0=p, p1=p + 32), W("TP", 0, 256, 16, p0=p - 32, p1=p), AF.Copy)
+        cp(W("TP", 256, 272, p1=32), W("TP", 0, 256, 16, p0=96))
         o = PW * t
-        for d in range(5):
-            for g0, g1, to in ((0, 8 - d, 16 * d), (8 - d, 8, 0)):
-                if g0 < g1:
-                    rows_to("sa"[d > 2], "dP", W("pls", o + 8 * d, o + 8 * d + 7, p0=to, p1=to + 16 * (g1 - g0)), "Pp", g0, g1, K)
-        if t == 0:
-            act(W("A5"), ind(W("X", 0, 4 * C), W("lA")), AF.Copy)
-        columns(W("P4"), W("wE"), W("qi"), W("qj"), W("lE"))
+        pl, plo = W("pls", o, o + 40), W("pll", o, o + 40)
+
+        def lists():
+            ts(W("pls", o, o + PW), ind(W("TP"), lsp), 1.0 / UNIT, A.mult)
+            send(plo, pl, ap, "ap%d" % t)
+        act(W("A5"), ind(W("X", 0, 4 * C), W("lA")), AF.Copy)
+        columns(P4, W("wE"), W("qi"), W("qj"), W("lE"), lists)
         tt(W("Et", 0, 448), ind(W("X", 0, 4 * C), W("lE")), W("A5"), A.add)
         quant("eq", 128 * t, 128 * t + 128, W("Et"))
-        pl, plo = W("pls", o, o + PW), W("pll", o, o + PW)
         e, eo = W("eq", 128 * t, 128 * t + 128), W("le", 128 * t, 128 * t + 128)
         es, eso = W("eqs", 128 * t, 128 * t + 128), W("les", 128 * t, 128 * t + 128)
-        for i in ORD:
-            send(*[(plo, pl, ap, "ap%d" % t), (eo, e, by, "ae%d" % t), (eso, es, ap, "ae%d" % t)][i])
-        ts(W("XS"), W("X", 0, 4 * C), 2.0 ** -5, A.mult)
+        send(eo, e, by, "ae%d" % t)
+        send(eso, es, ap, "ae%d" % t)
         if t == 0:
             consts_late()
         arrive([plo], "ap%d" % t, np_)
@@ -521,46 +531,40 @@ def rank_program(g, core, T, topo):
         act(W("qa", 1, 2 * K, 2), ind(W("Q3"), W("pll", o + 24, o + 31)), AF.Copy)
         act(W("qb", 0, 2 * K, 2), ind(W("Q4"), W("pll", o + 32, o + 39)), AF.Copy)
         for b in range(4):
-            mm(2 + b, "cq", 128 * b, "le", 128 * t, 128)
-        for b in range(NA):
-            act(W("DE", b, 448, 4), bk(2 + b, 0, K), AF.Copy, scale=-2.0 ** -6)
+            mm(2 + b, "cq", CZ + 128 * b, "le", 128 * t, 128)
         cp(W("q0"), ind(W("Q1"), W("pll", o + 8, o + 15)))
         tt(W("q1"), ind(W("TG"), W("pll", o, o + 7)), W("q0"), A.max)
         tt(W("qa", 0, 2 * K, 2), ind(W("Q2"), W("pll", o + 16, o + 23)), W("q1"), A.max)
         scan(W("q4", 0, 2 * K), W("qa"), W("qb"), 0.0, A.max, A.max)
-        columns(W("q4", 1, 2 * K, 2), W("wE"), W("qi"), W("qj"), W("lQ"))
-        act(W("FQ"), ind(W("X", 0, 4 * C), W("lQ")), AF.Copy)
-        for b in range(NA, 4):
-            ts(W("DE", b, 448, 4), bk(2 + b, 0, K), -2.0 ** -6, A.mult)
-        tt(W("Vt", 0, 448), ind(W("XS"), W("lQ")), W("DE"), A.add)
+        columns(W("q4", 1, 2 * K, 2), W("wE"), W("qi"), W("qj"), W("lQ"),
+                lambda: scan(W("w1"), W("q4", 3, 2 * K + 2, 2), W("M5"), LIFT * UNIT, A.min, A.add))
+        ts(W("DE", 0, 256), ind(W("X", 0, 4 * C), W("lQ", 0, 16)), 2.0 ** -5, A.mult)
+        act(W("DE", 256, 448), ind(W("X", 0, 4 * C), W("lQ", 16, 28)), AF.Copy, scale=2.0 ** -5)
+        act(W("FQ"), W("DE"), AF.Copy, scale=2.0 ** 5)
+        tt(W("eqn"), W("wE", 3, K, 4), W("w1", 3, K, 4), A.subtract)
+        tt(W("sel"), W("qj"), W("eqn"), A.max)
+        for b in range(4):
+            tt(W("Vt", b, 448, 4), W("DE", b, 448, 4), bk(2 + b, 0, K), A.subtract)
         if t == ROUNDS - 1:
-            act(W("q0"), W("q4", 1, 2 * K, 2), AF.Copy)
-            act(W("q1"), ind(W("q0"), lrq), scale=-1.0 / UNIT, bias=C - 1.0)
+            act(W("q0"), W("q4", 1, 2 * K, 2), scale=-1.0 / UNIT, bias=WHOLE + C - 1)
+            act(W("lqf"), ind(W("q0"), lrq), bias=-WHOLE)
+            emit("s", lambda: g.sync.dma_start(T.lq[:, :], T.lqf[0:128:16, 0:K]), [], [W("lqf")], dma="dlq")
         quant("vq", 0, 128, W("Vt"))
         hb = (0, 1, 6, 7)
         for b in range(4):
             mm(hb[b], "wq", 128 * b, "vq", 0, 128)
-        scan(W("w1"), W("q4", 3, 2 * K + 2, 2), W("M5"), LIFT * UNIT, A.min, A.add)
-        tt(W("CV", 0, 448, 4), bk(hb[0], 0, K), W("FQ", 0, 448, 4), A.add)
-        tt(W("eqn"), W("wE", 3, K, 4), W("w1", 3, K, 4), A.subtract)
-        tt(W("CV", 1, 448, 4), bk(hb[1], 0, K), W("FQ", 1, 448, 4), A.add)
-        tt(W("sel"), W("qj"), W("eqn"), A.max)
-        tt(W("CV", 2, 448, 4), bk(hb[2], 0, K), W("FQ", 2, 448, 4), A.add)
         cp(W("lX"), W("sel"))
-        tt(W("CV", 3, 448, 4), bk(hb[3], 0, K), W("FQ", 3, 448, 4), A.add)
+        for b in range(4):
+            tt(W("CV", b, 448, 4), bk(hb[b], 0, K), W("FQ", b, 448, 4), A.add)
         scatter(W("X"), W("lX"), W("CV"))
     quant("qx", 0, C, W("X", 0, 4 * C))
     HY = 160
     mm(0, "qv", 0, "qx", 0, HY)
     mm(1, "qv", 0, "qx", HY, C - HY)
-    emit("a", lambda: g.scalar.dma_start(T.oc[:, :], by(W("qx"))), [], [W("qx")], dma="doc")
-    cp(W("qz"), W("q1"))
-    cp(W("yo", 0, HY), bk(0, 0, HY))
-    act(W("yo", HY, C), bk(1, 0, C - HY), AF.Copy)
-    emit("s", lambda: g.sync.dma_start(T.y[:, 0:HY], T.yo[:, 0:HY]), [], [W("yo", 0, HY)], dma="dy")
-    emit("a", lambda: g.scalar.dma_start(T.y[:, HY:C], T.yo[:, HY:C]), [], [W("yo", HY, C)], dma="dy")
-    cp(W("lqf"), W("qz"))
+    emit("s", lambda: g.sync.dma_start(T.oc[:, :], by(W("qx"))), [], [W("qx")], dma="doc")
     for k in range(4):
         emit("s", lambda: g.sync.dma_start(T.osc[4 * k:4 * k + 4, :], T.qxs[32 * k:32 * k + 4, 0:C]), [], [W("qxs")], dma="doc")
-    emit("s", lambda: g.sync.dma_start(T.lq[:, :], T.lqf[0:128:16, 0:K]), [], [W("lqf")], dma="dlq")
+    cp(W("yo", 0, HY), bk(0, 0, HY))
+    act(W("yo", HY, C), bk(1, 0, C - HY), AF.Copy)
+    emit("a", lambda: g.scalar.dma_start(T.y[:, :], T.yo[:, :]), [], [W("yo")], dma="dy")
     finish([("rl", rlc[0])] + [("ap%d" % t, np_) for t in range(ROUNDS)] + [("ae%d" % t, 2 * np_) for t in range(ROUNDS)])

@@ -3,23 +3,31 @@ from concourse.mybir import dt, AluOpType, ActivationFunctionType
 C, K, ROUNDS = 288, 112, 3
 NJ = C // 16
 UNIT = 8192.0
-MID = 144.0
+MID = 128.0
 BIG = 1024.0
 LIFT = 512.0
 WHOLE = 2.0 ** 23
 TINY = 1e-36
-MW = C + 16
+MARK = 8
+HUGE = 2.0 ** 90
+SMALL = 1.0 / 64
+HC = C // 2
+T2, S1, S2, TW = C, 2 * C + 32, 2 * C + 72, 2 * C + 128
 PW = 48
 CODE, F32, BF, I32, U16, U8 = "float8_e4m3fn_x4", "float32", "bfloat16", "int32", "uint16", "uint8"
-HV = (6, 6, 6, 6)
-CHUNKS = [[9, 8, 7], [6, 5], [4, 3], [2, 1], ["lt", "eq"]]
-PLANE = {"lt": (0, 0), "eq": (0, 1), 9: (216, 0)}
-GW = 360
-for _k in (8, 6, 4, 2):
-    GW += 8 * _k if _k < 8 else 0
-    PLANE[_k], PLANE[_k - 1] = (GW, 0), (GW, 1)
+HV = (4, 6, 6, 6)
+DV = 12
+SP = 3
+FAR = 8
+EARLY = 14
+CHUNKS = [(0, 9), (1, 2), (3, 4), (5, 6), (7, 8)]
+PLANE = {}
+GW = 0
+for _a, _b in CHUNKS:
+    GW += 8 * _b
+    PLANE[_a], PLANE[_b] = (GW, 0), (GW, 1)
     GW += 144
-CE, CC, CD, CI, CS, CZ = 0, 512, 640, 768, 1024, 1152
+CE, CC, CI, CZ = 0, 512, 640, 896
 
 SCRATCH = {"ps": ("psum", [128, 4096], F32)}
 
@@ -29,22 +37,23 @@ def _sb(dtype, **names):
         SCRATCH[n] = ("sbuf", [128, w], dtype)
 
 
-_sb(BF, x0=4 * C, X=1600, ub=512, vb=512, neg=528, OH=528, cb=1536, G=4 * GW, m16=C, e64=128,
-    A5=448, Et=512, Vt=512, DE=448, CV=448, MT=4 * MW, wrb=C, wrS=MW, am=MW, BR=320, TR=320)
-_sb(F32, r4=K, r8=144, r16=C, pflt=24, ic=C, cd=C, dm=28, c16=28, yl=NJ, lf=72, ya=8, yb=16, KR=96, KT=96, TP=320,
-    z=C, zs=C, zz=144, B16=C, B8=144, M4=K, M5=K, M8=144, OE=C, sg=C, Vr=C, Rs=NJ, PL=C, ab=C, rl=2 * C, TG=C, c9=NJ,
-    Q1=C, Q2=C, Q3=C, Q4=C, P1=K, P2=K, P4=144, w1=K, wA=K, wE=K, FQ=448, eqn=28, sel=28, lqf=K, q0=K, q1=K, qa=2 * K, qb=2 * K,
+_sb(BF, x0=4 * C, X=1600, ub=512, vb=512, neg=528, OH=528, OI=528, cb=512, G=4 * GW, m16=C, B16=C, e64=72,
+    A5=448, Et=512, Vt=512, DE=448, CV=448, wrb=C, am=C, BR=320, TR=TW)
+_sb(F32, r4=K, r8=144, pflt=24, ic=C, cd=C, dm=28, c16=28, lk=10, lf=72, KS=160, KR=C, KT=12, TP=320,
+    z=C, zs=C, zz=144, B8=144, M4=K, M5=K, M8=144, OE=C, sg=C, Vr=C, Rs=NJ, PL=C, ab=C, rl=2 * C, TG=C, c9=NJ,
+    Q1=C, Q2=C, Q3=C, Q4=C, P1=K, P2=K, P4=144, w1=K, wA=K, wE=K, FQ=448, eqn=28, sel=28, lqf=K, q0=K, qa=2 * K, qb=2 * K,
     q4=2 * K + 2, yo=C)
-_sb(I32, rvt=NJ, pint=8, yi=8, qi=28, qj=28)
-_sb(U16, rvl=NJ, lu=76, lA=28, rkl=NJ, LL=80, lE=28, lQ=28, lX=28, pls=PW * ROUNDS, pll=PW * ROUNDS)
-for _n, _w in [("qx", C), ("qu", 128), ("qv", 128), ("uo", 128), ("um", 128), ("wq", 512), ("cq", CZ + 512), ("gq", GW), ("vq", 128),
-               ("mq", MW), ("eq", 128 * ROUNDS), ("le", 128 * ROUNDS)]:
+_sb(I32, rvt=NJ, pint=8, qi=28, qj=28)
+_sb(U16, rvl=NJ, lu=90, l16=NJ, lA=28, rkl=NJ, LL=80, lE=28, lQ=28, lX=28, pls=PW * ROUNDS, pll=PW * ROUNDS)
+for _n, _w in [("qx", C), ("qu", 128), ("qv", 128), ("uo", 128), ("wq", 512), ("cq", CZ + 512), ("gq", GW), ("vq", 128),
+               ("eq", 128 * ROUNDS), ("le", 16 + K * ROUNDS)]:
     SCRATCH[_n] = ("sbuf", [128, _w], CODE)
     SCRATCH[_n + "s"] = ("sbuf", [128, _w], U8)
 
 QS = {"v": "qsv", "a": "qsa", "t": "qst", "g": "qsg"}
-DS = ["dx", "du", "dv", "drv", "dwc", "dws", "dG", "dpad", "dwr", "dlq", "doc", "dy"]
-SEMAPHORES = list(QS.values()) + DS + ["rl"] + ["ap%d" % _t for _t in range(ROUNDS)] + ["ae%d" % _t for _t in range(ROUNDS)]
+DS = ["dx", "du", "dv", "drv", "dwc", "dws", "dG", "dpad", "dcb", "dz", "dk", "dle", "dlq", "doc", "dy"]
+JS = {"jg1": 4, "jg3": 4, "jg5": 4, "jg7": 4, "jn": 2, "jb": 6, "jq1": 2, "jq2": 2, "jq3": 2, "jq4": 3, "jp": 6, "jl": 4, "jv": 3, "jw": 2, "jx": 5}
+SEMAPHORES = list(QS.values()) + DS + list(JS) + ["rl"] + ["ap%d" % _t for _t in range(ROUNDS)] + ["ae%d" % _t for _t in range(ROUNDS)]
 
 
 def make_tracker(g, T):
@@ -54,6 +63,8 @@ def make_tracker(g, T):
     snaps = {}
     acc = {}
     seq = [0]
+    joint = []
+    last = {}
 
     def hit(a, b):
         if a[1] >= b[2] or b[1] >= a[2] or a[3] >= b[4] or b[3] >= a[4]:
@@ -80,6 +91,9 @@ def make_tracker(g, T):
                 return
             if sem in DS:
                 val = cnt[sem]
+            if sem in JS:
+                val = -(-val // JS[sem]) * JS[sem]
+                assert val <= cnt[sem], sem
             if need.get(sem, (0, 0))[0] < val:
                 need[sem] = (val, order)
         for r0 in ins:
@@ -94,13 +108,16 @@ def make_tracker(g, T):
                     want(rec)
         for sem, (val, order) in sorted(need.items(), key=lambda e: -e[1][1]):
             if clk[q].get(sem, 0) < val:
+                if sem == QS.get(q):
+                    val = max(val, cnt[sem] - (last.get(q) == sem))
                 eng[q].wait_ge(T.sem[sem], val)
                 merge(q, sem, val)
         made = call()
         seq[0] += 1
         if remote:
             return
-        sem = dma or QS[q]
+        sem = dma or joint.pop(0) if dma or joint else QS[q]
+        last[q] = sem
         cnt[sem] = cnt.get(sem, 0) + (16 if dma else 1)
         made.then_inc(T.sem[sem], 16 if dma else 1)
         snaps.setdefault(sem, []).append((cnt[sem], dict(clk[q])))
@@ -124,7 +141,10 @@ def make_tracker(g, T):
         for sem, val in extra:
             if clk["g"].get(sem, 0) < val:
                 g.wait_ge(T.sem[sem], val)
-    return emit, arrive, finish
+
+    def join(sem, n=1):
+        joint.extend([sem] * n)
+    return emit, arrive, finish, join
 
 
 def rank_program(g, core, T, topo):
@@ -134,7 +154,7 @@ def rank_program(g, core, T, topo):
     N = len(T.cores)
     nxt, prv = T.cores[(rank + 1) % N], T.cores[(rank - 1) % N]
     A, AF = AluOpType, ActivationFunctionType
-    emit, arrive, finish = make_tracker(g, T)
+    emit, arrive, finish, join = make_tracker(g, T)
 
     def W(n, c0=0, c1=None, s=1, p0=0, p1=128):
         return (n, p0, p1, c0, c1 if c1 is not None else (SCRATCH[n][1][1] if n in SCRATCH else T[n].shape[1]), s)
@@ -200,6 +220,9 @@ def rank_program(g, core, T, topo):
             outs.append(accum)
         emit("a", lambda: g.scalar.activation(ap(out), ap(a), fn, **kw), outs, ins)
 
+    def acp(out, a):
+        act(out, a, AF.Copy)
+
     def iota(out, pattern, base=0, cm=0):
         kw = {} if SCRATCH[out[0]][2] == I32 else {"allow_small_or_imprecise_dtypes": True}
         emit("g", lambda: g.iota(ap(out), pattern, base, cm, **kw), rg(out), [])
@@ -210,10 +233,6 @@ def rank_program(g, core, T, topo):
     def dma(q, sem, out, a, o8=False, a8=False):
         e = {"s": g.sync, "a": g.scalar}[q]
         emit(q, lambda: e.dma_start(by(out) if o8 else ap(out), by(a) if a8 else ap(a)), rg(out), rg(a), dma=sem)
-
-    def rows_to(q, sem, o, src, g0, g1, n):
-        e = {"s": g.sync, "a": g.scalar}[q]
-        emit(q, lambda: e.dma_start(ap(o), T[src][16 * g0:16 * g1:16, 0:n]), [o], [W(src, p0=16 * g0, p1=16 * g1)], dma=sem)
 
     def quant(n, c0, c1, src):
         o, s = W(n, c0, c1), W(n + "s", c0, c1)
@@ -231,135 +250,117 @@ def rank_program(g, core, T, topo):
         emit("v", lambda: g.vector.tensor_copy(ap(W(out)).bitcast(dt.uint32), ap(W("qu")).bitcast(dt.uint32).indirect(ap(off))), [W(out)], [W("qu"), off])
         emit("a", lambda: g.scalar.activation(ap(W(out + "s")), ap(W("qus")).indirect(ap(off)), AF.Copy), [W(out + "s")], [W("qus"), off])
 
-    LF, L2, L4, LQ, LB, LR, LA, LM, K2, K5, K6 = (W("pflt", i, i + 1) for i in range(11))
-    PI = W("pint", 0, 1)
-    C16 = W("c16", 0, NJ)
-    sO, sM, lOE, lrv, lrq, lsel, lsp = (W("lu", a, b) for a, b in ((0, 8), (8, 16), (16, 34), (34, 52), (52, 59), (60, 65), (68, 71)))
+    LF, L2, L4, LQ, LB, LR, LA, LM, K2, K5, K6, LH, LV = (W("pflt", i, i + 1) for i in range(13))
+    PI, l16 = W("pint", 0, 1), W("l16")
+    C16 = W("lf", 0, NJ)
+    sO, lrv, lrq, lks, lsel, lsp = (W("lu", a, b) for a, b in ((0, 8), (36, 54), (82, 89), (54, 64), (76, 81), (72, 75)))
 
-    def columns(row, tmp, i1, i2, out, between):
-        scan(tmp, row, W("M4"), LIFT * UNIT, A.min, A.add)
-        between()
-        ts(i1, (tmp[0], 0, 128, 3, K, 4), LB, A.add)
-        ts(i2, i1, int(UNIT) - 1, A.bitwise_and)
-        cp(out, i2)
+    def columns(row, tmp, i1, i2, out, between=()):
+        steps = [lambda: scan(tmp, row, W("M4"), LIFT * UNIT, A.min, A.add), lambda: ts(i1, (tmp[0], 0, 128, 3, K, 4), LB, A.add),
+                 lambda: ts(i2, i1, int(UNIT) - 1, A.bitwise_and), lambda: cp(out, i2)]
+        for n, step in enumerate(steps):
+            step()
+            if n < len(between):
+                between[n]()
 
     def lane(k, c0, c1):
         o = 4 * PLANE[k][0] + PLANE[k][1]
         return W("G", o + 2 * c0, o + 2 * c1 - 1, 2)
 
-    def zero(sem, o):
-        dma("s", sem, o, W("MT", 0, o[4] - o[3]))
+    def across(eng, n, o, w, p, back, c0=0):
+        h, p0 = 64 if back == 64 else 32, (p - back) % 128
+        join("jb" if n == "TR" else "jp")
+        eng(W(n, o, o + w // 16, p0=p, p1=p + h), W(n, c0, w, 16, p0=p0, p1=p0 + h))
 
-    dma("a", "drv", W("rvt"), W("rv"))
-    dma("s", "du", W("ub"), W("u"))
-    dma("s", "dx", W("x0"), W("x"))
+    def zero(o):
+        act(o, W("neg", 0, o[4] - o[3]), AF.Copy, scale=0.0)
+
+    def pad(k):
+        return W("G", 4 * PLANE[k][0] - 32 * k, 4 * PLANE[k][0])
+
+    for n, sem, name in (("ub", "du", "u"), ("x0", "dx", "x")):
+        dma("s", sem, W(n), W(name))
 
     iota(PI, [[0, 1]], 0, 1)
-    iota(W("c16"), [[16, 28]])
-    iota(W("lf", 0, 16), [[8, 2], [16, 8]])
+    iota(W("lf", 0, 2 * NJ), [[15, 2], [16, NJ]])
     fill(W("neg"), -1.0)
-    fill(W("MT"), 0.0)
-    zero("dG", W("G", 4 * 144, 4 * PLANE[8][0]))
-    for k in (6, 4, 2):
-        zero("dG", W("G", 4 * PLANE[k][0] - 32 * k, 4 * PLANE[k][0]))
-    for i, mask in enumerate((15, 14, 12, 3)):
+    asel(W("OH"), W("neg"), [[-1, 528]], A.is_equal, 3, 4)
+    asel(W("e64"), W("neg", 0, 72), [[0, 9], [-1, 8]], A.is_ge, 3, 0)
+    iota(W("lk"), [[16, 5], [80, 2]])
+    for i, mask in enumerate((15, 14, 12)):
         ts(W("pint", i + 1, i + 2), PI, mask, A.bitwise_and)
-    act(W("lf", 16, 34), C16, bias=15.0)
-    for e in (0, 512):
-        act(W("cb", e, e + 512), W("neg", 0, 512), AF.Copy, scale=0.0)
-    cp(W("pflt", 0, 4), W("pint", 1, 5))
-    cp(W("lu", 0, 34), W("lf", 0, 34))
-    cp(W("rvl"), W("rvt"))
-    asel(W("e64", 0, 64), W("neg", 0, 64), [[-16, 8], [0, 8]], A.is_ge, 0, 1)
-    asel(W("e64", 64, 128), W("e64", 0, 64), [[16, 8], [0, 8]], A.is_ge, 15, -1)
-    for e in (0, 1, 6):
-        act(W("cb", e, 512, 8), W("e64", 64, 128), AF.Copy)
+    fill(W("B16"), HUGE)
+    cp(W("pflt", 0, 3), W("pint", 1, 4))
+    cp(W("lu", 0, 2 * NJ), W("lf", 0, 2 * NJ))
+    ts(l16, W("neg", 0, NJ), 0.0, A.mult, LF, A.add)
+    fill(W("B16", 0, C, 16), -HUGE)
+    fill(W("cb"), 0.0)
+    zero(pad(9))
+    zero(W("G", 4 * PLANE[9][0] + C, 4 * PLANE[1][0]))
+    act(LH, LF, scale=-HUGE)
+    act(K2, L2, scale=BIG)
+    act(W("m16"), ind(W("lf", 0, 16), l16), AF.Abs, scale=HUGE / 16, bias=LH)
+    for n in range(8):
+        dma("s", "dcb", W("cb", 64 * n, 64 * n + 64, p0=16 * n, p1=16 * n + 16), W("e64", 2, 66, p0=16 * n, p1=16 * n + 16))
+    emit("s", lambda: g.sync.dma_start(ap(W("rvt")), ap(W("rv"))), [W("rvt")], [W("x0")], dma="drv")
+    for sem, outs in (("dG", [pad(4), pad(6), pad(8)]), ("dpad", [W("TR", S1, TW), W("BR", C + 16, 320), W("Et", 448, 512), W("Vt", 448, 512)])):
+        for o in outs:
+            dma("s", sem, o, W("G", 0, o[4] - o[3]))
+    dma("s", "dwc", W("wq"), W("wc"), o8=True)
+    dma("s", "dws", W("wqs"), W("ws"))
+    dma("s", "dv", W("vb"), W("v"))
+
+    def unpacker(b):
+        quant("cq", CE + 128 * b, CE + 128 * b + 128, W("OH", 3 - b, 515 - b))
     quant("qu", 0, 128, W("ub"))
     pick("uo", sO)
-    pick("um", sM)
-    ts(LM, L2, 0.0, A.is_equal, 10 * BIG, A.mult)
-    ts(K2, L2, -BIG / 2, A.mult, 7 * BIG + C // 2 - 1, A.add)
-    iota(W("r16"), [[0, NJ], [1, 16]])
-    asel(W("OH"), W("neg"), [[-1, 528]], A.is_equal, 3, 4)
-    asel(W("OH", 1, 513, 4), W("OH", 1, 513, 4), [[1, 128]], A.not_equal, 0, -1, -1.0)
-    asel(W("cb", 513, 1024, 8), W("e64", 64, 128), [[16, 8], [2, 8]], A.is_gt, 0, -1)
-    asel(W("cb", 519, 1024, 8), W("e64", 64, 128), [[16, 8], [2, 8]], A.is_ge, 0, -1)
-    iota(W("r8"), [[0, NJ], [2, 8]], 1)
-    zero("dpad", W("cb", 1024, 1536))
-    zero("dpad", W("BR", MW, 320))
-    for n in ("Et", "Vt"):
-        zero("dpad", W(n, 448, 512))
+    unpacker(0)
+    unpacker(1)
+    acp(W("OI"), W("OH"))
+    acp(W("OI", 1, 513, 4), W("OH", 3, 515, 4))
+    act(LM, L2, AF.Square, scale=-16.0, bias=224.0)
+    act(K5, L4, AF.Relu, scale=-LIFT * UNIT, bias=LIFT * UNIT)
+    act(LQ, L4, scale=-1.0, bias=LF)
+    act(LV, LF, scale=-1.0, bias=C - 1.0)
+    act(LR, LM, scale=-1.0)
+    act(W("lf", 54, 64), W("lk"), bias=LF)
+    act(W("lf", 36, 54), C16, scale=-1.0, bias=LV)
 
     def consts_later():
-        iota(W("OH", 1, 513, 4), [[0, 128]])
-        iota(W("ic"), [[int(UNIT), C]])
-        iota(W("Rs", 8, NJ), [[0, NJ - 8]])
-        iota(W("c9"), [[16, 2], [0, 9]], -16)
+        iota(W("r8"), [[0, NJ], [2, 8]], 1)
+        iota(W("TP", 288, 320), [[0, 32]])
+        for o in (W("Rs", FAR, NJ), W("P4", 0, 16), W("P4", 128, 144)):
+            dma("s", "dz", o, W("TP", 288, 288 + o[4] - o[3]))
+        iota(W("c9"), [[16, 2], [0, 9]], -16 - int(BIG) - 128)
+        iota(W("B8"), [[0, 144]], -100 * int(BIG))
         iota(W("cd"), [[4, C]], 4)
-        for k in range(2):
-            for base in (-64, 64):
-                o = W("cb", 1024 + k, 1536, 4)
-                asel(o, o, [[32, 4], [1000, 4], [16, 8]], A.not_equal, base - 1000 * k, -1, LIFT)
-        for c0, c1, pattern, base in ((0, 16, [[0, 8], [24, 2]], 3), (16, 32, [[0, 8], [-24, 2]], 12),
-                                      (32, 40, [[32, 4], [160, 2]], 0), (40, 48, [[2, 4], [10, 2]], 257), (48, 64, [[-16, 2], [32, 4], [-128, 2]], 144),
-                                      (64, 80, [[17, 2], [2, 4], [10, 2]], 240), (80, 96, [[-1, 2], [2, 4], [-8, 2]], 249)):
+        for c0, c1, pattern, base in ((0, 36, [[-1, 2], [2, 9], [20, 2]], S1 + 1), (36, 72, [[-1, 2], [2, 9], [20, 2]], S2 + 1), (72, 80, [[0, 8]], 0),
+                                      (80, 98, [[32, 9], [-T2, 2]], T2 + MARK), (98, 134, [[-1, 2], [2, 9], [-NJ, 2]], S1 + 1 + NJ),
+                                      (134, 160, [[2, 13], [-NJ, 2]], S2 + 1 + NJ)):
+            iota(W("KS", c0, c1), pattern, base)
+        for c0, c1, pattern, base in ((0, 8, [[32, 4], [160, 2]], 0), (8, 16, [[2, 4], [10, 2]], 257), (16, 32, [[-16, 2], [32, 4], [-128, 2]], 144),
+                                      (32, 48, [[17, 2], [2, 4], [10, 2]], 256), (48, 64, [[-1, 2], [2, 4], [-8, 2]], 265),
+                                      (64, 80, [[17, 2], [2, 4], [10, 2]], 272), (80, 96, [[-1, 2], [2, 4], [-8, 2]], 281), (96, 128, [[0, 32]], 0)):
             iota(W("KR", c0, c1), pattern, base)
         iota(W("r4"), [[0, 28], [4, 4]], 2)
-        iota(W("P4", 0, 16), [[0, 16]])
-        iota(W("P4", 128, 144), [[0, 16]])
-        iota(W("TP", 288, 320), [[0, 32]])
+        iota(W("BR", 0, 32), [[0, 32]], int(-MID * SMALL))
+        iota(W("ic"), [[int(UNIT), C]])
+        iota(W("c16"), [[16, 28]])
         iota(W("q4", 2 * K + 1, 2 * K + 2), [[0, 1]], int(LIFT * UNIT))
-        iota(W("qb", 1, 2 * K, 2), [[0, K]])
-
-    def consts_first():
-        ts(W("m16"), W("r16"), LF, A.is_equal)
-        act(W("B16"), W("r16"), AF.Sign)
-        for e in (7, 512, 518):
-            act(W("cb", e, e // 512 * 512 + 512, 8), W("e64", 64, 128), AF.Copy)
-        dma("s", "dwc", W("wq"), W("wc"), o8=True)
-        dma("s", "dws", W("wqs"), W("ws"))
-        dma("s", "dv", W("vb"), W("v"))
-
-    def consts_count():
-        ts(W("yl"), C16, LF, A.add)
-        quant("cq", CI, CI + 128, W("OH", 1, 513))
-        quant("cq", CI + 128, CS, W("OH", 0, 512))
-        ts(lrv, W("yl"), -1.0, A.mult, C - 1.0, A.add)
-        consts_later()
 
     def consts_rank():
-        act(W("zz"), W("r8"), AF.Sign, scale=-1.0, bias=L2)
-        act(W("yo"), W("ic"), AF.Relu, scale=1.0 / UNIT, bias=-1.0)
-        act(W("M8"), W("zz"), scale=5 * BIG, bias=4 * BIG)
-        act(LR, LM, scale=-1.0, bias=K2)
-        for b in range(4):
-            quant("cq", 128 * b, 128 * b + 128, W("OH", 3 - b, 515 - b))
-
-    def consts_rv():
-        act(W("Q4"), ind(W("yo"), W("rvl")), scale=-1.0, bias=C - 1 - MID)
-        act(W("B8"), W("r8"), scale=0.0, bias=-100 * BIG)
-        act(W("wrS"), W("neg", 0, MW), AF.Copy, scale=MID)
-        act(W("wrb"), ind(W("Q4"), lrv), AF.Copy)
-        for k in range(2):
-            for a in range(4):
-                g0 = (2 * a - 4) % 8
-                for r0, r1 in ((0, min(5, 8 - g0)), (min(5, 8 - g0), 5)):
-                    if r0 < r1:
-                        n = C if k == 0 else C - 1
-                        o = W("wrS", 1 + 16 * k, 1 + 16 * k + n, p0=32 * a + 8 * k + r0, p1=32 * a + 8 * k + r1)
-                        rows_to("s", "dwr", o, "wrb", (g0 + r0) % 8, (g0 + r0) % 8 + r1 - r0, n)
-
-    def consts_bounds():
-        turn(W("KT"), W("KR"))
-        ts(W("yi"), W("yl", 0, 8), -8.5, A.add, 1.0 / 18, A.mult)
-        act(W("yb", 0, 8), W("yl", 0, 8), scale=16.0, bias=W("KT", 0, 1))
-        act(W("yb", 8, 9), W("KT", 32, 33))
-        act(W("yb", 9, 11), W("c16", 1, 3), bias=W("KT", 64, 65))
-        ts(W("ya"), W("yi"), -289.0, A.mult)
+        act(W("M8"), W("r8"), scale=-BIG, bias=K2)
+        act(W("B8", 0, 144, 8), W("c9"), bias=LR)
+        act(W("Q4"), ind(W("cd"), W("rvl")), AF.Relu, scale=0.25, bias=-2.0)
+        act(W("wrb"), ind(W("Q4"), lrv), scale=-SMALL, bias=(C - 1 - MID) * SMALL)
+        acp(W("KR", 128, C), ind(W("KS"), lks))
+        for c in range(9):
+            dma("s", "dk", W("KT", c, c + 1), W("KR", 32 * c, 32 * c + 32, p1=4))
+        dma("s", "dle", W("le", 0, 16), W("gq", 0, 16), o8=True, a8=True)
+        dma("s", "dle", W("les", 0, 16), W("gqs", 0, 16))
 
     def consts_lists():
         act(W("w1"), W("r4"), AF.Sign, scale=-1.0, bias=L4)
-        act(K5, L4, AF.Relu, scale=-LIFT * UNIT, bias=LIFT * UNIT)
         act(LB, LQ, bias=3 * UNIT - 4)
         act(W("M4"), W("w1"), scale=(LIFT + 1) / 2 * UNIT, bias=(LIFT - 1) / 2 * UNIT)
         act(K6, L4, scale=-UNIT / 4, bias=LB)
@@ -368,11 +369,10 @@ def rank_program(g, core, T, topo):
 
     def consts_late():
         act(W("dm"), W("c16"), scale=-1.0, bias=K5)
-        act(W("lf", 52, 59), W("yl", 0, 7), scale=-1.0, bias=K - 1.0)
         cp(W("M5"), W("M4"))
         ts(W("M5", 3, K, 4), W("dm"), LF, A.subtract, -4.0 * C, A.add)
         act(W("OH"), W("OH"), AF.Copy, scale=2.0 ** -6)
-        cp(lrq, W("lf", 52, 59))
+        ts(lrq, W("lf", 36, 43), K - float(C), A.add)
         quant("qv", 0, 128, W("vb"))
         for b in range(4):
             quant("cq", CZ + 128 * b, CZ + 128 * b + 128, W("OH", 3 - b, 515 - b))
@@ -386,165 +386,162 @@ def rank_program(g, core, T, topo):
         rlc[0] += ne
 
     for t in range(ROUNDS):
-        quant("qx", 0, C, W("x0") if t == 0 else W("X", 0, 4 * C))
-        if t == 0:
-            consts_first()
+        hb2 = (2, 7)
+        for h in range(2):
+            quant("qx", HC * h, HC * (h + 1), W("x0" if t == 0 else "X", 4 * HC * h, 4 * HC * (h + 1)))
+            mm(hb2[h], "uo", 0, "qx", HC * h, HC)
+        mm(3, "qu", 0, "qx", 0, C)
         mm(0, "uo", 0, "qx", 0, C)
-        mm(1, "um", 0, "qx", 0, C)
-        mm(7, "uo", 0, "qx", 0, C)
 
-        def unpack():
-            for b in range(4):
-                mm(2 + b, "cq", 128 * b, "qx", 0, C)
-
-        def state():
-            for b in range(4):
-                act(W("X", b, 4 * C, 4), bk(2 + b, 0, C), AF.Copy, scale=-1.0)
+        def marks():
+            act(W("sg"), bk(3, 0, C), AF.Sign, bias=-TINY)
         if t:
-            unpack()
-        So = bk(0, 0, C)
-        tt(W("z"), So, W("m16"), A.mult)
-        act(W("sg"), bk(1, 0, C), AF.Sign, bias=-TINY)
-        scan(W("zs"), W("B16"), W("z"), 0.0, A.mult, A.add)
-        if t == 0:
-            act(W("OE"), ind(W("zs"), lOE), AF.Copy)
-            consts_count()
+            marks()
         else:
-            act(W("OE", 64, C), ind(W("zs"), W("lu", 20, 34)), AF.Copy)
-            scan(W("Vr"), W("cd"), W("sg"), 0.0, A.max, A.mult)
-            cp(W("OE", 0, 64), ind(W("zs"), W("lu", 16, 20)))
+            quant("cq", CI, CI + 128, W("OI", 1, 513))
+        for h in range(2):
+            tt(W("z", HC * h, HC * (h + 1)), bk(hb2[h], 0, HC), W("m16", HC * h, HC * (h + 1)), A.subtract)
+        for c0, c1 in ((128, C), (0, 128)):
+            scan(W("zs", c0, c1), W("B16", c0, c1), W("z", c0, c1), -HUGE, A.min, A.max)
+            acp(W("OE", c0, c1), ind(W("zs", c0, c1), W("lu", NJ, NJ + (c1 - c0) // 16)))
+        tt(lane(0, 0, C), bk(0, 0, C), W("zs"), A.is_le)
+        if t == 0:
+            quant("cq", CI + 128, CZ, W("OI", 0, 512))
+            quant("cq", CC, CI, W("cb"))
+            consts_later()
 
         def far(k):
             o = 8 * k * (k - 1)
-            act(W("rl", o, o + 16 * k), bk(7, C - 16 * k, C), AF.Sign, scale=-1.0, bias=W("zs", 16 * (8 - k) + 15, 16 * (8 - k) + 16))
+            act(W("rl", o, o + 16 * k), bk(7, HC - 16 * k, HC), AF.Sign, scale=-1.0, bias=W("zs", 16 * (FAR - k) + 15, 16 * (FAR - k) + 16))
 
         def won(k):
             o = 8 * k * (k - 1)
-            act(lane(k, C - 16 * k, C), W("rl", o, o + 16 * k), AF.Sign, bias=1.0, accum=W("Rs", 8 - k, 9 - k))
-
-        def chunk(ch):
-            o0, end = PLANE[ch[0]][0], PLANE[ch[-1]][0] + 144
-            if t == 0 and ch[0] != "lt":
-                o0 -= 8 * ch[0]
-            quant("gq", o0, end, W("G", 4 * o0, 4 * end))
-            if ch[0] != "lt":
-                for k in ch:
-                    mm(1, "cq", CI + 128 * PLANE[k][1], "gq", PLANE[k][0] - 8 * k, 144, start=(k == 9), stop=(k == 1))
-            for k in ch:
-                if PLANE[k][1] == 0:
-                    mm(6, "cq", CD if k == "lt" else CC, "gq", PLANE[k][0], 144, start=(k == 9), stop=(k == "lt"))
-        far(8)
-        for k in range(8, 0, -1):
-            if k > 1:
-                far(k - 1)
+            join("jg%d" % (k - 1 + k % 2))
+            act(lane(k, C - 16 * k, C), W("rl", o, o + 16 * k), AF.Sign, bias=1.0, accum=W("Rs", FAR - k, FAR + 1 - k))
+        far(1)
+        for k in range(1, FAR + 1):
+            if k < FAR:
+                far(k + 1)
             won(k)
-        for n, ch in enumerate(CHUNKS[:-1]):
+        if t == 0:
+            marks()
+        for ch in CHUNKS:
             for k in ch:
-                tt(lane(k, 0, C - 16 * k), bk(0, 0, C - 16 * k), W("OE", 16 * k, C), A.is_lt)
-            if t == 0 and n == 0:
-                quant("cq", CC, CI, W("cb", 0, 1024))
-            if t == 0 and n == 2:
-                consts_rank()
-                consts_rv()
-            if n:
-                chunk(CHUNKS[n - 1])
-        tt(lane("lt", 0, C), So, W("OE"), A.is_lt)
-        chunk(CHUNKS[-2])
-        tt(lane("eq", 0, C), So, W("OE"), A.is_equal)
-        chunk(CHUNKS[-1])
+                if 0 < k < 9:
+                    join("jg%d" % ch[0])
+                if k:
+                    tt(lane(k, 0, C - 16 * k), bk(0, 0, C - 16 * k), W("OE", 16 * k, C), A.is_lt)
+            if t == 0 and ch[0] > 3:
+                unpacker(ch[0] // 2)
+                cp(*((W("rvl"), W("rvt")) if ch[0] == 5 else (W("lu", 36, 64), W("lf", 36, 64))))
+            o0, end = PLANE[ch[0]][0] - (0 if t else 8 * ch[1]), PLANE[ch[0]][0] + 144
+            quant("gq", o0, end, W("G", 4 * o0, 4 * end))
+            for k in ch:
+                mm(1, "cq", CI + 128 * PLANE[k][1], "gq", PLANE[k][0] - 8 * k, 144, start=(k == 0), stop=(k == 8))
+            if ch[1] == 8:
+                join("jn")
+            mm(6, "cq", CC, "gq", PLANE[ch[0]][0], 144, start=(ch[0] == 0), stop=(ch[1] == 8))
+        for b in range(4):
+            mm(2 + b, "cq", CE + 128 * b, "qx", 0, C)
         if t == 0:
-            ts(W("B8", 0, 144, 8), W("c9"), LM, A.subtract)
-            scan(W("Vr"), W("cd"), W("sg"), 0.0, A.max, A.mult)
+            consts_rank()
+            consts_lists()
+        scan(W("Vr"), W("cd"), W("sg"), 0.0, A.max, A.mult)
         scan(W("zz"), W("B8"), bk(1, 0, 144), -100 * BIG, A.max, A.add)
-        if t == 0:
-            unpack()
-        state()
+        join("jn")
         tt(W("M8", 7, 144, 8), W("Rs"), W("zz", 7, 144, 8), A.subtract)
         scan(W("zz"), bk(6, 0, 144), W("M8"), 4 * BIG, A.min, A.add)
-        ts(W("rkl"), W("zz", 7, 144, 8), LR, A.add)
-        if t == 0:
-            quant("cq", CS, CZ, W("cb", 1024, 1536))
+        ts(W("rkl"), W("zz", 7, 144, 8), LF, A.add, -BIG, A.add)
         scatter(W("PL"), W("rkl"), W("Vr"))
-        ts(W("MT", 4, 4 * C + 4, 4), W("PL"), 0.0, A.is_gt, -0.5, A.add)
-        act(W("MT", 69, 4 * MW, 4), W("PL", 0, C - 1), AF.Sign)
+
+        def state(b):
+            act(W("X", b, 4 * C, 4), bk(2 + b, 0, C), AF.Copy, scale=-1.0)
+        for b in range(3 if t else 0):
+            state(b)
         act(W("ab"), W("PL"), AF.Abs)
-        quant("mq", 0, MW, W("MT"))
-        mm(1, "cq", CS, "mq", 0, MW)
+        for b in range(3, 4) if t else range(3):
+            state(b)
+        scan(W("am"), W("PL"), W("wrb"), -MID * SMALL, A.max, A.min)
+        scan(W("BR", 17, 17 + C), W("am"), W("am"), -MID * SMALL, A.max, A.max)
+        turn(W("TR", 0, T2), W("BR", 16, 16 + C))
+        turn(W("TR", T2, S1), W("BR"))
+        for p in (0, 32, 64, 96):
+            across(acp, "TR", S1, S1, p, 32, MARK)
         if t == 0:
-            consts_bounds()
-            consts_lists()
+            cp(W("lu", 72, 81), W("KT", 0, 9))
+        scan(W("TG"), W("ic"), W("ab"), 0.0, A.max, A.add)
+        for p in (0, 64):
+            across(cp, "TR", S2, S1, p, 64, MARK)
+        if t == 0:
+            state(3)
+        ts(W("LL"), ind(W("TR"), lsel), 1.0 / SMALL, A.mult, MID, A.add)
 
         def fixed():
             scan(W("wA"), W("ab", 1, 2 * K, 2), W("M4"), LIFT * UNIT, A.min, A.add)
             ts(W("lA"), W("wA", 3, K, 4), LA, A.add)
-        scan(W("TG"), W("ic"), W("ab"), 0.0, A.max, A.add)
-        tt(W("am"), bk(1, 0, MW), W("wrS"), A.min)
-        if t == 0:
-            tt(W("yb", 0, 8), W("yb", 0, 8), W("ya"), A.add)
-        scan(W("BR", 0, MW), W("am"), W("am"), -MID, A.max, A.max)
-        if t == 0:
-            cp(W("lu", 60, 71), W("yb", 0, 11))
         odd = {n: (n, 0, 128, 1, 2 * K, 2) for n in ("TG", "Q1", "Q2", "Q3", "Q4")}
-        turn(W("TR"), W("BR"))
-        ts(W("LL"), ind(W("TR"), lsel), MID, A.add)
         for d in range(1, 5):
-            H = HV[d - 1]
+            H, end = HV[d - 1], NJ if d < 4 else EARLY
             src, o = W("TG") if d == 1 else W("Q%d" % (d - 1)), NJ * (d - 1)
+            join("jq%d" % d, 2)
             cp(W("Q%d" % d, 0, 16 * H), ind(src, W("LL", o, o + H)))
-            if H < NJ:
-                act(W("Q%d" % d, 16 * H, C), ind(src, W("LL", o + H, o + NJ)), AF.Copy)
+            acp(W("Q%d" % d, 16 * H, 16 * end), ind(src, W("LL", o + H, o + end)))
             if d == 2:
                 scan(W("P1"), odd["TG"], odd["Q1"], 0.0, A.max, A.max)
             if d == 3:
                 scan(W("P2"), W("P1"), odd["Q2"], 0.0, A.max, A.max)
             if d == 4:
+                join("jq4")
                 scan(W("P1"), W("P2"), odd["Q3"], 0.0, A.max, A.max)
             if d == 1:
                 fixed()
+        acp(W("A5"), ind(W("X", 0, 4 * C), W("lA")))
         P4 = W("P4", 16, 16 + K)
         scan(P4, W("P1"), odd["Q4"], 0.0, A.max, A.max)
         turn(W("TP", 0, 128), W("P4", 16, 144))
         turn(W("TP", 128, 256), W("P4", 0, 128))
+        for n, p in enumerate((0, 32, 64, 96)):
+            across(acp if n < SP else cp, "TP", 256, 256, p, 32)
         for p in (0, 64):
-            cp(W("TP", 272, 288, p0=p, p1=p + 64), W("TP", 0, 256, 16, p0=64 - p, p1=128 - p))
-        for p in (32, 64, 96):
-            act(W("TP", 256, 272, p0=p, p1=p + 32), W("TP", 0, 256, 16, p0=p - 32, p1=p), AF.Copy)
-        cp(W("TP", 256, 272, p1=32), W("TP", 0, 256, 16, p0=96))
+            across(cp, "TP", 272, 256, p, 64)
+        acp(W("Q4", 16 * EARLY, C), ind(W("Q3"), W("LL", 3 * NJ + EARLY, 4 * NJ)))
         o = PW * t
         pl, plo = W("pls", o, o + 40), W("pll", o, o + 40)
 
         def lists():
             ts(W("pls", o, o + PW), ind(W("TP"), lsp), 1.0 / UNIT, A.mult)
             send(plo, pl, ap, "ap%d" % t)
-        act(W("A5"), ind(W("X", 0, 4 * C), W("lA")), AF.Copy)
-        columns(P4, W("wE"), W("qi"), W("qj"), W("lE"), lists)
+        columns(P4, W("wE"), W("qi"), W("qj"), W("lE"), [lists])
         tt(W("Et", 0, 448), ind(W("X", 0, 4 * C), W("lE")), W("A5"), A.add)
         quant("eq", 128 * t, 128 * t + 128, W("Et"))
-        e, eo = W("eq", 128 * t, 128 * t + 128), W("le", 128 * t, 128 * t + 128)
-        es, eso = W("eqs", 128 * t, 128 * t + 128), W("les", 128 * t, 128 * t + 128)
+        e, eo = W("eq", 128 * t, 128 * t + K), W("le", 16 + K * t, 16 + K * (t + 1))
+        es, eso = W("eqs", 128 * t, 128 * t + K), W("les", 16 + K * t, 16 + K * (t + 1))
         send(eo, e, by, "ae%d" % t)
         send(eso, es, ap, "ae%d" % t)
         if t == 0:
             consts_late()
         arrive([plo], "ap%d" % t, np_)
         arrive([eo, eso], "ae%d" % t, 2 * np_)
-        act(W("qa", 1, 2 * K, 2), ind(W("Q3"), W("pll", o + 24, o + 31)), AF.Copy)
-        act(W("qb", 0, 2 * K, 2), ind(W("Q4"), W("pll", o + 32, o + 39)), AF.Copy)
+        acp(W("q0"), ind(W("Q1"), W("pll", o + 8, o + 15)))
+        join("jl", 4)
+        acp(W("qa", 1, 2 * K, 2), ind(W("Q3"), W("pll", o + 24, o + 31)))
+        acp(W("qb", 0, 2 * K, 2), ind(W("Q4"), W("pll", o + 32, o + 39)))
+        cp(W("qb", 1, 2 * K, 2), ind(W("TG"), W("pll", o, o + 7)))
+        tt(W("qa", 0, 2 * K, 2), ind(W("Q2"), W("pll", o + 16, o + 23)), W("q0"), A.max)
         for b in range(4):
-            mm(2 + b, "cq", CZ + 128 * b, "le", 128 * t, 128)
-        cp(W("q0"), ind(W("Q1"), W("pll", o + 8, o + 15)))
-        tt(W("q1"), ind(W("TG"), W("pll", o, o + 7)), W("q0"), A.max)
-        tt(W("qa", 0, 2 * K, 2), ind(W("Q2"), W("pll", o + 16, o + 23)), W("q1"), A.max)
+            if b == 0:
+                join("jv")
+            mm(2 + b, "cq", CZ + 128 * b, "le", K * t, 128)
         scan(W("q4", 0, 2 * K), W("qa"), W("qb"), 0.0, A.max, A.max)
-        columns(W("q4", 1, 2 * K, 2), W("wE"), W("qi"), W("qj"), W("lQ"),
-                lambda: scan(W("w1"), W("q4", 3, 2 * K + 2, 2), W("M5"), LIFT * UNIT, A.min, A.add))
-        ts(W("DE", 0, 256), ind(W("X", 0, 4 * C), W("lQ", 0, 16)), 2.0 ** -5, A.mult)
-        act(W("DE", 256, 448), ind(W("X", 0, 4 * C), W("lQ", 16, 28)), AF.Copy, scale=2.0 ** -5)
+        columns(W("q4", 1, 2 * K, 2), W("wE"), W("qi"), W("qj"), W("lQ"))
+        join("jv", 2)
+        ts(W("DE", 0, 16 * DV), ind(W("X", 0, 4 * C), W("lQ", 0, DV)), 2.0 ** -5, A.mult)
+        act(W("DE", 16 * DV, 448), ind(W("X", 0, 4 * C), W("lQ", DV, 28)), AF.Copy, scale=2.0 ** -5)
+        scan(W("w1"), W("q4", 3, 2 * K + 2, 2), W("M5"), LIFT * UNIT, A.min, A.add)
+        join("jw")
         act(W("FQ"), W("DE"), AF.Copy, scale=2.0 ** 5)
-        tt(W("eqn"), W("wE", 3, K, 4), W("w1", 3, K, 4), A.subtract)
-        tt(W("sel"), W("qj"), W("eqn"), A.max)
         for b in range(4):
-            tt(W("Vt", b, 448, 4), W("DE", b, 448, 4), bk(2 + b, 0, K), A.subtract)
+            tt(W("Vt", b, 448, 4), W("DE", b, 448, 4), bk(2 + b, 16, 16 + K), A.subtract)
         if t == ROUNDS - 1:
             act(W("q0"), W("q4", 1, 2 * K, 2), scale=-1.0 / UNIT, bias=WHOLE + C - 1)
             act(W("lqf"), ind(W("q0"), lrq), bias=-WHOLE)
@@ -552,19 +549,28 @@ def rank_program(g, core, T, topo):
         quant("vq", 0, 128, W("Vt"))
         hb = (0, 1, 6, 7)
         for b in range(4):
+            if b == 0:
+                join("jw")
             mm(hb[b], "wq", 128 * b, "vq", 0, 128)
-        cp(W("lX"), W("sel"))
+        tt(W("eqn"), W("wE", 3, K, 4), W("w1", 3, K, 4), A.subtract)
         for b in range(4):
+            join("jx")
             tt(W("CV", b, 448, 4), bk(hb[b], 0, K), W("FQ", b, 448, 4), A.add)
+            if b == 0:
+                tt(W("sel"), W("qj"), W("eqn"), A.max)
+            if b == 1:
+                join("jx")
+                cp(W("lX"), W("sel"))
         scatter(W("X"), W("lX"), W("CV"))
-    quant("qx", 0, C, W("X", 0, 4 * C))
-    HY = 160
-    mm(0, "qv", 0, "qx", 0, HY)
-    mm(1, "qv", 0, "qx", HY, C - HY)
-    emit("s", lambda: g.sync.dma_start(T.oc[:, :], by(W("qx"))), [], [W("qx")], dma="doc")
+    for h in range(2):
+        quant("qx", HC * h, HC * (h + 1), W("X", 4 * HC * h, 4 * HC * (h + 1)))
+        mm(h, "qv", 0, "qx", HC * h, HC)
+    for h in range(2):
+        half = W("yo", HC * h, HC * (h + 1))
+        (acp, cp)[h](half, bk(h, 0, HC))
+        dma("a", "dy", W("y", HC * h, HC * (h + 1)), half)
+        if h == 0:
+            emit("s", lambda: g.sync.dma_start(T.oc[:, :], by(W("qx"))), [], [W("qx")], dma="doc")
     for k in range(4):
         emit("s", lambda: g.sync.dma_start(T.osc[4 * k:4 * k + 4, :], T.qxs[32 * k:32 * k + 4, 0:C]), [], [W("qxs")], dma="doc")
-    cp(W("yo", 0, HY), bk(0, 0, HY))
-    act(W("yo", HY, C), bk(1, 0, C - HY), AF.Copy)
-    emit("a", lambda: g.scalar.dma_start(T.y[:, :], T.yo[:, :]), [], [W("yo")], dma="dy")
     finish([("rl", rlc[0])] + [("ap%d" % t, np_) for t in range(ROUNDS)] + [("ae%d" % t, 2 * np_) for t in range(ROUNDS)])

@@ -1,4 +1,4 @@
-from concourse.mybir import dt, AluOpType, ActivationFunctionType
+from concourse.mybir import dt, AluOpType, AxisListType, ActivationFunctionType
 
 C, K, ROUNDS = 288, 112, 3
 NJ = C // 16
@@ -15,9 +15,10 @@ HC = C // 2
 T2, S1, S2, TW = C, 2 * C + 32, 2 * C + 72, 2 * C + 128
 PW = 48
 CODE, F32, BF, I32, U16, U8 = "float8_e4m3fn_x4", "float32", "bfloat16", "int32", "uint16", "uint8"
-HV = (4, 6, 6, 6)
+HV = (4, 6, 6, 4)
 DV = 12
 SP = 3
+NEAR = (0, 1, 1)
 FAR = 8
 EARLY = 14
 CHUNKS = [(0, 9), (1, 2), (3, 4), (5, 6), (7, 8)]
@@ -40,7 +41,7 @@ def _sb(dtype, **names):
 _sb(BF, x0=4 * C, X=1600, ub=512, vb=512, neg=528, OH=528, OI=528, cb=512, G=4 * GW, m16=C, B16=C, e64=72,
     A5=448, Et=512, Vt=512, DE=448, CV=448, wrb=C, am=C, BR=320, TR=TW)
 _sb(F32, r4=K, r8=144, pflt=24, ic=C, cd=C, dm=28, c16=28, lk=10, lf=72, KS=160, KR=C, KT=12, TP=320,
-    z=C, zs=C, zz=144, B8=144, M4=K, M5=K, M8=144, OE=C, sg=C, Vr=C, Rs=NJ, PL=C, ab=C, rl=2 * C, TG=C, c9=NJ,
+    z=C, zs=C, zz=144, zc=144, rk=NJ, B8=144, M4=K, M5=K, M8=144, OE=C, sg=C, Vr=C, Rs=NJ, PL=C, ab=C, rl=2 * C, TG=C,
     Q1=C, Q2=C, Q3=C, Q4=C, P1=K, P2=K, P4=144, w1=K, wA=K, wE=K, FQ=448, eqn=28, sel=28, lqf=K, q0=K, qa=2 * K, qb=2 * K,
     q4=2 * K + 2, yo=C)
 _sb(I32, rvt=NJ, pint=8, qi=28, qj=28)
@@ -52,7 +53,7 @@ for _n, _w in [("qx", C), ("qu", 128), ("qv", 128), ("uo", 128), ("wq", 512), ("
 
 QS = {"v": "qsv", "a": "qsa", "t": "qst", "g": "qsg"}
 DS = ["dx", "du", "dv", "drv", "dwc", "dws", "dG", "dpad", "dcb", "dz", "dk", "dle", "dlq", "doc", "dy"]
-JS = {"jg1": 4, "jg3": 4, "jg5": 4, "jg7": 4, "jn": 2, "jb": 6, "jq1": 2, "jq2": 2, "jq3": 2, "jq4": 3, "jp": 6, "jl": 4, "jv": 3, "jw": 2, "jx": 5}
+JS = {"jg1": 4, "jg3": 4, "jg5": 4, "jg7": 4, "jb": 6, "jq1": 2, "jq2": 2, "jq3": 2, "jq4": 3, "jp": 6, "jl": 4, "jv": 3, "jw": 2, "jx": 5}
 SEMAPHORES = list(QS.values()) + DS + list(JS) + ["rl"] + ["ap%d" % _t for _t in range(ROUNDS)] + ["ae%d" % _t for _t in range(ROUNDS)]
 
 
@@ -200,6 +201,9 @@ def rank_program(g, core, T, topo):
     def scan(out, d0, d1, init, op0, op1):
         emit("v", lambda: g.vector.tensor_tensor_scan(ap(out), ap(d0), ap(d1), init, op0, op1), [out], [d0, d1])
 
+    def total(out, a):
+        emit("v", lambda: g.vector.tensor_reduce(ap(out), ap(a), AxisListType.X, A.add), [out], [a])
+
     def turn(out, a):
         emit("v", lambda: g.vector.transpose(ap(out), ap(a)), [out], [a])
 
@@ -295,6 +299,7 @@ def rank_program(g, core, T, topo):
     ts(l16, W("neg", 0, NJ), 0.0, A.mult, LF, A.add)
     fill(W("B16", 0, C, 16), -HUGE)
     fill(W("cb"), 0.0)
+    fill(W("OI"), 0.0)
     zero(pad(9))
     zero(W("G", 4 * PLANE[9][0] + C, 4 * PLANE[1][0]))
     act(LH, LF, scale=-HUGE)
@@ -313,16 +318,16 @@ def rank_program(g, core, T, topo):
     def unpacker(b):
         quant("cq", CE + 128 * b, CE + 128 * b + 128, W("OH", 3 - b, 515 - b))
     quant("qu", 0, 128, W("ub"))
-    pick("uo", sO)
     unpacker(0)
+    pick("uo", sO)
     unpacker(1)
-    acp(W("OI"), W("OH"))
-    acp(W("OI", 1, 513, 4), W("OH", 3, 515, 4))
+    for e in (1, 3):
+        acp(W("OI", e, 512 + e, 4), W("OH", 3, 515, 4))
     act(LM, L2, AF.Square, scale=-16.0, bias=224.0)
     act(K5, L4, AF.Relu, scale=-LIFT * UNIT, bias=LIFT * UNIT)
     act(LQ, L4, scale=-1.0, bias=LF)
     act(LV, LF, scale=-1.0, bias=C - 1.0)
-    act(LR, LM, scale=-1.0)
+    act(LR, LM, bias=BIG)
     act(W("lf", 54, 64), W("lk"), bias=LF)
     act(W("lf", 36, 54), C16, scale=-1.0, bias=LV)
 
@@ -331,8 +336,7 @@ def rank_program(g, core, T, topo):
         iota(W("TP", 288, 320), [[0, 32]])
         for o in (W("Rs", FAR, NJ), W("P4", 0, 16), W("P4", 128, 144)):
             dma("s", "dz", o, W("TP", 288, 288 + o[4] - o[3]))
-        iota(W("c9"), [[16, 2], [0, 9]], -16 - int(BIG) - 128)
-        iota(W("B8"), [[0, 144]], -100 * int(BIG))
+        iota(W("B8"), [[16, 2], [0, 9], [-4096, 8]], -16 - 128)
         iota(W("cd"), [[4, C]], 4)
         for c0, c1, pattern, base in ((0, 36, [[-1, 2], [2, 9], [20, 2]], S1 + 1), (36, 72, [[-1, 2], [2, 9], [20, 2]], S2 + 1), (72, 80, [[0, 8]], 0),
                                       (80, 98, [[32, 9], [-T2, 2]], T2 + MARK), (98, 134, [[-1, 2], [2, 9], [-NJ, 2]], S1 + 1 + NJ),
@@ -349,8 +353,6 @@ def rank_program(g, core, T, topo):
         iota(W("q4", 2 * K + 1, 2 * K + 2), [[0, 1]], int(LIFT * UNIT))
 
     def consts_rank():
-        act(W("M8"), W("r8"), scale=-BIG, bias=K2)
-        act(W("B8", 0, 144, 8), W("c9"), bias=LR)
         act(W("Q4"), ind(W("cd"), W("rvl")), AF.Relu, scale=0.25, bias=-2.0)
         act(W("wrb"), ind(W("Q4"), lrv), scale=-SMALL, bias=(C - 1 - MID) * SMALL)
         acp(W("KR", 128, C), ind(W("KS"), lks))
@@ -377,37 +379,39 @@ def rank_program(g, core, T, topo):
         for b in range(4):
             quant("cq", CZ + 128 * b, CZ + 128 * b + 128, W("OH", 3 - b, 515 - b))
 
-    ne, np_ = len(topo.engines(core, nxt)), len(topo.engines(prv, core))
     rid, pid = topo.addr(nxt, core)
     rlc = [0]
+    few = min(len(topo.engines(a, b)) for a, b in zip(T.cores, T.cores[1:] + T.cores[:1]))
+    np_ = len(topo.engines(prv, core))
 
-    def send(out, src, view, sem):
-        emit("g", lambda: g.remote_dma(view(out), view(src), T.sem[sem], T.sem.rl, pid, rid, topo.mask(core, nxt)), [], [src], remote=True)
-        rlc[0] += ne
+    def send(out, src, view, sem, n=None):
+        engines = topo.engines(core, nxt)[:n]
+        emit("g", lambda: g.remote_dma(view(out), view(src), T.sem[sem], T.sem.rl, pid, rid, sum(1 << e for e in engines)), [], [src], remote=True)
+        rlc[0] += len(engines)
 
     for t in range(ROUNDS):
         hb2 = (2, 7)
-        for h in range(2):
+        for h in (1, 0):
             quant("qx", HC * h, HC * (h + 1), W("x0" if t == 0 else "X", 4 * HC * h, 4 * HC * (h + 1)))
             mm(hb2[h], "uo", 0, "qx", HC * h, HC)
-        mm(3, "qu", 0, "qx", 0, C)
+        mm(4, "qu", 0, "qx", HC, HC)
         mm(0, "uo", 0, "qx", 0, C)
+        mm(3, "qu", 0, "qx", 0, HC)
 
-        def marks():
-            act(W("sg"), bk(3, 0, C), AF.Sign, bias=-TINY)
-        if t:
-            marks()
-        else:
+        def marks(h):
+            act(W("sg", HC * h, HC * (h + 1)), bk(3 + h, 0, HC), AF.Sign, bias=-TINY)
+        marks(1)
+        if t == 0:
             quant("cq", CI, CI + 128, W("OI", 1, 513))
-        for h in range(2):
+        for h in (1, 0):
             tt(W("z", HC * h, HC * (h + 1)), bk(hb2[h], 0, HC), W("m16", HC * h, HC * (h + 1)), A.subtract)
-        for c0, c1 in ((128, C), (0, 128)):
+        for c0, c1 in ((HC, C), (0, HC)):
             scan(W("zs", c0, c1), W("B16", c0, c1), W("z", c0, c1), -HUGE, A.min, A.max)
-            acp(W("OE", c0, c1), ind(W("zs", c0, c1), W("lu", NJ, NJ + (c1 - c0) // 16)))
-        tt(lane(0, 0, C), bk(0, 0, C), W("zs"), A.is_le)
+            acp(W("OE", c0, c1), ind(W("zs", c0, c1), W("lu", NJ, NJ + HC // 16)))
+        for c0, c1 in ((HC, C), (0, HC)):
+            tt(lane(0, c0, c1), bk(0, c0, c1), W("zs", c0, c1), A.is_le)
         if t == 0:
             quant("cq", CI + 128, CZ, W("OI", 0, 512))
-            quant("cq", CC, CI, W("cb"))
             consts_later()
 
         def far(k):
@@ -418,40 +422,55 @@ def rank_program(g, core, T, topo):
             o = 8 * k * (k - 1)
             join("jg%d" % (k - 1 + k % 2))
             act(lane(k, C - 16 * k, C), W("rl", o, o + 16 * k), AF.Sign, bias=1.0, accum=W("Rs", FAR - k, FAR + 1 - k))
-        far(1)
-        for k in range(1, FAR + 1):
+        far(NEAR[t] + 1)
+        for k in range(NEAR[t] + 1, FAR + 1):
             if k < FAR:
                 far(k + 1)
             won(k)
-        if t == 0:
-            marks()
-        for ch in CHUNKS:
-            for k in ch:
-                if 0 < k < 9:
-                    join("jg%d" % ch[0])
-                if k:
-                    tt(lane(k, 0, C - 16 * k), bk(0, 0, C - 16 * k), W("OE", 16 * k, C), A.is_lt)
-            if t == 0 and ch[0] > 3:
-                unpacker(ch[0] // 2)
-                cp(*((W("rvl"), W("rvt")) if ch[0] == 5 else (W("lu", 36, 64), W("lf", 36, 64))))
-            o0, end = PLANE[ch[0]][0] - (0 if t else 8 * ch[1]), PLANE[ch[0]][0] + 144
+
+        def plane(k):
+            pair = "jg%d" % (k - 1 + k % 2)
+            if k <= NEAR[t]:
+                join(pair)
+                ts(lane(k, C - 16 * k, C), bk(0, C - 16 * k, C), W("zs", 16 * (FAR - k) + 15, 16 * (FAR - k) + 16), A.is_le)
+            if k < 9:
+                join(pair)
+            tt(lane(k, 0, C - 16 * k), bk(0, 0, C - 16 * k), W("OE", 16 * k, C), A.is_lt)
+
+        def count(chs):
+            for k in range(1, NEAR[t] + 1):
+                if (k - 1 + k % 2, k + k % 2) in chs:
+                    total(W("Rs", FAR - k, FAR + 1 - k), lane(k, C - 16 * k, C))
+            o0, end = PLANE[chs[0][0]][0] - (0 if t else 8 * chs[0][1]), PLANE[chs[-1][0]][0] + 144
             quant("gq", o0, end, W("G", 4 * o0, 4 * end))
-            for k in ch:
-                mm(1, "cq", CI + 128 * PLANE[k][1], "gq", PLANE[k][0] - 8 * k, 144, start=(k == 0), stop=(k == 8))
-            if ch[1] == 8:
-                join("jn")
-            mm(6, "cq", CC, "gq", PLANE[ch[0]][0], 144, start=(ch[0] == 0), stop=(ch[1] == 8))
-        for b in range(4):
-            mm(2 + b, "cq", CE + 128 * b, "qx", 0, C)
+            for ch in chs:
+                for k in ch:
+                    mm(1, "cq", CI + 128 * PLANE[k][1], "gq", PLANE[k][0] - 8 * k, 144, start=(k == 0), stop=(k == 8))
+                mm(6, "cq", CC, "gq", PLANE[ch[0]][0], 144, start=(ch[0] == 0), stop=(ch[1] == 8))
+        for k in (9, 1, 2, 3, 4, 5, 6, 7, 8):
+            plane(k)
+            if t == 0 and k == 3:
+                quant("cq", CC, CI, W("cb"))
+            if k in (3, 5, 7):
+                count(CHUNKS[:2] if k == 3 else [CHUNKS[k // 2]])
+            if t == 0 and k in (6, 8):
+                unpacker(k // 2 - 1)
+                cp(*((W("rvl"), W("rvt")) if k == 6 else (W("lu", 36, 64), W("lf", 36, 64))))
+        count(CHUNKS[-1:])
+        if t == 0:
+            act(W("M8"), W("r8"), scale=-BIG, bias=K2)
+        marks(0)
+        act(W("M8", 7, 144, 8), W("Rs"), bias=LR)
         if t == 0:
             consts_rank()
             consts_lists()
+        for b in range(4):
+            mm(2 + b, "cq", CE + 128 * b, "qx", 0, C)
         scan(W("Vr"), W("cd"), W("sg"), 0.0, A.max, A.mult)
         scan(W("zz"), W("B8"), bk(1, 0, 144), -100 * BIG, A.max, A.add)
-        join("jn")
-        tt(W("M8", 7, 144, 8), W("Rs"), W("zz", 7, 144, 8), A.subtract)
-        scan(W("zz"), bk(6, 0, 144), W("M8"), 4 * BIG, A.min, A.add)
-        ts(W("rkl"), W("zz", 7, 144, 8), LF, A.add, -BIG, A.add)
+        scan(W("zc"), bk(6, 0, 144), W("M8"), 4 * BIG, A.min, A.add)
+        tt(W("rk"), W("zc", 7, 144, 8), W("zz", 7, 144, 8), A.subtract)
+        ts(W("rkl"), W("rk"), LF, A.add, -BIG, A.add)
         scatter(W("PL"), W("rkl"), W("Vr"))
 
         def state(b):
@@ -510,7 +529,7 @@ def rank_program(g, core, T, topo):
 
         def lists():
             ts(W("pls", o, o + PW), ind(W("TP"), lsp), 1.0 / UNIT, A.mult)
-            send(plo, pl, ap, "ap%d" % t)
+            send(plo, pl, ap, "ap%d" % t, None if t else few)
         columns(P4, W("wE"), W("qi"), W("qj"), W("lE"), [lists])
         tt(W("Et", 0, 448), ind(W("X", 0, 4 * C), W("lE")), W("A5"), A.add)
         quant("eq", 128 * t, 128 * t + 128, W("Et"))
@@ -520,9 +539,9 @@ def rank_program(g, core, T, topo):
         send(eso, es, ap, "ae%d" % t)
         if t == 0:
             consts_late()
-        arrive([plo], "ap%d" % t, np_)
+        arrive([plo], "ap%d" % t, np_ if t else few)
         arrive([eo, eso], "ae%d" % t, 2 * np_)
-        acp(W("q0"), ind(W("Q1"), W("pll", o + 8, o + 15)))
+        cp(W("q0"), ind(W("Q1"), W("pll", o + 8, o + 15)))
         join("jl", 4)
         acp(W("qa", 1, 2 * K, 2), ind(W("Q3"), W("pll", o + 24, o + 31)))
         acp(W("qb", 0, 2 * K, 2), ind(W("Q4"), W("pll", o + 32, o + 39)))
@@ -553,24 +572,22 @@ def rank_program(g, core, T, topo):
                 join("jw")
             mm(hb[b], "wq", 128 * b, "vq", 0, 128)
         tt(W("eqn"), W("wE", 3, K, 4), W("w1", 3, K, 4), A.subtract)
+        tt(W("sel"), W("qj"), W("eqn"), A.max)
         for b in range(4):
             join("jx")
             tt(W("CV", b, 448, 4), bk(hb[b], 0, K), W("FQ", b, 448, 4), A.add)
             if b == 0:
-                tt(W("sel"), W("qj"), W("eqn"), A.max)
-            if b == 1:
                 join("jx")
                 cp(W("lX"), W("sel"))
         scatter(W("X"), W("lX"), W("CV"))
     for h in range(2):
         quant("qx", HC * h, HC * (h + 1), W("X", 4 * HC * h, 4 * HC * (h + 1)))
         mm(h, "qv", 0, "qx", HC * h, HC)
+        dma("s", "doc", W("oc", 4 * HC * h, 4 * HC * (h + 1)), W("qx", HC * h, HC * (h + 1)), a8=True)
     for h in range(2):
         half = W("yo", HC * h, HC * (h + 1))
         (acp, cp)[h](half, bk(h, 0, HC))
         dma("a", "dy", W("y", HC * h, HC * (h + 1)), half)
-        if h == 0:
-            emit("s", lambda: g.sync.dma_start(T.oc[:, :], by(W("qx"))), [], [W("qx")], dma="doc")
     for k in range(4):
         emit("s", lambda: g.sync.dma_start(T.osc[4 * k:4 * k + 4, :], T.qxs[32 * k:32 * k + 4, 0:C]), [], [W("qxs")], dma="doc")
-    finish([("rl", rlc[0])] + [("ap%d" % t, np_) for t in range(ROUNDS)] + [("ae%d" % t, 2 * np_) for t in range(ROUNDS)])
+    finish([("rl", rlc[0])] + [("ap%d" % t, np_ if t else few) for t in range(ROUNDS)] + [("ae%d" % t, 2 * np_) for t in range(ROUNDS)])

from concourse.mybir import dt, AluOpType, AxisListType, ActivationFunctionType

C, K, ROUNDS = 288, 112, 3
NJ = C // 16
UNIT = 8192.0
MID = 128.0
BIG = 1024.0
LIFT = 512.0
WHOLE = 2.0 ** 23
TINY = 1e-36
MARK = 8
HUGE = 2.0 ** 90
SMALL = 1.0 / 64
HC = C // 2
T2, S1, S2, TW = C, 2 * C + 32, 2 * C + 72, 2 * C + 128
PW = 48
CODE, F32, BF, I32, U16, U8 = "float8_e4m3fn_x4", "float32", "bfloat16", "int32", "uint16", "uint8"
HV = (4, 6, 6, 4)
DV = 12
SP = 3
NEAR = (0, 1, 1)
FAR = 8
EARLY = 14
CHUNKS = [(0, 9), (1, 2), (3, 4), (5, 6), (7, 8)]
PLANE = {}
GW = 0
for _a, _b in CHUNKS:
    GW += 8 * _b
    PLANE[_a], PLANE[_b] = (GW, 0), (GW, 1)
    GW += 144
CE, CC, CI, CZ = 0, 512, 640, 896

SCRATCH = {"ps": ("psum", [128, 4096], F32)}


def _sb(dtype, **names):
    for n, w in names.items():
        SCRATCH[n] = ("sbuf", [128, w], dtype)


_sb(BF, x0=4 * C, X=1600, ub=512, vb=512, neg=528, OH=528, OI=528, cb=512, G=4 * GW, m16=C, B16=C, e64=72,
    A5=448, Et=512, Vt=512, DE=448, CV=448, wrb=C, am=C, BR=320, TR=TW)
_sb(F32, r4=K, r8=144, pflt=24, ic=C, cd=C, dm=28, c16=28, lk=10, lf=72, KS=160, KR=C, KT=12, TP=320,
    z=C, zs=C, zz=144, zc=144, rk=NJ, B8=144, M4=K, M5=K, M8=144, OE=C, sg=C, Vr=C, Rs=NJ, PL=C, ab=C, rl=2 * C, TG=C,
    Q1=C, Q2=C, Q3=C, Q4=C, P1=K, P2=K, P4=144, w1=K, wA=K, wE=K, FQ=448, eqn=28, sel=28, lqf=K, q0=K, qa=2 * K, qb=2 * K,
    q4=2 * K + 2, yo=C)
_sb(I32, rvt=NJ, pint=8, qi=28, qj=28)
_sb(U16, rvl=NJ, lu=90, l16=NJ, lA=28, rkl=NJ, LL=80, lE=28, lQ=28, lX=28, pls=PW * ROUNDS, pll=PW * ROUNDS)
for _n, _w in [("qx", C), ("qu", 128), ("qv", 128), ("uo", 128), ("wq", 512), ("cq", CZ + 512), ("gq", GW), ("vq", 128),
               ("eq", 128 * ROUNDS), ("le", 16 + K * ROUNDS)]:
    SCRATCH[_n] = ("sbuf", [128, _w], CODE)
    SCRATCH[_n + "s"] = ("sbuf", [128, _w], U8)

QS = {"v": "qsv", "a": "qsa", "t": "qst", "g": "qsg"}
DS = ["dx", "du", "dv", "drv", "dwc", "dws", "dG", "dpad", "dcb", "dz", "dk", "dle", "dlq", "doc", "dy"]
JS = {"jg1": 4, "jg3": 4, "jg5": 4, "jg7": 4, "jb": 6, "jq1": 2, "jq2": 2, "jq3": 2, "jq4": 3, "jp": 6, "jl": 4, "jv": 3, "jw": 2, "jx": 5}
SEMAPHORES = list(QS.values()) + DS + list(JS) + ["rl"] + ["ap%d" % _t for _t in range(ROUNDS)] + ["ae%d" % _t for _t in range(ROUNDS)]


def make_tracker(g, T):
    eng = {"v": g.vector, "a": g.scalar, "t": g.tensor, "g": g, "s": g.sync}
    clk = {q: {} for q in eng}
    cnt = {}
    snaps = {}
    acc = {}
    seq = [0]
    joint = []
    last = {}

    def hit(a, b):
        if a[1] >= b[2] or b[1] >= a[2] or a[3] >= b[4] or b[3] >= a[4]:
            return False
        return not (a[5] == b[5] and a[5] > 1 and (a[3] - b[3]) % a[5])

    def bank(r):
        return (r[0], 0, 128, r[3] // 512 * 512, (r[4] + 511) // 512 * 512, 1) if r[0] == "ps" else r

    def merge(q, sem, val):
        own = clk[q]
        own[sem] = max(own.get(sem, 0), val)
        for v, s in snaps.get(sem, []):
            if v <= val:
                for a, b in s.items():
                    own[a] = max(own.get(a, 0), b)

    def emit(q, call, outs, ins, dma=None, remote=False):
        need = {}

        def want(rec):
            sem, val, order = rec[2], rec[3], rec[4]
            if clk[q].get(sem, 0) >= val:
                return
            if sem in DS:
                val = cnt[sem]
            if sem in JS:
                val = -(-val // JS[sem]) * JS[sem]
                assert val <= cnt[sem], sem
            if need.get(sem, (0, 0))[0] < val:
                need[sem] = (val, order)
        for r0 in ins:
            r = bank(r0)
            for rec in acc.get(r[0], []):
                if hit(r, rec[0]) and (rec[1] or (r[0] == "ps" and rec[5] != q)):
                    want(rec)
        for r0 in outs:
            r = bank(r0)
            for rec in acc.get(r[0], []):
                if hit(r, rec[0]) and not (rec[5] == q == "t"):
                    want(rec)
        for sem, (val, order) in sorted(need.items(), key=lambda e: -e[1][1]):
            if clk[q].get(sem, 0) < val:
                if sem == QS.get(q):
                    val = max(val, cnt[sem] - (last.get(q) == sem))
                eng[q].wait_ge(T.sem[sem], val)
                merge(q, sem, val)
        made = call()
        seq[0] += 1
        if remote:
            return
        sem = dma or joint.pop(0) if dma or joint else QS[q]
        last[q] = sem
        cnt[sem] = cnt.get(sem, 0) + (16 if dma else 1)
        made.then_inc(T.sem[sem], 16 if dma else 1)
        snaps.setdefault(sem, []).append((cnt[sem], dict(clk[q])))
        for r0, wr in [(r, True) for r in outs] + [(r, False) for r in ins]:
            r = bank(r0)
            lst = acc.setdefault(r[0], [])
            if wr:
                lst[:] = [e for e in lst if not (e[0][1] >= r[1] and e[0][2] <= r[2] and e[0][3] >= r[3] and e[0][4] <= r[4] and r[5] == 1)]
            lst.append((r, wr, sem, cnt[sem], seq[0], q, dma))

    def arrive(regs, sem, val):
        seq[0] += 1
        for r in regs:
            acc.setdefault(r[0], []).append((r, True, sem, val, seq[0], "r", sem))

    def finish(extra):
        for sem in list(cnt):
            if clk["g"].get(sem, 0) < cnt[sem]:
                g.wait_ge(T.sem[sem], cnt[sem])
                merge("g", sem, cnt[sem])
        for sem, val in extra:
            if clk["g"].get(sem, 0) < val:
                g.wait_ge(T.sem[sem], val)

    def join(sem, n=1):
        joint.extend([sem] * n)
    return emit, arrive, finish, join


def rank_program(g, core, T, topo):
    rank = T.rank_of(core)
    if rank is None:
        return
    N = len(T.cores)
    nxt, prv = T.cores[(rank + 1) % N], T.cores[(rank - 1) % N]
    A, AF = AluOpType, ActivationFunctionType
    emit, arrive, finish, join = make_tracker(g, T)

    def W(n, c0=0, c1=None, s=1, p0=0, p1=128):
        return (n, p0, p1, c0, c1 if c1 is not None else (SCRATCH[n][1][1] if n in SCRATCH else T[n].shape[1]), s)

    def ap(r):
        if len(r) == 2:
            return ap(r[0]).indirect(ap(r[1]))
        n, p0, p1, c0, c1, s = r
        return T[n][p0:p1, c0:c1] if s == 1 else T[n][p0:p1, c0:c1:s]

    def by(r):
        return ap(r).bitcast(dt.uint8)

    def rg(*rs):
        o = []
        for r in rs:
            o += list(r) if len(r) == 2 else [r]
        return o

    def ind(win, off):
        return (win, off)

    def tt(out, a, b, op):
        emit("v", lambda: g.vector.tensor_tensor(ap(out), ap(a), ap(b), op), rg(out), rg(a, b))

    def ts(out, a, s1, op0, s2=None, op1=None):
        x1, x2 = (ap(s) if isinstance(s, tuple) else s for s in (s1, s2))
        sc = [s for s in (s1, s2) if isinstance(s, tuple)]
        if op1 is None:
            emit("v", lambda: g.vector.tensor_scalar(ap(out), ap(a), x1, None, op0), rg(out), rg(a, *sc))
        else:
            emit("v", lambda: g.vector.tensor_scalar(ap(out), ap(a), x1, x2, op0, op1), rg(out), rg(a, *sc))

    def cp(out, a):
        emit("v", lambda: g.vector.tensor_copy(ap(out), ap(a)), rg(out), rg(a))

    def scatter(win, off, a):
        emit("v", lambda: g.vector.tensor_copy(ap((win, off)), ap(a)), [win], [off, a])

    def fill(out, val):
        emit("v", lambda: g.vector.memset(ap(out), val), rg(out), [])

    def scan(out, d0, d1, init, op0, op1):
        emit("v", lambda: g.vector.tensor_tensor_scan(ap(out), ap(d0), ap(d1), init, op0, op1), [out], [d0, d1])

    def total(out, a):
        emit("v", lambda: g.vector.tensor_reduce(ap(out), ap(a), AxisListType.X, A.add), [out], [a])

    def turn(out, a):
        emit("v", lambda: g.vector.transpose(ap(out), ap(a)), [out], [a])

    def act(out, a, fn=AF.Identity, scale=1.0, bias=0.0, accum=None):
        kw, ins, outs = {}, rg(a), rg(out)
        if isinstance(scale, tuple):
            kw["scale"] = ap(scale)
            ins.append(scale)
        elif scale != 1.0:
            kw["scale"] = scale
        if isinstance(bias, tuple):
            kw["bias"] = ap(bias)
            ins.append(bias)
        elif bias != 0.0:
            kw["bias"] = bias
        if accum is not None:
            kw["accum_out"] = ap(accum)
            outs.append(accum)
        emit("a", lambda: g.scalar.activation(ap(out), ap(a), fn, **kw), outs, ins)

    def acp(out, a):
        act(out, a, AF.Copy)

    def iota(out, pattern, base=0, cm=0):
        kw = {} if SCRATCH[out[0]][2] == I32 else {"allow_small_or_imprecise_dtypes": True}
        emit("g", lambda: g.iota(ap(out), pattern, base, cm, **kw), rg(out), [])

    def asel(out, a, pattern, op, base, cm, other=0.0):
        emit("g", lambda: g.affine_select(ap(out), ap(a), pattern, op, other, base, cm), rg(out), rg(a))

    def dma(q, sem, out, a, o8=False, a8=False):
        e = {"s": g.sync, "a": g.scalar}[q]
        emit(q, lambda: e.dma_start(by(out) if o8 else ap(out), by(a) if a8 else ap(a)), rg(out), rg(a), dma=sem)

    def quant(n, c0, c1, src):
        o, s = W(n, c0, c1), W(n + "s", c0, c1)
        emit("v", lambda: g.vector.quantize_mx(ap(o), ap(s), ap(src)), rg(o, s), rg(src))

    def mm(bank, wn, w0, xn, x0, n, start=True, stop=True):
        o = W("ps", 512 * bank, 512 * bank + n)
        w, ws, x, xs = W(wn, w0, w0 + 128), W(wn + "s", w0, w0 + 128), W(xn, x0, x0 + n), W(xn + "s", x0, x0 + n)
        emit("t", lambda: g.tensor.matmul_mx(ap(o), ap(w), ap(ws), ap(x), ap(xs), start, stop), rg(o), rg(w, ws, x, xs))

    def bk(b, c0, c1):
        return W("ps", 512 * b + c0, 512 * b + c1)

    def pick(out, off):
        emit("v", lambda: g.vector.tensor_copy(ap(W(out)).bitcast(dt.uint32), ap(W("qu")).bitcast(dt.uint32).indirect(ap(off))), [W(out)], [W("qu"), off])
        emit("a", lambda: g.scalar.activation(ap(W(out + "s")), ap(W("qus")).indirect(ap(off)), AF.Copy), [W(out + "s")], [W("qus"), off])

    LF, L2, L4, LQ, LB, LR, LA, LM, K2, K5, K6, LH, LV = (W("pflt", i, i + 1) for i in range(13))
    PI, l16 = W("pint", 0, 1), W("l16")
    C16 = W("lf", 0, NJ)
    sO, lrv, lrq, lks, lsel, lsp = (W("lu", a, b) for a, b in ((0, 8), (36, 54), (82, 89), (54, 64), (76, 81), (72, 75)))

    def columns(row, tmp, i1, i2, out, between=()):
        steps = [lambda: scan(tmp, row, W("M4"), LIFT * UNIT, A.min, A.add), lambda: ts(i1, (tmp[0], 0, 128, 3, K, 4), LB, A.add),
                 lambda: ts(i2, i1, int(UNIT) - 1, A.bitwise_and), lambda: cp(out, i2)]
        for n, step in enumerate(steps):
            step()
            if n < len(between):
                between[n]()

    def lane(k, c0, c1):
        o = 4 * PLANE[k][0] + PLANE[k][1]
        return W("G", o + 2 * c0, o + 2 * c1 - 1, 2)

    def across(eng, n, o, w, p, back, c0=0):
        h, p0 = 64 if back == 64 else 32, (p - back) % 128
        join("jb" if n == "TR" else "jp")
        eng(W(n, o, o + w // 16, p0=p, p1=p + h), W(n, c0, w, 16, p0=p0, p1=p0 + h))

    def zero(o):
        act(o, W("neg", 0, o[4] - o[3]), AF.Copy, scale=0.0)

    def pad(k):
        return W("G", 4 * PLANE[k][0] - 32 * k, 4 * PLANE[k][0])

    for n, sem, name in (("ub", "du", "u"), ("x0", "dx", "x")):
        dma("s", sem, W(n), W(name))

    iota(PI, [[0, 1]], 0, 1)
    iota(W("lf", 0, 2 * NJ), [[15, 2], [16, NJ]])
    fill(W("neg"), -1.0)
    asel(W("OH"), W("neg"), [[-1, 528]], A.is_equal, 3, 4)
    asel(W("e64"), W("neg", 0, 72), [[0, 9], [-1, 8]], A.is_ge, 3, 0)
    iota(W("lk"), [[16, 5], [80, 2]])
    for i, mask in enumerate((15, 14, 12)):
        ts(W("pint", i + 1, i + 2), PI, mask, A.bitwise_and)
    fill(W("B16"), HUGE)
    cp(W("pflt", 0, 3), W("pint", 1, 4))
    cp(W("lu", 0, 2 * NJ), W("lf", 0, 2 * NJ))
    ts(l16, W("neg", 0, NJ), 0.0, A.mult, LF, A.add)
    fill(W("B16", 0, C, 16), -HUGE)
    fill(W("cb"), 0.0)
    fill(W("OI"), 0.0)
    zero(pad(9))
    zero(W("G", 4 * PLANE[9][0] + C, 4 * PLANE[1][0]))
    act(LH, LF, scale=-HUGE)
    act(K2, L2, scale=BIG)
    act(W("m16"), ind(W("lf", 0, 16), l16), AF.Abs, scale=HUGE / 16, bias=LH)
    for n in range(8):
        dma("s", "dcb", W("cb", 64 * n, 64 * n + 64, p0=16 * n, p1=16 * n + 16), W("e64", 2, 66, p0=16 * n, p1=16 * n + 16))
    emit("s", lambda: g.sync.dma_start(ap(W("rvt")), ap(W("rv"))), [W("rvt")], [W("x0")], dma="drv")
    for sem, outs in (("dG", [pad(4), pad(6), pad(8)]), ("dpad", [W("TR", S1, TW), W("BR", C + 16, 320), W("Et", 448, 512), W("Vt", 448, 512)])):
        for o in outs:
            dma("s", sem, o, W("G", 0, o[4] - o[3]))
    dma("s", "dwc", W("wq"), W("wc"), o8=True)
    dma("s", "dws", W("wqs"), W("ws"))
    dma("s", "dv", W("vb"), W("v"))

    def unpacker(b):
        quant("cq", CE + 128 * b, CE + 128 * b + 128, W("OH", 3 - b, 515 - b))
    quant("qu", 0, 128, W("ub"))
    unpacker(0)
    pick("uo", sO)
    unpacker(1)
    for e in (1, 3):
        acp(W("OI", e, 512 + e, 4), W("OH", 3, 515, 4))
    act(LM, L2, AF.Square, scale=-16.0, bias=224.0)
    act(K5, L4, AF.Relu, scale=-LIFT * UNIT, bias=LIFT * UNIT)
    act(LQ, L4, scale=-1.0, bias=LF)
    act(LV, LF, scale=-1.0, bias=C - 1.0)
    act(LR, LM, bias=BIG)
    act(W("lf", 54, 64), W("lk"), bias=LF)
    act(W("lf", 36, 54), C16, scale=-1.0, bias=LV)

    def consts_later():
        iota(W("r8"), [[0, NJ], [2, 8]], 1)
        iota(W("TP", 288, 320), [[0, 32]])
        for o in (W("Rs", FAR, NJ), W("P4", 0, 16), W("P4", 128, 144)):
            dma("s", "dz", o, W("TP", 288, 288 + o[4] - o[3]))
        iota(W("B8"), [[16, 2], [0, 9], [-4096, 8]], -16 - 128)
        iota(W("cd"), [[4, C]], 4)
        for c0, c1, pattern, base in ((0, 36, [[-1, 2], [2, 9], [20, 2]], S1 + 1), (36, 72, [[-1, 2], [2, 9], [20, 2]], S2 + 1), (72, 80, [[0, 8]], 0),
                                      (80, 98, [[32, 9], [-T2, 2]], T2 + MARK), (98, 134, [[-1, 2], [2, 9], [-NJ, 2]], S1 + 1 + NJ),
                                      (134, 160, [[2, 13], [-NJ, 2]], S2 + 1 + NJ)):
            iota(W("KS", c0, c1), pattern, base)
        for c0, c1, pattern, base in ((0, 8, [[32, 4], [160, 2]], 0), (8, 16, [[2, 4], [10, 2]], 257), (16, 32, [[-16, 2], [32, 4], [-128, 2]], 144),
                                      (32, 48, [[17, 2], [2, 4], [10, 2]], 256), (48, 64, [[-1, 2], [2, 4], [-8, 2]], 265),
                                      (64, 80, [[17, 2], [2, 4], [10, 2]], 272), (80, 96, [[-1, 2], [2, 4], [-8, 2]], 281), (96, 128, [[0, 32]], 0)):
            iota(W("KR", c0, c1), pattern, base)
        iota(W("r4"), [[0, 28], [4, 4]], 2)
        iota(W("BR", 0, 32), [[0, 32]], int(-MID * SMALL))
        iota(W("ic"), [[int(UNIT), C]])
        iota(W("c16"), [[16, 28]])
        iota(W("q4", 2 * K + 1, 2 * K + 2), [[0, 1]], int(LIFT * UNIT))

    def consts_rank():
        act(W("Q4"), ind(W("cd"), W("rvl")), AF.Relu, scale=0.25, bias=-2.0)
        act(W("wrb"), ind(W("Q4"), lrv), scale=-SMALL, bias=(C - 1 - MID) * SMALL)
        acp(W("KR", 128, C), ind(W("KS"), lks))
        for c in range(9):
            dma("s", "dk", W("KT", c, c + 1), W("KR", 32 * c, 32 * c + 32, p1=4))
        dma("s", "dle", W("le", 0, 16), W("gq", 0, 16), o8=True, a8=True)
        dma("s", "dle", W("les", 0, 16), W("gqs", 0, 16))

    def consts_lists():
        act(W("w1"), W("r4"), AF.Sign, scale=-1.0, bias=L4)
        act(LB, LQ, bias=3 * UNIT - 4)
        act(W("M4"), W("w1"), scale=(LIFT + 1) / 2 * UNIT, bias=(LIFT - 1) / 2 * UNIT)
        act(K6, L4, scale=-UNIT / 4, bias=LB)
        act(W("M4", 3, K, 4), W("r4", 0, 28), scale=0.0, bias=K5)
        act(LA, K5, scale=-1.0, bias=K6)

    def consts_late():
        act(W("dm"), W("c16"), scale=-1.0, bias=K5)
        cp(W("M5"), W("M4"))
        ts(W("M5", 3, K, 4), W("dm"), LF, A.subtract, -4.0 * C, A.add)
        act(W("OH"), W("OH"), AF.Copy, scale=2.0 ** -6)
        ts(lrq, W("lf", 36, 43), K - float(C), A.add)
        quant("qv", 0, 128, W("vb"))
        for b in range(4):
            quant("cq", CZ + 128 * b, CZ + 128 * b + 128, W("OH", 3 - b, 515 - b))

    rid, pid = topo.addr(nxt, core)
    rlc = [0]
    few = min(len(topo.engines(a, b)) for a, b in zip(T.cores, T.cores[1:] + T.cores[:1]))
    np_ = len(topo.engines(prv, core))

    def send(out, src, view, sem, n=None):
        engines = topo.engines(core, nxt)[:n]
        emit("g", lambda: g.remote_dma(view(out), view(src), T.sem[sem], T.sem.rl, pid, rid, sum(1 << e for e in engines)), [], [src], remote=True)
        rlc[0] += len(engines)

    for t in range(ROUNDS):
        hb2 = (2, 7)
        for h in (1, 0):
            quant("qx", HC * h, HC * (h + 1), W("x0" if t == 0 else "X", 4 * HC * h, 4 * HC * (h + 1)))
            mm(hb2[h], "uo", 0, "qx", HC * h, HC)
        mm(4, "qu", 0, "qx", HC, HC)
        mm(0, "uo", 0, "qx", 0, C)
        mm(3, "qu", 0, "qx", 0, HC)

        def marks(h):
            act(W("sg", HC * h, HC * (h + 1)), bk(3 + h, 0, HC), AF.Sign, bias=-TINY)
        marks(1)
        if t == 0:
            quant("cq", CI, CI + 128, W("OI", 1, 513))
        for h in (1, 0):
            tt(W("z", HC * h, HC * (h + 1)), bk(hb2[h], 0, HC), W("m16", HC * h, HC * (h + 1)), A.subtract)
        for c0, c1 in ((HC, C), (0, HC)):
            scan(W("zs", c0, c1), W("B16", c0, c1), W("z", c0, c1), -HUGE, A.min, A.max)
            acp(W("OE", c0, c1), ind(W("zs", c0, c1), W("lu", NJ, NJ + HC // 16)))
        for c0, c1 in ((HC, C), (0, HC)):
            tt(lane(0, c0, c1), bk(0, c0, c1), W("zs", c0, c1), A.is_le)
        if t == 0:
            quant("cq", CI + 128, CZ, W("OI", 0, 512))
            consts_later()

        def far(k):
            o = 8 * k * (k - 1)
            act(W("rl", o, o + 16 * k), bk(7, HC - 16 * k, HC), AF.Sign, scale=-1.0, bias=W("zs", 16 * (FAR - k) + 15, 16 * (FAR - k) + 16))

        def won(k):
            o = 8 * k * (k - 1)
            join("jg%d" % (k - 1 + k % 2))
            act(lane(k, C - 16 * k, C), W("rl", o, o + 16 * k), AF.Sign, bias=1.0, accum=W("Rs", FAR - k, FAR + 1 - k))
        far(NEAR[t] + 1)
        for k in range(NEAR[t] + 1, FAR + 1):
            if k < FAR:
                far(k + 1)
            won(k)

        def plane(k):
            pair = "jg%d" % (k - 1 + k % 2)
            if k <= NEAR[t]:
                join(pair)
                ts(lane(k, C - 16 * k, C), bk(0, C - 16 * k, C), W("zs", 16 * (FAR - k) + 15, 16 * (FAR - k) + 16), A.is_le)
            if k < 9:
                join(pair)
            tt(lane(k, 0, C - 16 * k), bk(0, 0, C - 16 * k), W("OE", 16 * k, C), A.is_lt)

        def count(chs):
            for k in range(1, NEAR[t] + 1):
                if (k - 1 + k % 2, k + k % 2) in chs:
                    total(W("Rs", FAR - k, FAR + 1 - k), lane(k, C - 16 * k, C))
            o0, end = PLANE[chs[0][0]][0] - (0 if t else 8 * chs[0][1]), PLANE[chs[-1][0]][0] + 144
            quant("gq", o0, end, W("G", 4 * o0, 4 * end))
            for ch in chs:
                for k in ch:
                    mm(1, "cq", CI + 128 * PLANE[k][1], "gq", PLANE[k][0] - 8 * k, 144, start=(k == 0), stop=(k == 8))
                mm(6, "cq", CC, "gq", PLANE[ch[0]][0], 144, start=(ch[0] == 0), stop=(ch[1] == 8))
        for k in (9, 1, 2, 3, 4, 5, 6, 7, 8):
            plane(k)
            if t == 0 and k == 3:
                quant("cq", CC, CI, W("cb"))
            if k in (3, 5, 7):
                count(CHUNKS[:2] if k == 3 else [CHUNKS[k // 2]])
            if t == 0 and k in (6, 8):
                unpacker(k // 2 - 1)
                cp(*((W("rvl"), W("rvt")) if k == 6 else (W("lu", 36, 64), W("lf", 36, 64))))
        count(CHUNKS[-1:])
        if t == 0:
            act(W("M8"), W("r8"), scale=-BIG, bias=K2)
        marks(0)
        act(W("M8", 7, 144, 8), W("Rs"), bias=LR)
        if t == 0:
            consts_rank()
            consts_lists()
        for b in range(4):
            mm(2 + b, "cq", CE + 128 * b, "qx", 0, C)
        scan(W("Vr"), W("cd"), W("sg"), 0.0, A.max, A.mult)
        scan(W("zz"), W("B8"), bk(1, 0, 144), -100 * BIG, A.max, A.add)
        scan(W("zc"), bk(6, 0, 144), W("M8"), 4 * BIG, A.min, A.add)
        tt(W("rk"), W("zc", 7, 144, 8), W("zz", 7, 144, 8), A.subtract)
        ts(W("rkl"), W("rk"), LF, A.add, -BIG, A.add)
        scatter(W("PL"), W("rkl"), W("Vr"))

        def state(b):
            act(W("X", b, 4 * C, 4), bk(2 + b, 0, C), AF.Copy, scale=-1.0)
        for b in range(3 if t else 0):
            state(b)
        act(W("ab"), W("PL"), AF.Abs)
        for b in range(3, 4) if t else range(3):
            state(b)
        scan(W("am"), W("PL"), W("wrb"), -MID * SMALL, A.max, A.min)
        scan(W("BR", 17, 17 + C), W("am"), W("am"), -MID * SMALL, A.max, A.max)
        turn(W("TR", 0, T2), W("BR", 16, 16 + C))
        turn(W("TR", T2, S1), W("BR"))
        for p in (0, 32, 64, 96):
            across(acp, "TR", S1, S1, p, 32, MARK)
        if t == 0:
            cp(W("lu", 72, 81), W("KT", 0, 9))
        scan(W("TG"), W("ic"), W("ab"), 0.0, A.max, A.add)
        for p in (0, 64):
            across(cp, "TR", S2, S1, p, 64, MARK)
        if t == 0:
            state(3)
        ts(W("LL"), ind(W("TR"), lsel), 1.0 / SMALL, A.mult, MID, A.add)

        def fixed():
            scan(W("wA"), W("ab", 1, 2 * K, 2), W("M4"), LIFT * UNIT, A.min, A.add)
            ts(W("lA"), W("wA", 3, K, 4), LA, A.add)
        odd = {n: (n, 0, 128, 1, 2 * K, 2) for n in ("TG", "Q1", "Q2", "Q3", "Q4")}
        for d in range(1, 5):
            H, end = HV[d - 1], NJ if d < 4 else EARLY
            src, o = W("TG") if d == 1 else W("Q%d" % (d - 1)), NJ * (d - 1)
            join("jq%d" % d, 2)
            cp(W("Q%d" % d, 0, 16 * H), ind(src, W("LL", o, o + H)))
            acp(W("Q%d" % d, 16 * H, 16 * end), ind(src, W("LL", o + H, o + end)))
            if d == 2:
                scan(W("P1"), odd["TG"], odd["Q1"], 0.0, A.max, A.max)
            if d == 3:
                scan(W("P2"), W("P1"), odd["Q2"], 0.0, A.max, A.max)
            if d == 4:
                join("jq4")
                scan(W("P1"), W("P2"), odd["Q3"], 0.0, A.max, A.max)
            if d == 1:
                fixed()
        acp(W("A5"), ind(W("X", 0, 4 * C), W("lA")))
        P4 = W("P4", 16, 16 + K)
        scan(P4, W("P1"), odd["Q4"], 0.0, A.max, A.max)
        turn(W("TP", 0, 128), W("P4", 16, 144))
        turn(W("TP", 128, 256), W("P4", 0, 128))
        for n, p in enumerate((0, 32, 64, 96)):
            across(acp if n < SP else cp, "TP", 256, 256, p, 32)
        for p in (0, 64):
            across(cp, "TP", 272, 256, p, 64)
        acp(W("Q4", 16 * EARLY, C), ind(W("Q3"), W("LL", 3 * NJ + EARLY, 4 * NJ)))
        o = PW * t
        pl, plo = W("pls", o, o + 40), W("pll", o, o + 40)

        def lists():
            ts(W("pls", o, o + PW), ind(W("TP"), lsp), 1.0 / UNIT, A.mult)
            send(plo, pl, ap, "ap%d" % t, None if t else few)
        columns(P4, W("wE"), W("qi"), W("qj"), W("lE"), [lists])
        tt(W("Et", 0, 448), ind(W("X", 0, 4 * C), W("lE")), W("A5"), A.add)
        quant("eq", 128 * t, 128 * t + 128, W("Et"))
        e, eo = W("eq", 128 * t, 128 * t + K), W("le", 16 + K * t, 16 + K * (t + 1))
        es, eso = W("eqs", 128 * t, 128 * t + K), W("les", 16 + K * t, 16 + K * (t + 1))
        send(eo, e, by, "ae%d" % t)
        send(eso, es, ap, "ae%d" % t)
        if t == 0:
            consts_late()
        arrive([plo], "ap%d" % t, np_ if t else few)
        arrive([eo, eso], "ae%d" % t, 2 * np_)
        cp(W("q0"), ind(W("Q1"), W("pll", o + 8, o + 15)))
        join("jl", 4)
        acp(W("qa", 1, 2 * K, 2), ind(W("Q3"), W("pll", o + 24, o + 31)))
        acp(W("qb", 0, 2 * K, 2), ind(W("Q4"), W("pll", o + 32, o + 39)))
        cp(W("qb", 1, 2 * K, 2), ind(W("TG"), W("pll", o, o + 7)))
        tt(W("qa", 0, 2 * K, 2), ind(W("Q2"), W("pll", o + 16, o + 23)), W("q0"), A.max)
        for b in range(4):
            if b == 0:
                join("jv")
            mm(2 + b, "cq", CZ + 128 * b, "le", K * t, 128)
        scan(W("q4", 0, 2 * K), W("qa"), W("qb"), 0.0, A.max, A.max)
        columns(W("q4", 1, 2 * K, 2), W("wE"), W("qi"), W("qj"), W("lQ"))
        join("jv", 2)
        ts(W("DE", 0, 16 * DV), ind(W("X", 0, 4 * C), W("lQ", 0, DV)), 2.0 ** -5, A.mult)
        act(W("DE", 16 * DV, 448), ind(W("X", 0, 4 * C), W("lQ", DV, 28)), AF.Copy, scale=2.0 ** -5)
        scan(W("w1"), W("q4", 3, 2 * K + 2, 2), W("M5"), LIFT * UNIT, A.min, A.add)
        join("jw")
        act(W("FQ"), W("DE"), AF.Copy, scale=2.0 ** 5)
        for b in range(4):
            tt(W("Vt", b, 448, 4), W("DE", b, 448, 4), bk(2 + b, 16, 16 + K), A.subtract)
        if t == ROUNDS - 1:
            act(W("q0"), W("q4", 1, 2 * K, 2), scale=-1.0 / UNIT, bias=WHOLE + C - 1)
            act(W("lqf"), ind(W("q0"), lrq), bias=-WHOLE)
            emit("s", lambda: g.sync.dma_start(T.lq[:, :], T.lqf[0:128:16, 0:K]), [], [W("lqf")], dma="dlq")
        quant("vq", 0, 128, W("Vt"))
        hb = (0, 1, 6, 7)
        for b in range(4):
            if b == 0:
                join("jw")
            mm(hb[b], "wq", 128 * b, "vq", 0, 128)
        tt(W("eqn"), W("wE", 3, K, 4), W("w1", 3, K, 4), A.subtract)
        tt(W("sel"), W("qj"), W("eqn"), A.max)
        for b in range(4):
            join("jx")
            tt(W("CV", b, 448, 4), bk(hb[b], 0, K), W("FQ", b, 448, 4), A.add)
            if b == 0:
                join("jx")
                cp(W("lX"), W("sel"))
        scatter(W("X"), W("lX"), W("CV"))
    for h in range(2):
        quant("qx", HC * h, HC * (h + 1), W("X", 4 * HC * h, 4 * HC * (h + 1)))
        mm(h, "qv", 0, "qx", HC * h, HC)
        dma("s", "doc", W("oc", 4 * HC * h, 4 * HC * (h + 1)), W("qx", HC * h, HC * (h + 1)), a8=True)
    for h in range(2):
        half = W("yo", HC * h, HC * (h + 1))
        (acp, cp)[h](half, bk(h, 0, HC))
        dma("a", "dy", W("y", HC * h, HC * (h + 1)), half)
    for k in range(4):
        emit("s", lambda: g.sync.dma_start(T.osc[4 * k:4 * k + 4, :], T.qxs[32 * k:32 * k + 4, 0:C]), [], [W("qxs")], dma="doc")
    finish([("rl", rlc[0])] + [("ap%d" % t, np_ if t else few) for t in range(ROUNDS)] + [("ae%d" % t, 2 * np_) for t in range(ROUNDS)])
